import numpy as np, ml_dtypes
CORES = [3,7,11,15,131,135,139,143]
N = 8
BF = ml_dtypes.bfloat16
L, WX, W, FD, RO = 256, 4096, 1024, 64, 3
LW = 10
WT = 2 * np.arange(16) + 1
KINDS = np.array([[16, 0, 0, 0], [15, 1, 0, 0], [8, 8, 0, 0], [4, 4, 4, 4], [13, 1, 1, 1], [7, 6, 2, 1], [14, 2, 0, 0], [6, 5, 5, 0]])
SEQ = np.stack([np.repeat(np.arange(4), a) for a in KINDS])
def move(a):
    return np.ascontiguousarray(a.reshape(N, 8, 16, N, L // N).transpose(3, 1, 2, 0, 4)).reshape(N, 8, 16, L)
def pack(X, C, M, S, Z):
    return {"x0": np.ascontiguousarray(X.reshape(N, 128, WX)).astype(np.float32).astype(BF), "cm": np.ascontiguousarray((W * M + C).reshape(N, 128, W)).astype(np.int32),
            "s0": np.ascontiguousarray(S.reshape(N, 128, L)).astype(np.int32), "z0": np.ascontiguousarray(Z.reshape(N, 128, L)).astype(np.float32).astype(BF)}
def parts(rng):
    X = rng.integers(0, 256, (N, 8, 16, WX)); C = rng.integers(0, W, (N, 8, 16, W)); M = rng.integers(0, W, (N, 8, 16, W))
    share = rng.choice(np.array([0.1, 0.3, 0.6]), (N, 8, 1, 1)); pool = rng.integers(0, W, (N, 8, 1, 64))
    few = np.take_along_axis(pool, rng.integers(0, 64, (N, 8, 1, 16 * W)), 3).reshape(N, 8, 16, W)
    C = np.where(rng.random(C.shape) < share, few, C)
    return X, C, M, rng.integers(0, W, (N, 8, 16, L)), rng.integers(0, 256, (N, 8, 16, L))
def classes(rng, kinds):
    s = np.take_along_axis(np.argsort(rng.random((L, 4)), axis=1), SEQ[kinds], 1)
    return np.take_along_axis(s, np.argsort(rng.random((L, 16)), axis=1), 1).T
def juries(rng, X, C, S, Z, q, g, cl):
    v = rng.permutation(W); off = rng.integers(0, W, 16); kind = int(rng.integers(0, 4))
    C[q, g] = v[(np.arange(W)[None, :] + off[:, None]) % W]
    base = np.zeros(16, np.int64) if kind == 0 else np.full(16, 255) if kind == 1 else rng.integers(0, 256, 16)
    Z[q, g] = base[np.argsort(rng.random((16, L)), axis=0)]
    u = int(np.add.reduce(base)); h = (((v * (u + 1)) >> 5) + v) & (WX - 1)
    b = np.add.reduce(X[q, g][:, h] * WT[:, None], axis=0) & 3
    start = rng.integers(0, W, (1, L))
    for c in range(4):
        m = (cl == c).astype(np.int64); before = np.add.accumulate(m, axis=0) - m
        pl = np.flatnonzero(b == c)
        if len(pl) == 0: pl = np.arange(W)
        S[q, g] = np.where(m == 1, (pl[(start + before) % len(pl)] - off[:, None]) % W, S[q, g])
    return off
def setup_inputs(rng):
    return pack(*parts(rng))
def setup_inputs_spread(rng):
    def uneven(n, hi, *shape):
        return np.minimum((hi * rng.random((N, 8, 16, n)) ** rng.choice(np.array([0.125, 0.5, 1.0, 2.0, 5.0]), shape)).astype(np.int64), hi - 1)
    return pack(uneven(WX, 256, N, 8, 1, WX), uneven(W, W, N, 8, 1, 1), uneven(W, W, N, 8, 16, 1), uneven(L, W, N, 8, 1, L), uneven(L, 256, N, 8, 1, L))
def setup_inputs_ends(rng):
    p = np.array([0.0, 0.1, 0.5, 0.9, 1.0])
    X = 255 * (rng.random((N, 8, 16, WX)) < rng.choice(p, (N, 8, 1, WX))).astype(np.int64)
    C = (W - 1) * rng.integers(0, 2, (N, 8, 16, W)); S = (W - 1) * rng.integers(0, 2, (N, 8, 16, L))
    Z = 255 * (rng.random((N, 8, 16, L)) < rng.choice(p, (N, 8, 1, L))).astype(np.int64)
    Z[..., L - 1] = 255; Z[..., 0] = 255; Z[..., 1] = 0; Z[..., L - 2] = 0
    C[:, :, 15, W - 1] = W - 1; S[:, :, 15, L - 1] = W - 1; S[:, :, 15, 0] = W - 1
    X[:, 0] = X[:, 0, :1]
    X[:, :, :, WX - 1] = 255; X[:, ::2, :, 0] = 255; X[:, 1::2, :, 0] = 0
    C[:, 7, :, W - 1] = W - 1; S[:, 7, :, L - 1] = W - 1; S[:, 7, :, 2] = W - 1
    C[:, 5, :, 0] = 0; C[:, 5, :, W - 1] = W - 1
    S[:, 5] = (W - 1) * (np.arange(16)[:, None] == rng.integers(0, 16, (N, 1, L)))
    Z[:, 5] = np.where(Z[:, 5, :1] > 0, 255, 0)
    X[:, 5, :, (613 * np.arange(15)) & (WX - 1)] = 0
    for u in (0, 4080):
        h = ((((W - 1) * (u + 1)) >> 5) + W - 1) & (WX - 1)
        X[:, 5, :, h] = 0; X[:, 5, 0, h] = 255
    M = np.where(rng.random(C.shape) < 0.8, C, W - 1 - C)
    return pack(X, C, M, S, Z)
def setup_inputs_corners(rng):
    X, C, M, S, Z = parts(rng)
    for q in range(N):
        for g in range(8):
            off = juries(rng, X, C, S, Z, q, g, classes(rng, rng.integers(0, 8, L)))
            w = rng.random(L); c = rng.integers(0, W, L)
            S[q, g] = np.where((w < 0.15)[None, :], (c[None, :] - off[:, None]) % W, S[q, g])
            S[q, g, 15] = np.where(w > 0.8, (S[q, g, 0] + off[0] - off[15]) % W, S[q, g, 15])
    return pack(X, C, M, S, Z)
def setup_inputs_crowd(rng):
    X, C, M, S, Z = parts(rng)
    for q in range(N):
        for g in range(8):
            w = (g + q) % 8; kinds = np.full(L, (1, 1, 0, 5, 5, 6, 3, 4)[w]); one = int(rng.integers(0, L))
            if w == 1: kinds[one] = 0
            off = juries(rng, X, C, S, Z, q, g, classes(rng, kinds))
            if w == 3: S[q, g] = S[q, g, :, :1].copy()
            if w == 4: S[q, g] = ((int(rng.integers(0, W)) - off) % W)[:, None]
            if w == 5:
                mine = S[q, g, :, one].copy(); S[q, g] = S[q, g, :, (one + 1) % L].copy()[:, None]; S[q, g, :, one] = mine
    return pack(X, C, M, S, Z)
def setup_inputs_tops(rng):
    X, C, M, S, Z = parts(rng)
    X[:, 1::2] = 255 - (rng.random((N, 4, 16, WX)) < 0.25).astype(np.int64)
    C = np.where(rng.random(C.shape) < 0.5, rng.choice(np.array([W - 17, W - 5, W - 3, W - 1]), C.shape), rng.integers(W - 96, W, C.shape))
    lack = rng.integers(0, 17, (N, 8, 1, L)); lack[..., 0::4] = 4; lack[..., 1::4] = 6; lack[..., 2::4] = 0; lack[..., L - 1] = 4
    Z = 255 - (np.argsort(rng.random((N, 8, 16, L)), axis=2) < lack).astype(np.int64)
    C[:, :, 15, W - 1] = W - 5; S[:, :, 15, L - 1] = W - 1
    return pack(X, C, M, S, Z)
def check_inputs(d):
    bad = []
    for k, hi in (("x0", 255), ("cm", W * W - 1), ("s0", W - 1), ("z0", 255)):
        a = np.asarray(d[k]).astype(np.float64)
        if not (np.min(a) >= 0 and np.max(a) <= hi): bad.append("range of " + k)
        elif np.any(a != np.floor(a)): bad.append("whole numbers in " + k)
    return bad
def reference(x0, cm, s0, z0):
    X = x0.astype(np.float32).astype(np.int64).reshape(N, 8, 16, WX); both = cm.astype(np.int64).reshape(N, 8, 16, W)
    C = both & (W - 1); M = both >> LW
    S = s0.astype(np.int64).reshape(N, 8, 16, L); Z = z0.astype(np.float32).astype(np.int64).reshape(N, 8, 16, L)
    A = np.zeros((N, 8, 1, 1), np.int64); k = np.arange(16); lane = np.arange(L); less = (k[:, None] > k[None, :])[:, :, None]
    for t in range(RO):
        e = np.take_along_axis(C[:, :, (k + t) & 15], S, 3)
        same = (e[:, :, :, None, :] == e[:, :, None, :, :]) & less
        o = np.add.reduce(same.astype(np.int64), axis=3)
        u = np.add.reduce(Z, axis=2)[:, :, None, :]
        h = (((e * (u + 1)) >> 5) + e + 613 * o + A) & (WX - 1)
        x = np.take_along_axis(X, h.reshape(N, 8, 1, 16 * L), 3).reshape(N, 8, 16, 16, L)
        b = np.add.reduce(x * WT[:, None, None], axis=2) & 3
        count = np.stack([np.add.reduce((b == c).astype(np.int64), axis=2) for c in range(4)], axis=2)
        best = np.argmin(np.where(count == 0, 99, count), axis=2)[:, :, None, :]
        sv = b == best; si = sv.astype(np.int64)
        ns = np.add.reduce(si, axis=2)[:, :, None, :]; before = np.add.accumulate(si, axis=2) - si
        place = np.where(sv, before, ns + k[:, None] - before)
        order = np.zeros_like(e); np.put_along_axis(order, place, e, 2)
        first = np.argmax(sv, axis=2)[:, :, None, :]
        hf = np.take_along_axis(h, first, 2); xf = np.take_along_axis(x, first[:, :, None], 3)[:, :, :, 0]
        y = np.take_along_axis(M, e.reshape(N, 8, 1, 16 * L), 3).reshape(N, 8, 16, 16, L)
        Z = np.maximum.reduce(np.where(sv[:, :, None], x, 0), axis=3)
        S = np.maximum.reduce(np.where(sv[:, :, None], y, 0), axis=3)
        np.put_along_axis(C, np.broadcast_to((W // L) * lane + (u & (W // L - 1)), (N, 8, 16, L)), order, 3)
        np.put_along_axis(X, np.broadcast_to(hf - (hf & (L - 1)) + lane, (N, 8, 16, L)), (xf + Z) >> 1, 3)
        A = np.add.reduce((ns == 1).astype(np.int64), axis=3)[..., None]
        if t < RO - 1:
            S = move(S); Z = move(Z)
    yx = np.add.reduce(X.reshape(N, 128, WX // FD, FD) * np.arange(1, WX // FD + 1)[:, None], axis=2)
    yc = np.add.reduce(C.reshape(N, 128, W // FD, FD) * np.arange(1, W // FD + 1)[:, None], axis=2)
    return {"yx": yx.astype(np.float32), "yc": yc.astype(np.float32), "ys": np.ascontiguousarray(S).reshape(N, 128, L).astype(np.float32), "yz": np.ascontiguousarray(Z).reshape(N, 128, L).astype(np.float32).astype(BF)}

@@ -1,0 +1,544 @@
+from concourse.bass import DstId, RemoteDMATransfer
+from concourse.mybir import dt, AluOpType, AxisListType, ActivationFunctionType
+
+A = AluOpType
+AF = ActivationFunctionType
+LEVELS = 3
+
+_B, _H, _F, _I, _U = "bfloat16", "float16", "float32", "int32", "uint16"
+PACK, _w = {}, {}
+for _b, _n, _c in [("B7", x, 128) for x in ("VK", "SV", "AL", "PR", "TP", "SVL", "VM")] + [
+        ("IS", "UI", 16), ("IS", "KI", 32), ("IS", "KJ", 24), ("IS", "BN", 16)]:
+    PACK[_n] = (_b, _w.get(_b, 0), _c)
+    _w[_b] = _w.get(_b, 0) + _c
+KP = {_n: 128 * _i for _i, _n in enumerate(("KM7", "KM2", "KC16", "NI", "I2"))}
+SCRATCH = {
+    "XW": ("sbuf", [128, 4096], _B), "CM": ("sbuf", [128, 1024], _I), "CW": ("sbuf", [128, 1024], _I),
+    "MW": ("sbuf", [128, 1024], _I), "S3": ("sbuf", [128, 8, 2, 16], _I), "Z3": ("sbuf", [128, 8, 2, 16], _B),
+    "CF": ("sbuf", [128, 1024], _H),
+    "ON2": ("sbuf", [128, 128], _B), "ON3": ("sbuf", [128, 8, 8, 16], _B), "ID": ("sbuf", [128, 128], _B),
+    "ID3": ("sbuf", [128, 8, 16], _B), "BO": ("sbuf", [128, 8, 16], _B), "WB": ("sbuf", [128, 8], _B),
+    "LS": ("sbuf", [128, 8, 8, 16], _B), "DG": ("sbuf", [128, 128], _B), "FQ": ("sbuf", [128, 4, 8, 16], _B),
+    "BK": ("sbuf", [128, 16, 8, 16], _B), "I613": ("sbuf", [128, 128], _H), "KP": ("sbuf", [128, 640], _B),
+    "RM": ("sbuf", [128, 512], _B), "RM8": ("sbuf", [128, 128], _B), "KCC": ("sbuf", [128, 32], _B),
+    "MUL": ("sbuf", [128, 48], _I), "AD": ("sbuf", [128, 48], _I), "BS": ("sbuf", [128, 48], _I),
+    "QI": ("sbuf", [128, 16], _I), "QJ": ("sbuf", [128, 16], _I), "QC": ("sbuf", [128, 16], _F),
+    "RA": ("sbuf", [128, 16], _F), "RB": ("sbuf", [128, 16], _F), "DI": ("sbuf", [128, 64, 128], _B),
+    "CG": ("sbuf", [128, 4096], _H), "YG": ("sbuf", [128, 4096], _H), "XG": ("sbuf", [128, 4096], _B),
+    "XS": ("sbuf", [128, 4096], _H), "YS": ("sbuf", [128, 4096], _H), "DS": ("sbuf", [128, 4096], _B),
+    "LM": ("sbuf", [128, 128], _H), "LV": ("sbuf", [128, 128], _H), "VI": ("sbuf", [128, 16], _I),
+    "RL": ("sbuf", [128, 48], _I), "LST": ("sbuf", [128, 48], _U), "NZ": ("sbuf", [128, 256], _H),
+    "XQ": ("sbuf", [128, 256], _I), "XR": ("sbuf", [128, 256], _I), "FC": ("sbuf", [128, 256], _F),
+    "OS": ("sbuf", [128, 8, 2, 16], _F), "OZ": ("sbuf", [128, 8, 2, 16], _B),
+    "OX": ("sbuf", [128, 64], _F), "OC": ("sbuf", [128, 64], _F),
+    "D0": ("psum", [128, 512], _F), "D1": ("psum", [128, 512], _F),
+}
+for _c in "01":
+    SCRATCH.update({
+        "E" + _c: ("psum", [128, 4, 8, 16], _F), "Q" + _c: ("psum", [128, 4, 8, 16], _F),
+        "L" + _c: ("psum", [128, 512], _F),
+        "B7" + _c: ("sbuf", [128, _w["B7"]], _B), "IS" + _c: ("sbuf", [128, _w["IS"]], _I),
+        "ZC" + _c: ("sbuf", [128, 128], _H), "OFS" + _c: ("sbuf", [128, 128], _U), "OFM" + _c: ("sbuf", [128, 128], _U),
+        "OFX" + _c: ("sbuf", [128, 128], _U),
+        "ES" + _c: ("sbuf", [128, 8, 16], _H), "EQ" + _c: ("sbuf", [128, 15, 8, 16], _B),
+        "U1" + _c: ("sbuf", [128, 8, 16], _F), "U3" + _c: ("sbuf", [128, 8], _F),
+        "WI" + _c: ("sbuf", [128, 8, 16], _I), "HI" + _c: ("sbuf", [128, 8, 16], _I), "H8" + _c: ("sbuf", [128, 8, 16], _I),
+        "HF" + _c: ("sbuf", [128, 8, 16], _H), "BI" + _c: ("sbuf", [128, 128], _I),
+        "IN" + _c: ("sbuf", [128, 512], _B), "CT" + _c: ("sbuf", [128, 512], _B), "KB" + _c: ("sbuf", [128, 256], _B),
+        "BB" + _c: ("sbuf", [128, 256], _B),
+        "TT" + _c: ("sbuf", [128, 8, 3, 16], _H), "TL" + _c: ("sbuf", [128, 4, 8, 16], _H),
+        "FR" + _c: ("sbuf", [128, 16, 8, 16], _H), "O1" + _c: ("sbuf", [128, 8, 16], _B), "VT" + _c: ("sbuf", [128, 8], _H),
+        "SZ0" + _c: ("sbuf", [128, 8, 32], _H), "SZ1" + _c: ("sbuf", [128, 8, 32], _H),
+        "RZ0" + _c: ("sbuf", [128, 8, 32], _H), "RZ1" + _c: ("sbuf", [128, 8, 32], _H),
+    })
+SEMAPHORES = ["V", "S", "P", "G", "ds", "dz", "dc", "dx", "os", "oz", "ox", "oc"] + [
+    k + t + c for k in ("arr", "snt") for t in "01" for c in "01"]
+
+
+def calls_of(src, cores, topo):
+    here = [c for c in topo.cores_of(src) if c in cores and c != src]
+    off = [c for c in cores if c != src and c not in here]
+    off.sort(key=lambda c: (2 if topo.mates(src, c) else 1 if topo.same_plane(src, c) else 0, c))
+    eng = topo.engines(src, off[0])
+    half = len(off) - 2
+    w = len(eng) // half
+    first = [(d, eng[w * i:w * i + w]) for i, d in enumerate(off[:half])]
+    w = len(eng) // 2
+    second = [(d, eng[w * i:w * i + w]) for i, d in enumerate(off[half:])]
+    for d in here:
+        second.append((d, [e for e in topo.engines(src, d) if e not in eng]))
+    return [first, second]
+
+
+def rank_program(g, core, T, topo):
+    rank = T.rank_of(core)
+    if rank is None:
+        return
+    cores = list(T.cores)
+    E = {"V": g.vector, "S": g.scalar, "P": g.tensor, "G": g, "Y": g.sync}
+    cnt, known = {}, {e: {} for e in E}
+    wr, rd, bank = {}, {}, {}
+
+    def sync(e, R, W, B):
+        need = {}
+        toks = [wr[r] for r in list(R) + list(W) if r in wr]
+        for w in W:
+            toks += list(rd.get(w, {}).values())
+        for b in B:
+            toks += [t for f, t in bank.get(b, {}).items() if f != e]
+        for t in toks:
+            if t[0] not in need or need[t[0]][1] < t[1]:
+                need[t[0]] = t
+        for sem in sorted(need, key=lambda x: x == e):
+            sm, val, clk = need[sem]
+            if known[e].get(sm, 0) < val:
+                E[e].wait_ge(T.sem[sm], val)
+                for k2, v2 in clk.items():
+                    known[e][k2] = max(known[e].get(k2, 0), v2)
+                known[e][sm] = val
+
+    def note(e, tok, R, W, B):
+        for w in W:
+            wr[w] = tok
+            rd[w] = {}
+        for r in R:
+            rd.setdefault(r, {})[tok[0]] = tok
+        for b in B:
+            bank.setdefault(b, {})[e] = tok
+
+    def op(e, R, W, B, f):
+        sync(e, R, W, B)
+        ins = f()
+        for i in (ins if isinstance(ins, list) else [ins]):
+            i.then_inc(T.sem[e], 1)
+            cnt[e] = cnt.get(e, 0) + 1
+        note(e, (e, cnt[e], dict(known[e])), R, W, B)
+
+    def dma(e, sem, out, in_, R, W):
+        sync(e, R, W, [])
+        E[e].dma_start(out, in_).then_inc(T.sem[sem], 16)
+        cnt[sem] = cnt.get(sem, 0) + 16
+        note(e, (sem, cnt[sem], dict(known[e])), R, W, [])
+
+    v, s, p = g.vector, g.scalar, g.tensor
+
+    def copy(out, in_, R, W, B=()):
+        op("V", R, W, B, lambda: v.tensor_copy(out, in_))
+
+    def ts(out, in0, s1, op0, R, W, B=(), s2=None, op1=None):
+        if op1 is None:
+            op("V", R, W, B, lambda: v.tensor_scalar(out, in0, s1, None, op0))
+        else:
+            op("V", R, W, B, lambda: v.tensor_scalar(out, in0, s1, s2, op0, op1))
+
+    def tt(out, a, b, o, R, W, B=()):
+        op("V", R, W, B, lambda: v.tensor_tensor(out, a, b, o))
+
+    def scan(out, a, b, ini, o0, o1, R, W, B=()):
+        op("V", R, W, B, lambda: v.tensor_tensor_scan(out, a, b, ini, o0, o1))
+
+    def fill(ap, x, W):
+        op("V", [], W, [], lambda: v.memset(ap, x))
+
+    def iota(out, pat, base, cm, W, small=True):
+        op("G", [], W, [], lambda: g.iota(out, pat, base, cm, allow_small_or_imprecise_dtypes=True) if small
+           else g.iota(out, pat, base, cm))
+
+    def sel(out, in_, pat, cmp, fl, base, cm, R, W):
+        op("G", R, W, [], lambda: g.affine_select(out, in_, pat, cmp, fl, base, cm))
+
+    def X(name, c):
+        return T[name + str(c)]
+
+    def K(name, c, a=0, b=None, st=1):
+        buf, off, w = PACK[name]
+        return T[buf + str(c)][:, off + a:off + (w if b is None else b):st]
+
+    def fan(name, c, a=0, st=1):
+        return T[name][:, 2048 * c + a:2048 * c + 2048:st]
+
+    def C(name):
+        return T.KP[:, KP[name]:KP[name] + 128]
+
+    dma("S", "dc", T.CM[:], T.cm[:], [], ["CM"])
+    dma("Y", "ds", T.S3[:], T.s0[:], [], ["S3"])
+    dma("Y", "dz", T.Z3[:], T.z0[:], [], ["Z3"])
+    dma("Y", "dx", T.XW[:], T.x0[:], [], ["XW"])
+    fill(T.ON2[:], 1.0, ["ON2"])
+    fill(T.ON3[:], 1.0, ["ON3"])
+    iota(T.QI[:], [[-1, 16]], 0, 1, ["QI"], False)
+    sel(T.ID[:], T.ON2[:], [[-1, 128]], A.is_equal, 0.0, 0, 1, ["ON2"], ["ID"])
+    sel(T.BO[:], T.ON3[:, 0], [[-16, 8], [0, 16]], A.is_ge, 0.0, 0, 1, ["ON3"], ["BO"])
+    sel(T.BO[:], T.BO[:], [[16, 8], [0, 16]], A.is_ge, 0.0, 15, -1, ["BO"], ["BO"])
+    iota(C("KC16"), [[0, 8], [-16, 16]], 240, 0, ["KC16"])
+    iota(T.KCC[:], [[1, 4], [0, 8]], -4, 0, ["KCC"])
+    iota(C("KM7"), [[0, 8], [1, 16]], -7, 0, ["KM7"])
+    iota(C("KM2"), [[0, 8], [-1, 16]], -2, 0, ["KM2"])
+    sel(T.LS[:], T.ON3[:], [[-16, 8], [0, 8], [-1, 16]], A.is_equal, 0.0, 0, 1, ["ON3"], ["LS"])
+    iota(T.FQ[:], [[0, 4], [0, 8], [2048, 16]], -16384, 0, ["FQ"])
+    sel(T.FQ[:], T.FQ[:], [[-1, 4], [-12, 8], [0, 16]], A.is_equal, 0.0, -4, 1, ["FQ"], ["FQ"])
+    sel(T.FQ[:], T.FQ[:], [[-1, 4], [-12, 8], [0, 16]], A.not_equal, 1.0, 0, 1, ["FQ"], ["FQ"])
+    sel(T.FQ[:], T.FQ[:], [[-1, 4], [-12, 8], [0, 16]], A.not_equal, -1024.0, -8, 1, ["FQ"], ["FQ"])
+    sel(T.DG[:], T.ON2[:], [[0, 16], [-16, 8]], A.is_ge, 0.0, 0, 1, ["ON2"], ["DG"])
+    sel(T.DG[:], T.DG[:], [[0, 16], [16, 8]], A.is_ge, 0.0, 15, -1, ["DG"], ["DG"])
+    iota(T.BS[:, 0:16], [[16, 2], [32, 8]], 0, 0, ["BSa"], False)
+    iota(T.BS[:, 16:32], [[64, 2], [128, 8]], 0, 0, ["BSb"], False)
+    iota(T.BS[:, 32:48], [[2048, 2], [256, 8]], 15, 0, ["BSc"], False)
+    ts(T.QJ[:], T.QI[:], 15, A.bitwise_and, ["QI"], ["QJ"])
+    q = T.QC
+    copy(q[:, 0:1], T.QJ[:, 0:1], ["QJ"], ["q0"])
+    fill(T.RM[:], 1.0, ["RM"])
+    ts(q[:, 1:2], q[:, 0:1], 2.0, A.mult, ["q0"], ["q1"], (), 1.0, A.add)
+    ts(q[:, 2:3], q[:, 0:1], 4.0, A.mult, ["q0"], ["q2"])
+    ts(q[:, 3:4], q[:, 0:1], 16.0, A.mult, ["q0"], ["q3"])
+    ts(q[:, 4:5], q[:, 0:1], -8.0, A.add, ["q0"], ["q4"])
+    ts(T.RA[:], T.QJ[:], 0, A.is_equal, ["QJ"], ["RA"], (), 1024.0, A.mult)
+    ts(T.RB[:], T.QJ[:], 1, A.is_equal, ["QJ"], ["RB"], (), 1024.0, A.mult)
+    tt(q[:, 5:6], q[:, 4:5], q[:, 4:5], A.mult, ["q4"], ["q5"])
+    tt(T.RA[:, 0:15], T.RA[:, 0:15], T.RB[:, 0:15], A.subtract, ["RA", "RB"], ["RA"])
+    ts(q[:, 6:7], q[:, 5:6], -1024.0, A.mult, ["q5"], ["q6"])
+    copy(T.ID3[:], T.ID[:], ["ID"], ["ID3"])
+    ts(T.I613[:], T.ID[:], 613.0, A.mult, ["ID"], ["I613"])
+    ts(C("NI"), T.ID[:], -1.0, A.mult, ["ID"], ["NI"])
+    ts(C("I2"), T.ID[:], 2.0, A.mult, ["ID"], ["I2"])
+    ts(T.WB[:], T.BO[:, :, 0], q[:, 1:2], A.mult, ["BO", "q1"], ["WB"])
+    fill(T.RM8[:], 1.0, ["RM8"])
+    fill(T.KB0[:], 0.0, ["KB0"])
+    fill(T.KB1[:], 0.0, ["KB1"])
+    fill(T.RM[:, ::16], 0.0, ["RM"])
+    fill(T.RM8[:, ::8], 0.0, ["RM8"])
+    fill(T.MUL[:, 0:16], 256, ["MULa"])
+    fill(T.MUL[:, 16:32], 1, ["MULb"])
+    fill(T.MUL[:, 32:48], -1, ["MULc"])
+    for k in range(16):
+        ts(T.BK[:, k], T.BO[:], T.RA[:, k:k + 1], A.mult, ["BO", "RA"], ["BK%d" % k])
+
+    def late_constants():
+        for j, n in ((0, 0), (1, 2), (2, 3)):
+            ts(T.AD[:, 16 * j:16 * j + 16], T.BS[:, 16 * j:16 * j + 16], q[:, n:n + 1], A.add,
+               ["BS" + "abc"[j], "q%d" % n], ["AD" + "abc"[j]])
+
+    def gather(e, out, win, off, R, W):
+        if e == "V":
+            op("V", R, W, [], lambda: v.tensor_copy(out, win.indirect(off)))
+        else:
+            op("S", R, W, [], lambda: s.activation(out, win.indirect(off), AF.Copy))
+
+    def seats(t, c):
+        n = str(c)
+        if t == 0:
+            copy(X("OFS", c)[:], T.S3[:, :, c, :], ["S3"], ["OFS" + n])
+        else:
+            key = "RZ%d%d" % (t - 1, c)
+            ts(X("OFS", c)[:], T[key][:, :, 0:16], 0.0, A.add, [key, key + "o"], ["OFS" + n])
+
+    def zrow(t, c):
+        n = str(c)
+        if t == 0:
+            copy(X("ZC", c)[:], T.Z3[:, :, c, :], ["Z3"], ["ZC" + n])
+        else:
+            key = "RZ%d%d" % (t - 1, c)
+            copy(X("ZC", c)[:], T[key][:, :, 16:32], [key, key + "o"], ["ZC" + n])
+        Eb = X("E", c)
+        op("P", ["ZC" + n, "BO"], [], ["E" + n], lambda: [
+            p.matmul(Eb[:, 1], X("ZC", c)[:], T.BO[:], True, True),
+            p.matmul(Eb[:, 2, :, 0], X("ZC", c)[:], T.BO[:, :, 0], True, True)])
+
+    def part(name, c, a, b):
+        return T[name][:, 2048 * c + 16 * a:2048 * c + 16 * b]
+
+    def cgather(e, c, a, b):
+        gather(e, part("CG", c, a, b), T.CW[:, 0:1024], X("OFS", c)[:, a:b], ["CW", "OFS%d" % c],
+               ["CG%d%s" % (c, "b" if a else "a")])
+
+    def mgather(e, c, a, b):
+        gather(e, part("YG", c, a, b), T.MW[:, 0:1024], X("OFM", c)[:, a:b], ["MW", "OFM%d" % c],
+               ["YG%d%s" % (c, "b" if a else "a")])
+
+    def xgather(e, c):
+        gather(e, fan("XG", c), T.XW[:, 0:4096], X("OFX", c)[:, 0:128], ["XW", "OFX%d" % c], ["XG%d" % c])
+
+    def members(t, c):
+        n = str(c)
+        op("P", ["CG" + n + "a", "CG" + n + "b", "ID"], [], ["E" + n], lambda: [
+            p.matmul(X("E", c)[:, 0, :, k], fan("CG", c, k, 16), T.ID[:, (k + t) & 15::16], True, True) for k in range(16)])
+
+    def hashes(t, c):
+        n = str(c)
+        Eb, Qb, Lb = X("E", c), X("Q", c), X("L", c)
+        es, eq, u1, wi, hi = X("ES", c), X("EQ", c), X("U1", c), X("WI", c), X("HI", c)
+        EB = ["E" + n]
+        copy(es[:], Eb[:, 0], [], ["ES" + n], EB)
+        op("P", ["ES" + n, "ID"], [], ["L" + n], lambda: p.matmul(Lb[:, 0:128], es[:], T.ID[:], True, True))
+
+        def base():
+            r = [p.matmul(Qb[:, 0], T.ID[:], es[:], True, False)]
+            if t > 0:
+                r += [p.matmul(Qb[:, 0], T.ON2[:], X("O1", j)[:], False, False) for j in (0, 1)]
+            return r
+        op("P", ["ES" + n, "ID", "ON2", "O10", "O11"], [], ["Q" + n], base)
+        ts(u1[:], Eb[:, 1], 1.0, A.add, [], ["U1" + n], EB)
+
+        def equal(d):
+            tt(eq[:, d - 1, :, d:16], es[:, :, d:16], Eb[:, 0, :, 0:16 - d], A.is_equal, ["ES" + n], ["EQ%d_%d" % (c, d)], EB)
+            op("P", ["EQ%d_%d" % (c, d), "I613"], [], ["Q" + n],
+               lambda: p.matmul(Qb[:, 0, :, d:16], T.I613[:], eq[:, d - 1, :, d:16], False, d == 15))
+        equal(1)
+        equal(2)
+        copy(X("OFM", c)[:], Lb[:, 0:128], [], ["OFM" + n], ["L" + n])
+        tt(wi[:], u1[:], Eb[:, 0], A.mult, ["U1" + n], ["WI" + n], EB)
+        equal(3)
+        equal(4)
+        ts(wi[:], wi[:], 5, A.arith_shift_right, ["WI" + n], ["WI" + n])
+        copy(K("UI", c, 0, 8), Eb[:, 2, :, 0], [], ["UIa" + n], EB)
+        equal(5)
+        equal(6)
+        ts(K("UI", c, 8, 16), K("UI", c, 0, 8), 3, A.bitwise_and, ["UIa" + n], ["UIb" + n])
+        equal(7)
+        equal(8)
+        ts(X("U3", c)[:], K("UI", c, 8, 16), 256.0, A.mult, ["UIb" + n], ["U3" + n])
+        for d in range(9, 16):
+            equal(d)
+        copy(X("TT", c)[:, :, 0, :], es[:], ["ES" + n], ["TTa" + n])
+        tt(hi[:], wi[:], Qb[:, 0], A.add, ["WI" + n], ["HI" + n], ["Q" + n])
+        ts(hi[:], hi[:], 4095, A.bitwise_and, ["HI" + n], ["HI" + n])
+        ts(X("HF", c)[:], hi[:], -2048.0, A.add, ["HI" + n], ["HF" + n])
+        op("P", ["HF" + n, "ID"], [], ["L" + n], lambda: p.matmul(Lb[:, 0:128], X("HF", c)[:], T.ID[:], True, True))
+        ts(X("H8", c)[:], hi[:], 8, A.arith_shift_right, ["HI" + n], ["H8" + n])
+        ts(X("OFX", c)[:], Lb[:, 0:128], 2048.0, A.add, [], ["OFX" + n], ["L" + n])
+        tt(K("VK", c), X("H8", c)[:], C("KC16"), A.add, ["H8" + n, "KC16"], ["VK" + n])
+
+    def bins(c):
+        n = str(c)
+        op("P", ["XG" + n, "WB"], [], ["L" + n], lambda: [
+            p.matmul(X("L", c)[:, 128 + k:256:16], fan("XG", c, k, 16), T.WB[:], True, True) for k in range(16)])
+
+    def survivors(t, c):
+        n = str(c)
+        Lb, LB = X("L", c), ["L" + n]
+        bi, ind = X("BI", c), X("IN", c)
+        copy(bi[:], Lb[:, 128:256], [], ["BI" + n], LB)
+        ts(bi[:], bi[:], 3, A.bitwise_and, ["BI" + n], ["BI" + n])
+        ink = ["IN%d_%d" % (c, b) for b in range(4)]
+        for b in range(4):
+            ts(ind[:, 128 * b:128 * b + 128], bi[:], b, A.is_equal, ["BI" + n], [ink[b]], (), 4.0, A.mult)
+        scan(X("CT", c)[:], T.RM[:], ind[:], 0.0, A.mult, A.add, ["RM"] + ink, ["CT" + n])
+        tt(K("KI", c), X("CT", c)[:, 15::16], T.KCC[:], A.add, ["CT" + n, "KCC"], ["KI" + n])
+        ts(K("KI", c), K("KI", c), 127, A.bitwise_and, ["KI" + n], ["KI" + n])
+        tt(K("KJ", c, 0, 16), K("KI", c, 0, 16), K("KI", c, 16, 32), A.min, ["KI" + n], ["KJ" + n])
+        tt(K("KJ", c, 16, 24), K("KJ", c, 0, 8), K("KJ", c, 8, 16), A.min, ["KJ" + n], ["KK" + n])
+        ts(K("BN", c, 0, 8), K("KJ", c, 16, 24), 3, A.bitwise_and, ["KK" + n], ["BNa" + n])
+        ts(K("BN", c, 8, 16), K("KJ", c, 16, 24), 2, A.arith_shift_right, ["KK" + n], ["BNb" + n])
+        copy(X("KB", c)[:, ::16], K("BN", c), ["BNa" + n, "BNb" + n], ["KB" + n])
+        scan(X("BB", c)[:], T.RM[:, 0:256], X("KB", c)[:], 0.0, A.mult, A.add, ["RM", "KB" + n], ["BB" + n])
+        tt(K("SV", c), bi[:], X("BB", c)[:, 0:128], A.is_equal, ["BI" + n, "BB" + n], ["SV" + n])
+        op("P", ["SV" + n, "ID"], [], LB, lambda: p.matmul(Lb[:, 0:128], K("SV", c), T.ID[:], True, True))
+        scan(K("PR", c), T.RM[:, 0:128], K("SV", c), 0.0, A.mult, A.add, ["RM", "SV" + n], ["PR" + n])
+        ts(K("AL", c), Lb[:, 0:128], -2.0, A.add, [], ["AL" + n], LB)
+
+    def spread(c, ms):
+        n = str(c)
+        bks = ["BK%d" % k for k in range(16)]
+        for m in ms:
+            D, db = T["D%d" % (m & 1)], "D%d" % (m & 1)
+            op("P", ["AL" + n] + bks, [], [db], lambda: [
+                p.matmul(D[:, 128 * j:128 * j + 128], T.BK[:, 4 * m + j], K("AL", c), True, True) for j in range(4)])
+            op("S", [], ["DS%d_%d" % (c, m)], [db], lambda: [
+                s.activation(fan("DS", c, 4 * m + j, 16), D[:, 128 * j:128 * j + 128], AF.Copy) for j in range(4)])
+
+    def ranks(c):
+        n = str(c)
+        Lb, LB, bb = X("L", c), ["L" + n], X("BB", c)
+        op("P", ["PR" + n, "BB" + n, "ID", "NI", "I2", "KM7", "KM2"], [], LB, lambda: [
+            p.matmul(Lb[:, 384:512], T.ID[:], bb[:, 128:256], True, False),
+            p.matmul(Lb[:, 384:512], T.ID[:], C("KM7"), False, False),
+            p.matmul(Lb[:, 384:512], C("NI"), K("PR", c), False, True),
+            p.matmul(Lb[:, 256:384], C("NI"), bb[:, 128:256], True, False),
+            p.matmul(Lb[:, 256:384], T.ID[:], C("KM2"), False, False),
+            p.matmul(Lb[:, 256:384], C("I2"), K("PR", c), False, True)])
+
+    def places(t, c):
+        n = str(c)
+        Lb, LB = X("L", c), ["L" + n]
+        bb, TTb = X("BB", c), X("TT", c)
+        tt(K("SVL", c), K("SV", c), K("VK", c), A.mult, ["SV" + n, "VK" + n], ["SVL" + n])
+        if t < LEVELS - 1:
+            ts(X("O1", c)[:], bb[:, 128:256], 0.0, A.is_equal, ["BB" + n], ["O1" + n])
+        tt(K("TP", c), K("SV", c), Lb[:, 256:384], A.mult, ["SV" + n], ["TP" + n], LB)
+        scan(K("VM", c), T.RM[:, 0:128], K("SVL", c), 0.0, A.mult, A.max, ["RM", "SVL" + n], ["VM" + n])
+        tt(TTb[:, :, 1, :], K("TP", c), Lb[:, 384:512], A.add, ["TP" + n], ["TTb" + n], LB)
+        tt(X("VT", c)[:], K("VM", c, 15, 128, 16), X("U3", c)[:], A.add, ["VM" + n, "U3" + n], ["VT" + n])
+        tt(TTb[:, :, 2, :], TTb[:, :, 1, :], TTb[:, :, 1, :], A.mult, ["TTb" + n], ["TTc" + n])
+
+    def turn(c):
+        n = str(c)
+        o = 128 + 64 * c
+        op("P", ["VT" + n, "LS"], [], ["L0"], lambda: [
+            p.matmul(T.L0[:, o + 8 * b:o + 8 * b + 8], T.LS[:, b], X("VT", c)[:], True, True) for b in range(8)])
+
+    def lists():
+        r = T.RL
+        tt(T.LM[:], T.DG[:], T.L0[:, 128:256], A.mult, ["DG"], ["LM"], ["L0"])
+        scan(T.LV[:], T.RM8[:], T.LM[:], 0.0, A.mult, A.add, ["RM8", "LM"], ["LV"])
+        copy(T.VI[:], T.LV[:, 7::8], ["LV"], ["VI"])
+        ts(r[:, 0:16], T.VI[:], 15, A.bitwise_and, ["VI"], ["Ra"])
+        ts(r[:, 16:32], T.VI[:], 8, A.arith_shift_right, ["VI"], ["Rb"])
+        ts(r[:, 32:48], T.VI[:], 4, A.arith_shift_right, ["VI"], ["Rc"], (), 15, A.bitwise_and)
+        rr = ["Ra", "Rb", "Rc"]
+        tt(r[:], r[:], T.MUL[:], A.mult, rr + ["MULa", "MULb", "MULc"], rr)
+        tt(r[:], r[:], T.AD[:], A.add, rr + ["ADa", "ADb", "ADc"], rr)
+        copy(T.LST[:], r[:], rr, ["LST"])
+
+    def maximum(c, x):
+        n = str(c)
+        src = ["XG" + n] if x == "X" else ["YG" + n + "a", "YG" + n + "b"]
+        scan(fan(x + "S", c), fan(x + "G", c), fan("DS", c), -1024.0, A.max, A.add,
+             src + ["DS%d_%d" % (c, m) for m in range(4)], [x + "S" + n])
+
+    def leave(t, c):
+        n = str(c)
+        xs, ys = fan("XS", c, 15, 16), fan("YS", c, 15, 16)
+        if t == LEVELS - 1:
+            ts(T.OS[:, :, c, :], ys, 1024.0, A.add, ["YS" + n], ["OS" + n])
+            ts(T.OZ[:, :, c, :], xs, 1024.0, A.add, ["XS" + n], ["OZ" + n])
+            return
+        key = "%d%d" % (t, c)
+        sz, rz = T["SZ" + key], T["RZ" + key]
+        ts(sz[:, :, 0:16], ys, 1024.0, A.add, ["YS" + n], ["SZa" + key])
+        ts(sz[:, :, 16:32], xs, 1024.0, A.add, ["XS" + n], ["SZb" + key])
+        sync("G", ["SZa" + key, "SZb" + key], [], [])
+        for call in calls_of(core, cores, topo):
+            g.remote_dma_fused([RemoteDMATransfer(
+                src=sz[:, cores.index(d), :], dst=rz[:, rank, :],
+                dst_ids=[DstId(rid=topo.addr(d, core)[0], pnc=topo.addr(d, core)[1])],
+                dma_engine_mask=sum(1 << e for e in en), remote_sem=T.sem["arr" + key]) for d, en in call],
+                local_sem=T.sem["snt" + key])
+        copy(rz[:, rank, :], sz[:, rank, :], ["SZa" + key, "SZb" + key], ["RZ" + key + "o"])
+        total = sum(len(en) for o in cores if o != core for call in calls_of(o, cores, topo) for d, en in call if d == core)
+        wr["RZ" + key] = ("arr" + key, total, {})
+
+    def features(c):
+        n = str(c)
+        op("P", ["TTa" + n, "TTb" + n, "TTc" + n, "ID3"], [], ["E" + n], lambda: [
+            p.matmul(X("E", c)[0:96, j], X("TT", c)[:, :, :, j::4], T.ID3[:], True, True) for j in range(4)])
+        op("S", [], ["TL" + n], ["E" + n], lambda: s.activation(X("TL", c)[0:96], X("E", c)[0:96], AF.Copy))
+
+    def pick(c, j):
+        n = str(c)
+        b, key = (X("E", c), "E" + n) if j & 1 else (X("Q", c), "Q" + n)
+        op("P", ["TL" + n, "FQ"], [], [key], lambda: [
+            p.matmul(b[:, i], T.FQ[0:96, i], X("TL", c)[0:96, j], True, True) for i in range(4)])
+        op("S", ["q6"], ["FR%d_%d" % (c, j)], [key],
+           lambda: s.activation(X("FR", c)[:, 4 * j:4 * j + 4], b[:], AF.Relu, bias=T.QC[:, 6:7]))
+
+    def total(c, j):
+        op("P", ["FR%d_%d" % (c, j), "ID"], [], ["E0"], lambda: [
+            p.matmul(T.E0[:, c], T.ID[:], X("FR", c)[:, i], i == 0, i == 15) for i in range(4 * j, 4 * j + 4)])
+
+    def cwrite():
+        copy(T.FC[:], T.E0[:, 0:2], [], ["FC"], ["E0"])
+        op("V", ["FC", "LST"], ["CW"], [], lambda: v.tensor_copy(T.CW[:, 0:1024].indirect(T.LST[:, 16:32]), T.FC[:]))
+
+    def xnew():
+        ts(T.NZ[:], T.XS[:, 15::16], 1024.0, A.add, ["XS0", "XS1"], ["NZ"])
+        op("V", ["XG0", "XG1", "LST", "NZ"], ["XQ"], [], lambda: v.tensor_tensor(
+            T.XQ[:], T.XG[:, 0:4096].indirect(T.LST[:, 32:48]), T.NZ[:], A.add))
+        ts(T.XR[:], T.XQ[:], 1, A.arith_shift_right, ["XQ"], ["XR"])
+
+    def xwrite():
+        op("V", ["XR", "LST"], ["XW"], [], lambda: v.tensor_copy(T.XW[:, 0:4096].indirect(T.LST[:, 0:16]), T.XR[:]))
+
+    def weights(a, b):
+        iota(T.DI[:, a:b], [[1, b - a], [0, 128]], a + 1, 0, ["DI%d" % a])
+        sel(T.DI[:, a:b], T.DI[:, a:b], [[0, b - a], [-1, 128]], A.is_equal, 0.0, 0, 1, ["DI%d" % a], ["DI%d" % a])
+
+    for t in range(LEVELS):
+        last = t == LEVELS - 1
+        seats(t, 0)
+        if t == 0:
+            seats(t, 1)
+            ts(T.CW[:], T.CM[:], 1023, A.bitwise_and, ["CM"], ["CW"])
+        cgather("S", 0, 0, 64)
+        cgather("V", 0, 64, 128)
+        zrow(t, 0)
+        if t > 0:
+            seats(t, 1)
+        cgather("S", 1, 0, 64)
+        cgather("S", 1, 64, 128)
+        zrow(t, 1)
+        if t == 0:
+            ts(T.MW[:], T.CM[:], 10, A.arith_shift_right, ["CM"], ["MW"])
+        else:
+            xnew()
+        members(t, 0)
+        hashes(t, 0)
+        mgather("S", 0, 0, 64)
+        if t == 0:
+            late_constants()
+        else:
+            xwrite()
+        members(t, 1)
+        xgather("S", 0)
+        hashes(t, 1)
+        xgather("S", 1)
+        mgather("S", 1, 0, 64)
+        bins(0)
+        bins(1)
+        survivors(t, 0)
+        ranks(0)
+        spread(0, (0, 1, 2, 3))
+        places(t, 0)
+        features(0)
+        for j in range(4):
+            pick(0, j)
+        mgather("V", 0, 64, 128)
+        mgather("S", 1, 64, 128)
+        survivors(t, 1)
+        ranks(1)
+        spread(1, (0, 1))
+        places(t, 1)
+        features(1)
+        turn(0)
+        turn(1)
+        spread(1, (2, 3))
+        for j in range(4):
+            total(0, j)
+        pick(1, 0)
+        pick(1, 1)
+        total(1, 0)
+        pick(1, 2)
+        total(1, 1)
+        pick(1, 3)
+        total(1, 2)
+        total(1, 3)
+        maximum(0, "X")
+        maximum(0, "Y")
+        leave(t, 0)
+        maximum(1, "X")
+        maximum(1, "Y")
+        leave(t, 1)
+        if not last:
+            weights(32 * t, 32 * t + 16)
+            weights(32 * t + 16, 32 * t + 32)
+        lists()
+        if last:
+            xnew()
+            xwrite()
+        cwrite()
+    dma("Y", "os", T.ys[:], T.OS[:], ["OS0", "OS1"], [])
+    dma("Y", "oz", T.yz[:], T.OZ[:], ["OZ0", "OZ1"], [])
+    dis = ["DI0", "DI16", "DI32", "DI48"]
+    op("P", ["XW"] + dis, [], ["L0"], lambda: [
+        p.matmul(T.L0[:, 0:64], T.DI[:, m], T.XW[:, 64 * m:64 * m + 64], m == 0, m == 63) for m in range(64)])
+    copy(T.CF[:], T.CW[:], ["CW"], ["CF"])
+    op("P", ["CF"] + dis, [], ["L1"], lambda: [
+        p.matmul(T.L1[:, 0:64], T.DI[:, m], T.CF[:, 64 * m:64 * m + 64], m == 0, m == 15) for m in range(16)])
+    copy(T.OX[:], T.L0[:, 0:64], [], ["OX"], ["L0"])
+    dma("Y", "ox", T.yx[:], T.OX[:], ["OX"], [])
+    copy(T.OC[:], T.L1[:, 0:64], [], ["OC"], ["L1"])
+    dma("Y", "oc", T.yc[:], T.OC[:], ["OC"], [])
+    for sem in sorted(cnt):
+        g.wait_ge(T.sem[sem], cnt[sem])
+    for t in range(LEVELS - 1):
+        for c in (0, 1):
+            g.wait_ge(T.sem["snt%d%d" % (t, c)], sum(len(en) for call in calls_of(core, cores, topo) for d, en in call))

@@ -1,57 +1,49 @@
+import math
 from concourse.bass import DstId, RemoteDMATransfer
 from concourse.mybir import dt, AluOpType, AxisListType, ActivationFunctionType
 
 A = AluOpType
 AF = ActivationFunctionType
 LEVELS = 3
+TE = ("V", "V")
+P0 = (16, 11)
+LN2 = math.log(2.0)
 
 _B, _H, _F, _I, _U = "bfloat16", "float16", "float32", "int32", "uint16"
-PACK, _w = {}, {}
-for _b, _n, _c in [("B7", x, 128) for x in ("VK", "SV", "AL", "PR", "TP", "SVL", "VM")] + [
-        ("IS", "UI", 16), ("IS", "KI", 32), ("IS", "KJ", 24), ("IS", "BN", 16)]:
-    PACK[_n] = (_b, _w.get(_b, 0), _c)
-    _w[_b] = _w.get(_b, 0) + _c
-KP = {_n: 128 * _i for _i, _n in enumerate(("KM7", "KM2", "KC16", "NI", "I2"))}
+MATS = ("ON", "ID", "BO2", "BOM", "KU", "KQ", "AB", "CJ", "TA", "TU", "TB", "W2", "W3", "CA", "TRI")
+COLS = ("P", "P1", "p", "g16", "cv", "sg", "a", "b", "nd", "dw", "dg", "b1", "bA", "bB", "bV", "sF", "bF0", "bF1", "nb1", "acc", "t0", "t1", "a32")
 SCRATCH = {
     "XW": ("sbuf", [128, 4096], _B), "CM": ("sbuf", [128, 1024], _I), "CW": ("sbuf", [128, 1024], _I),
-    "MW": ("sbuf", [128, 1024], _I), "S3": ("sbuf", [128, 8, 2, 16], _I), "Z3": ("sbuf", [128, 8, 2, 16], _B),
-    "CF": ("sbuf", [128, 1024], _H),
-    "ON2": ("sbuf", [128, 128], _B), "ON3": ("sbuf", [128, 8, 8, 16], _B), "ID": ("sbuf", [128, 128], _B),
-    "ID3": ("sbuf", [128, 8, 16], _B), "BO": ("sbuf", [128, 8, 16], _B), "WB": ("sbuf", [128, 8], _B),
-    "LS": ("sbuf", [128, 8, 8, 16], _B), "DG": ("sbuf", [128, 128], _B), "FQ": ("sbuf", [128, 4, 8, 16], _B),
-    "BK": ("sbuf", [128, 16, 8, 16], _B), "I613": ("sbuf", [128, 128], _H), "KP": ("sbuf", [128, 640], _B),
-    "RM": ("sbuf", [128, 512], _B), "RM8": ("sbuf", [128, 128], _B), "KCC": ("sbuf", [128, 32], _B),
-    "MUL": ("sbuf", [128, 48], _I), "AD": ("sbuf", [128, 48], _I), "BS": ("sbuf", [128, 48], _I),
-    "QI": ("sbuf", [128, 16], _I), "QJ": ("sbuf", [128, 16], _I), "QC": ("sbuf", [128, 16], _F),
-    "RA": ("sbuf", [128, 16], _F), "RB": ("sbuf", [128, 16], _F), "DI": ("sbuf", [128, 64, 128], _B),
+    "S3": ("sbuf", [128, 8, 2, 16], _I), "Z3": ("sbuf", [128, 8, 2, 16], _B), "CF": ("sbuf", [128, 1024], _H),
+    "MT": ("sbuf", [128, len(MATS), 128], _B), "BO": ("sbuf", [128, 8, 16], _B), "QC": ("sbuf", [128, 32], _F),
+    "QB": ("sbuf", [128, 2], _B), "QI": ("sbuf", [128, 16], _I), "QJ": ("sbuf", [128, 16], _I), "QK": ("sbuf", [128, 4], _I),
+    "CI": ("sbuf", [128, 144], _B), "PT": ("sbuf", [128, 16], _F), "PS": ("sbuf", [128, 16, 144], _B),
+    "ZS": ("sbuf", [128, 3, 144], _B), "JI": ("sbuf", [128, 2, 8], _I), "JT": ("sbuf", [128, 2, 8], _F),
+    "WD": ("sbuf", [128, 8, 128], _B), "RD": ("sbuf", [128, 8, 128], _H), "BK": ("sbuf", [128, 16, 128], _B),
+    "RA": ("sbuf", [128, 16], _F), "RB": ("sbuf", [128, 16], _F), "CR": ("sbuf", [128, 8], _I), "EA": ("sbuf", [128, 3, 8], _F),
+    "W1": ("sbuf", [128, 4, 128], _B), "W1T": ("sbuf", [128, 4, 128], _B),
+    "AD": ("sbuf", [128, 32], _I), "BS": ("sbuf", [128, 32], _I), "DI": ("sbuf", [128, 64, 128], _B),
     "CG": ("sbuf", [128, 4096], _H), "YG": ("sbuf", [128, 4096], _H), "XG": ("sbuf", [128, 4096], _B),
     "XS": ("sbuf", [128, 4096], _H), "YS": ("sbuf", [128, 4096], _H), "DS": ("sbuf", [128, 4096], _B),
-    "LM": ("sbuf", [128, 128], _H), "LV": ("sbuf", [128, 128], _H), "VI": ("sbuf", [128, 16], _I),
-    "RL": ("sbuf", [128, 48], _I), "LST": ("sbuf", [128, 48], _U), "NZ": ("sbuf", [128, 256], _H),
-    "XQ": ("sbuf", [128, 256], _I), "XR": ("sbuf", [128, 256], _I), "FC": ("sbuf", [128, 256], _F),
+    "OFS": ("sbuf", [128, 256], _U), "OFM": ("sbuf", [128, 256], _U), "OFX": ("sbuf", [128, 256], _U),
+    "ES": ("sbuf", [128, 256], _H), "EQ": ("sbuf", [128, 2, 8, 128], _B), "XX": ("sbuf", [128, 256], _F),
+    "HI": ("sbuf", [128, 256], _I), "HH": ("sbuf", [128, 256], _H), "QS": ("sbuf", [128, 256], _H),
+    "RR": ("sbuf", [128, 4, 256], _H), "T1": ("sbuf", [128, 256], _B), "T2": ("sbuf", [128, 256], _B),
+    "AL": ("sbuf", [128, 256], _B), "PW": ("sbuf", [128, 2, 256], _B), "VV": ("sbuf", [128, 256], _H),
+    "CL": ("sbuf", [128, 16, 256], _H), "VL": ("sbuf", [128, 256], _H), "JK": ("sbuf", [128, 256], _B),
+    "FC": ("sbuf", [128, 256], _F), "XQ": ("sbuf", [128, 256], _I),
+    "LI": ("sbuf", [128, 64], _I), "LC": ("sbuf", [128, 16], _U), "LX": ("sbuf", [128, 32], _U),
+    "Z0": ("sbuf", [128, 512], _H),
+    "SZ0": ("sbuf", [128, 512], _H), "SZ1": ("sbuf", [128, 512], _H), "SZ2": ("sbuf", [128, 512], _H),
+    "RZ0": ("sbuf", [128, 512], _H), "RZ1": ("sbuf", [128, 512], _H),
     "OS": ("sbuf", [128, 8, 2, 16], _F), "OZ": ("sbuf", [128, 8, 2, 16], _B),
     "OX": ("sbuf", [128, 64], _F), "OC": ("sbuf", [128, 64], _F),
+    "E0": ("psum", [128, 4, 128], _F), "E1": ("psum", [128, 4, 128], _F),
+    "Q0": ("psum", [128, 4, 128], _F), "Q1": ("psum", [128, 4, 128], _F),
     "D0": ("psum", [128, 512], _F), "D1": ("psum", [128, 512], _F),
+    "X1": ("psum", [128, 512], _F), "X2": ("psum", [128, 512], _F),
 }
-for _c in "01":
-    SCRATCH.update({
-        "E" + _c: ("psum", [128, 4, 8, 16], _F), "Q" + _c: ("psum", [128, 4, 8, 16], _F),
-        "L" + _c: ("psum", [128, 512], _F),
-        "B7" + _c: ("sbuf", [128, _w["B7"]], _B), "IS" + _c: ("sbuf", [128, _w["IS"]], _I),
-        "ZC" + _c: ("sbuf", [128, 128], _H), "OFS" + _c: ("sbuf", [128, 128], _U), "OFM" + _c: ("sbuf", [128, 128], _U),
-        "OFX" + _c: ("sbuf", [128, 128], _U),
-        "ES" + _c: ("sbuf", [128, 8, 16], _H), "EQ" + _c: ("sbuf", [128, 15, 8, 16], _B),
-        "U1" + _c: ("sbuf", [128, 8, 16], _F), "U3" + _c: ("sbuf", [128, 8], _F),
-        "WI" + _c: ("sbuf", [128, 8, 16], _I), "HI" + _c: ("sbuf", [128, 8, 16], _I), "H8" + _c: ("sbuf", [128, 8, 16], _I),
-        "HF" + _c: ("sbuf", [128, 8, 16], _H), "BI" + _c: ("sbuf", [128, 128], _I),
-        "IN" + _c: ("sbuf", [128, 512], _B), "CT" + _c: ("sbuf", [128, 512], _B), "KB" + _c: ("sbuf", [128, 256], _B),
-        "BB" + _c: ("sbuf", [128, 256], _B),
-        "TT" + _c: ("sbuf", [128, 8, 3, 16], _H), "TL" + _c: ("sbuf", [128, 4, 8, 16], _H),
-        "FR" + _c: ("sbuf", [128, 16, 8, 16], _H), "O1" + _c: ("sbuf", [128, 8, 16], _B), "VT" + _c: ("sbuf", [128, 8], _H),
-        "SZ0" + _c: ("sbuf", [128, 8, 32], _H), "SZ1" + _c: ("sbuf", [128, 8, 32], _H),
-        "RZ0" + _c: ("sbuf", [128, 8, 32], _H), "RZ1" + _c: ("sbuf", [128, 8, 32], _H),
-    })
-SEMAPHORES = ["V", "S", "P", "G", "ds", "dz", "dc", "dx", "os", "oz", "ox", "oc"] + [
+SEMAPHORES = ["V", "S", "P", "G", "ds", "dz", "dc0", "dc1", "dx", "os", "oz", "ox", "oc"] + [
     k + t + c for k in ("arr", "snt") for t in "01" for c in "01"]
 
 
@@ -140,6 +132,19 @@ def rank_program(g, core, T, topo):
     def fill(ap, x, W):
         op("V", [], W, [], lambda: v.memset(ap, x))
 
+    def act(out, in_, fn, R, W, B=(), bias=0.0, scale=1.0, acc=None):
+        op("S", R, W, B, lambda: s.activation(out, in_, fn, bias=bias, scale=scale, accum_out=acc))
+
+    def lin(e, out, in_, scale, bias, R, W, B=()):
+        if e == "V":
+            ts(out, in_, scale, A.mult, R, W, B, bias, A.add)
+        else:
+            act(out, in_, AF.Identity, R, W, B, bias, scale)
+
+    def mm(out, terms, R, B, start=True, stop=True):
+        n = len(terms)
+        op("P", R, [], B, lambda: [p.matmul(out, a, b, start and i == 0, stop and i == n - 1) for i, (a, b) in enumerate(terms)])
+
     def iota(out, pat, base, cm, W, small=True):
         op("G", [], W, [], lambda: g.iota(out, pat, base, cm, allow_small_or_imprecise_dtypes=True) if small
            else g.iota(out, pat, base, cm))
@@ -147,396 +152,494 @@ def rank_program(g, core, T, topo):
     def sel(out, in_, pat, cmp, fl, base, cm, R, W):
         op("G", R, W, [], lambda: g.affine_select(out, in_, pat, cmp, fl, base, cm))
 
-    def X(name, c):
-        return T[name + str(c)]
+    def M(name):
+        return T.MT[:, MATS.index(name)]
 
-    def K(name, c, a=0, b=None, st=1):
-        buf, off, w = PACK[name]
-        return T[buf + str(c)][:, off + a:off + (w if b is None else b):st]
+    def q(name):
+        i = COLS.index(name)
+        return T.QC[:, i:i + 1]
 
-    def fan(name, c, a=0, st=1):
-        return T[name][:, 2048 * c + a:2048 * c + 2048:st]
+    def col(name, src, s1, o0, s2=None, o1=None):
+        R = [x for x in (src, s1, s2) if isinstance(x, str)]
+        ts(q(name), q(src), q(s1) if isinstance(s1, str) else s1, o0, R, [name], (), q(s2) if isinstance(s2, str) else s2, o1)
 
-    def C(name):
-        return T.KP[:, KP[name]:KP[name] + 128]
+    def H(name, c):
+        return T[name][:, 128 * c:128 * c + 128]
 
-    dma("S", "dc", T.CM[:], T.cm[:], [], ["CM"])
+    def slide(j, k):
+        return T.ZS[:, j, 15 - k:143 - k]
+
+    dma("S", "dc0", T.CM[:, 0:512], T.cm[:, 0:512], [], ["CM0"])
     dma("Y", "ds", T.S3[:], T.s0[:], [], ["S3"])
+    dma("Y", "dc1", T.CM[:, 512:1024], T.cm[:, 512:1024], [], ["CM1"])
     dma("Y", "dz", T.Z3[:], T.z0[:], [], ["Z3"])
     dma("Y", "dx", T.XW[:], T.x0[:], [], ["XW"])
-    fill(T.ON2[:], 1.0, ["ON2"])
-    fill(T.ON3[:], 1.0, ["ON3"])
-    iota(T.QI[:], [[-1, 16]], 0, 1, ["QI"], False)
-    sel(T.ID[:], T.ON2[:], [[-1, 128]], A.is_equal, 0.0, 0, 1, ["ON2"], ["ID"])
-    sel(T.BO[:], T.ON3[:, 0], [[-16, 8], [0, 16]], A.is_ge, 0.0, 0, 1, ["ON3"], ["BO"])
-    sel(T.BO[:], T.BO[:], [[16, 8], [0, 16]], A.is_ge, 0.0, 15, -1, ["BO"], ["BO"])
-    iota(C("KC16"), [[0, 8], [-16, 16]], 240, 0, ["KC16"])
-    iota(T.KCC[:], [[1, 4], [0, 8]], -4, 0, ["KCC"])
-    iota(C("KM7"), [[0, 8], [1, 16]], -7, 0, ["KM7"])
-    iota(C("KM2"), [[0, 8], [-1, 16]], -2, 0, ["KM2"])
-    sel(T.LS[:], T.ON3[:], [[-16, 8], [0, 8], [-1, 16]], A.is_equal, 0.0, 0, 1, ["ON3"], ["LS"])
-    iota(T.FQ[:], [[0, 4], [0, 8], [2048, 16]], -16384, 0, ["FQ"])
-    sel(T.FQ[:], T.FQ[:], [[-1, 4], [-12, 8], [0, 16]], A.is_equal, 0.0, -4, 1, ["FQ"], ["FQ"])
-    sel(T.FQ[:], T.FQ[:], [[-1, 4], [-12, 8], [0, 16]], A.not_equal, 1.0, 0, 1, ["FQ"], ["FQ"])
-    sel(T.FQ[:], T.FQ[:], [[-1, 4], [-12, 8], [0, 16]], A.not_equal, -1024.0, -8, 1, ["FQ"], ["FQ"])
-    sel(T.DG[:], T.ON2[:], [[0, 16], [-16, 8]], A.is_ge, 0.0, 0, 1, ["ON2"], ["DG"])
-    sel(T.DG[:], T.DG[:], [[0, 16], [16, 8]], A.is_ge, 0.0, 15, -1, ["DG"], ["DG"])
-    iota(T.BS[:, 0:16], [[16, 2], [32, 8]], 0, 0, ["BSa"], False)
-    iota(T.BS[:, 16:32], [[64, 2], [128, 8]], 0, 0, ["BSb"], False)
-    iota(T.BS[:, 32:48], [[2048, 2], [256, 8]], 15, 0, ["BSc"], False)
-    ts(T.QJ[:], T.QI[:], 15, A.bitwise_and, ["QI"], ["QJ"])
-    q = T.QC
-    copy(q[:, 0:1], T.QJ[:, 0:1], ["QJ"], ["q0"])
-    fill(T.RM[:], 1.0, ["RM"])
-    ts(q[:, 1:2], q[:, 0:1], 2.0, A.mult, ["q0"], ["q1"], (), 1.0, A.add)
-    ts(q[:, 2:3], q[:, 0:1], 4.0, A.mult, ["q0"], ["q2"])
-    ts(q[:, 3:4], q[:, 0:1], 16.0, A.mult, ["q0"], ["q3"])
-    ts(q[:, 4:5], q[:, 0:1], -8.0, A.add, ["q0"], ["q4"])
-    ts(T.RA[:], T.QJ[:], 0, A.is_equal, ["QJ"], ["RA"], (), 1024.0, A.mult)
-    ts(T.RB[:], T.QJ[:], 1, A.is_equal, ["QJ"], ["RB"], (), 1024.0, A.mult)
-    tt(q[:, 5:6], q[:, 4:5], q[:, 4:5], A.mult, ["q4"], ["q5"])
-    tt(T.RA[:, 0:15], T.RA[:, 0:15], T.RB[:, 0:15], A.subtract, ["RA", "RB"], ["RA"])
-    ts(q[:, 6:7], q[:, 5:6], -1024.0, A.mult, ["q5"], ["q6"])
-    copy(T.ID3[:], T.ID[:], ["ID"], ["ID3"])
-    ts(T.I613[:], T.ID[:], 613.0, A.mult, ["ID"], ["I613"])
-    ts(C("NI"), T.ID[:], -1.0, A.mult, ["ID"], ["NI"])
-    ts(C("I2"), T.ID[:], 2.0, A.mult, ["ID"], ["I2"])
-    ts(T.WB[:], T.BO[:, :, 0], q[:, 1:2], A.mult, ["BO", "q1"], ["WB"])
-    fill(T.RM8[:], 1.0, ["RM8"])
-    fill(T.KB0[:], 0.0, ["KB0"])
-    fill(T.KB1[:], 0.0, ["KB1"])
-    fill(T.RM[:, ::16], 0.0, ["RM"])
-    fill(T.RM8[:, ::8], 0.0, ["RM8"])
-    fill(T.MUL[:, 0:16], 256, ["MULa"])
-    fill(T.MUL[:, 16:32], 1, ["MULb"])
-    fill(T.MUL[:, 32:48], -1, ["MULc"])
-    for k in range(16):
-        ts(T.BK[:, k], T.BO[:], T.RA[:, k:k + 1], A.mult, ["BO", "RA"], ["BK%d" % k])
 
-    def late_constants():
-        for j, n in ((0, 0), (1, 2), (2, 3)):
-            ts(T.AD[:, 16 * j:16 * j + 16], T.BS[:, 16 * j:16 * j + 16], q[:, n:n + 1], A.add,
-               ["BS" + "abc"[j], "q%d" % n], ["AD" + "abc"[j]])
+    def first_constants():
+        fill(M("ON"), 1.0, ["ON"])
+        iota(T.QI[:], [[-1, 16]], 0, 1, ["QI"], False)
+        iota(T.QC[:, 0:2], [[1, 2]], 0, 1, ["P", "P1"])
+        iota(T.CI[:], [[1, 144]], 1, 0, ["CI"])
+        iota(T.JI[:, 0], [[1, 8]], 1, 1, ["JIa"], False)
+        iota(T.JI[:, 1], [[-1, 8]], -1, 1, ["JIb"], False)
+        iota(M("CJ"), [[1, 128]], 0, 0, ["CJ"])
+        sel(T.BO[:], M("ON"), [[-16, 8], [0, 16]], A.is_ge, 0.0, 0, 1, ["ON"], ["BO"])
+        sel(T.BO[:], T.BO[:], [[16, 8], [0, 16]], A.is_ge, 0.0, 15, -1, ["BO"], ["BO"])
+        sel(M("ID"), M("ON"), [[-1, 128]], A.is_equal, 0.0, 0, 1, ["ON"], ["ID"])
+        fill(M("KU"), 41.0 / 128, ["KU"])
+        fill(M("KQ"), (4096 - 41 * 1024) / 128, ["KQ"])
+        fill(M("AB"), -4096.0, ["AB"])
+        ts(T.QJ[:], T.QI[:], 15, A.bitwise_and, ["QI"], ["QJ"])
+        copy(q("p"), T.QJ[:, 0:1], ["QJ"], ["p"])
+        ts(T.JI[:], T.JI[:], 15, A.bitwise_and, ["JIa", "JIb"], ["JIa", "JIb"])
+        col("g16", "P", "p", A.subtract)
+        col("cv", "g16", 16.0, A.add)
+        ts(T.JT[:, 0], T.JI[:, 0], q("g16"), A.add, ["JIa", "g16"], ["JTa"])
+        ts(T.JT[:, 1], T.JI[:, 1], q("p"), A.max, ["JIb", "g16", "p"], ["JTb"], (), q("g16"), A.add)
+        ts(T.PT[:], T.QJ[:], 0, A.is_equal, ["QJ", "cv"], ["PT"], (), q("cv"), A.mult)
+        for r in range(16):
+            ts(T.PS[:, r], T.CI[:], T.PT[:, r:r + 1], A.is_equal, ["CI", "PT"], ["PS%d" % r])
+        for d in range(8):
+            ts(T.WD[:, d], M("CJ"), T.JT[:, 0, d:d + 1], A.is_equal, ["CJ", "JTa"], ["WD%d" % d], (), -1.0, A.mult)
+        wd = ["WD%d" % d for d in range(8)]
+        sel(T.WD[:], T.WD[:], [[0, 8], [-1, 128]], A.not_equal, 1.0, 0, 1, wd, wd)
+        scalar_constants()
+        act(M("BO2"), T.BO[:], AF.Copy, ["BO"], ["BO2"], scale=2.0)
+        act(M("BOM"), T.BO[:], AF.Copy, ["BO"], ["BOM"], scale=-2048.0)
+        for c in (0, 1):
+            act(T.Z0[:, 256 * c + 1:256 * c + 256:2], T.Z3[:, :, c, :], AF.Identity, ["Z3"], ["Z0%d" % c], bias=-0.25, scale=0.5)
 
-    def gather(e, out, win, off, R, W):
-        if e == "V":
-            op("V", R, W, [], lambda: v.tensor_copy(out, win.indirect(off)))
-        else:
-            op("S", R, W, [], lambda: s.activation(out, win.indirect(off), AF.Copy))
+    def second_constants():
+        for d in range(8):
+            ts(T.RD[:, d], M("CJ"), T.JT[:, 1, d:d + 1], A.is_equal, ["CJ", "JTb"], ["RD%d" % d], (),
+               613.0 * (32 if d < 7 else 16), A.mult)
+        ts(T.RA[:], T.QJ[:], 0, A.is_equal, ["QJ"], ["RA"], (), 256.0, A.mult)
+        ts(T.RB[:], T.QJ[:], 1, A.is_equal, ["QJ"], ["RB"], (), 256.0, A.mult)
+        ts(T.QK[:, 0:1], T.QJ[:, 0:1], 1, A.bitwise_and, ["QJ"], ["QK0"])
+        ts(T.QK[:, 1:2], T.QJ[:, 0:1], 2, A.arith_shift_right, ["QJ"], ["QK1"])
+        ts(T.QK[:, 2:3], T.QJ[:, 0:1], 3, A.bitwise_and, ["QJ"], ["QK2"])
+        tt(T.RA[:, 0:15], T.RA[:, 0:15], T.RB[:, 0:15], A.subtract, ["RA", "RB"], ["RA"])
+        ts(q("sg"), T.QK[:, 0:1], -1.0, A.mult, ["QK0"], ["sg"], (), 0.5, A.add)
+        copy(q("a"), T.QK[:, 1:2], ["QK1"], ["a"])
+        copy(q("b"), T.QK[:, 2:3], ["QK2"], ["b"])
+        iota(T.CR[:], [[-1, 8]], 4, 0, ["CR"], False)
+        iota(M("CA"), [[0, 8], [1, 4], [0, 4]], 0, 0, ["CA"])
+        sel(M("TRI"), T.BO[:], [[1, 128]], A.is_gt, 0.0, 0, -1, ["BO"], ["TRI"])
+        sel(M("TU"), T.BO[:], [[-1, 128]], A.is_gt, 0.0, 0, 1, ["BO"], ["TU"])
+        sel(M("TA"), M("TRI"), [[-1, 128]], A.not_equal, 64.0, 0, 1, ["TRI"], ["TA"])
+        sel(M("TB"), M("TRI"), [[-1, 128]], A.not_equal, -64.0, 0, 1, ["TRI"], ["TB"])
+        sel(M("TU"), M("TU"), [[-1, 128]], A.not_equal, -64.0, 0, 1, ["TU"], ["TU"])
+        iota(T.BS[:, 0:16], [[128, 2], [16, 8]], 0, 0, ["BSa"], False)
+        iota(T.BS[:, 16:32], [[16, 2], [32, 8]], 0, 0, ["BSb"], False)
 
-    def seats(t, c):
-        n = str(c)
-        if t == 0:
-            copy(X("OFS", c)[:], T.S3[:, :, c, :], ["S3"], ["OFS" + n])
-        else:
-            key = "RZ%d%d" % (t - 1, c)
-            ts(X("OFS", c)[:], T[key][:, :, 0:16], 0.0, A.add, [key, key + "o"], ["OFS" + n])
+    def third_constants():
+        ts(T.ZS[:, 0], T.CI[:], q("cv"), A.is_equal, ["CI", "cv"], ["ZS0"])
+        ts(T.ZS[:, 1], T.CI[:], q("cv"), A.is_equal, ["CI", "cv", "sg"], ["ZS1"], (), q("sg"), A.mult)
+        tt(T.ZS[:, 2, 0:143], T.ZS[:, 0, 0:143], T.ZS[:, 0, 1:144], A.subtract, ["ZS0"], ["ZS2"])
+        ts(T.CR[:], T.CR[:], 3, A.bitwise_and, ["CR"], ["CR"])
+        col("nd", "a", "b", A.not_equal)
+        col("dg", "a", "b", A.is_equal, -1.0, A.mult)
+        col("dw", "a", "b", A.is_equal, 4.0, A.mult)
+        col("t0", "a", "b", A.is_lt, -0.5, A.add)
+        col("a32", "a", 1.0 / (32 if TE[1] == "S" else 16), A.mult)
+        ts(T.EA[:, 0], T.CR[:], q("a"), A.is_equal, ["CR", "a", "nd"], ["EA0"], (), q("nd"), A.mult)
+        ts(T.EA[:, 1], T.CR[:], q("b"), A.is_equal, ["CR", "b"], ["EA1"])
+        col("dw", "dw", 1.0, A.add)
+        tt(T.EA[:, 1], T.EA[:, 1], T.EA[:, 0], A.subtract, ["EA0", "EA1"], ["EA1"])
+        ts(M("W2"), M("CA"), q("a"), A.is_equal, ["CA", "a", "dw"], ["W2"], (), q("dw"), A.mult)
+        tt(T.EA[:, 2, 0:4], T.EA[:, 1, 0:4], T.EA[:, 1, 1:5], A.subtract, ["EA1"], ["EA2"])
+        ts(q("b1"), T.EA[:, 1, 0:1], 16.0, A.mult, ["EA1", "t0"], ["b1"], (), q("t0"), A.add)
+        ts(M("W2"), M("W2"), q("dg"), A.add, ["W2", "dg"], ["W2"])
+        col("nb1", "b1", -1.0, A.mult)
+        ts(M("W3"), T.BO[:], q("a32"), A.mult, ["BO", "a32"], ["W3"])
+        for i in range(4):
+            ts(T.W1T[:, i], T.BO[:], T.EA[:, 2, i:i + 1], A.mult, ["BO", "EA2"], ["W1T%d" % i])
+        tt(M("W2"), M("W2"), T.BO[:], A.mult, ["W2", "BO"], ["W2"])
+        for i in range(4):
+            mm(T.X1[:, 128 * i:128 * i + 128], [(T.W1T[:, i], M("ID"))], ["W1T%d" % i, "ID"], ["X1"])
+        col("bA", "p", 2 * LN2, A.mult, 53 * LN2, A.add)
+        col("bB", "p", -LN2, A.mult, -109 * LN2, A.add)
+        col("bV", "p", -126976.0, A.mult, 3801088.0, A.add)
+        for c in (0, 1):
+            b = "bF%d" % c
+            col(b, "p", P0[c] - 0.5, A.is_gt, 16384.0, A.mult)
+            ts(q("t1"), q("p"), 1024.0, A.mult, ["p"], ["t1"], (), -31744.0, A.add) if c == 0 else None
+            col(b, b, "t1", A.add)
+        copy(T.W1[:], T.X1[:], [], ["W1"], ["X1"])
+        ts(T.BS[:], T.BS[:], q("p"), A.add, ["BSa", "BSb", "p"], ["BSa", "BSb"])
+        ts(T.AD[:, 0:16], T.BS[:, 0:16], 65536.0, A.mult, ["BSa"], ["ADa"])
+        ts(T.AD[:, 16:32], T.BS[:, 16:32], 4.0, A.mult, ["BSb"], ["ADb"])
+        tt(T.AD[:, 0:16], T.AD[:, 0:16], T.BS[:, 16:32], A.add, ["ADa", "BSb"], ["ADa"])
 
-    def zrow(t, c):
-        n = str(c)
-        if t == 0:
-            copy(X("ZC", c)[:], T.Z3[:, :, c, :], ["Z3"], ["ZC" + n])
-        else:
-            key = "RZ%d%d" % (t - 1, c)
-            copy(X("ZC", c)[:], T[key][:, :, 16:32], [key, key + "o"], ["ZC" + n])
-        Eb = X("E", c)
-        op("P", ["ZC" + n, "BO"], [], ["E" + n], lambda: [
-            p.matmul(Eb[:, 1], X("ZC", c)[:], T.BO[:], True, True),
-            p.matmul(Eb[:, 2, :, 0], X("ZC", c)[:], T.BO[:, :, 0], True, True)])
+    def scalar_constants():
+        act(T.QB[:, 0:1], q("p"), AF.Exp, ["p"], ["QB"], bias=11 * LN2, scale=-LN2)
+        act(q("sF"), T.QB[:, 0:1], AF.Copy, ["QB"], ["sF"])
 
-    def part(name, c, a, b):
-        return T[name][:, 2048 * c + 16 * a:2048 * c + 16 * b]
-
-    def cgather(e, c, a, b):
-        gather(e, part("CG", c, a, b), T.CW[:, 0:1024], X("OFS", c)[:, a:b], ["CW", "OFS%d" % c],
-               ["CG%d%s" % (c, "b" if a else "a")])
-
-    def mgather(e, c, a, b):
-        gather(e, part("YG", c, a, b), T.MW[:, 0:1024], X("OFM", c)[:, a:b], ["MW", "OFM%d" % c],
-               ["YG%d%s" % (c, "b" if a else "a")])
-
-    def xgather(e, c):
-        gather(e, fan("XG", c), T.XW[:, 0:4096], X("OFX", c)[:, 0:128], ["XW", "OFX%d" % c], ["XG%d" % c])
-
-    def members(t, c):
-        n = str(c)
-        op("P", ["CG" + n + "a", "CG" + n + "b", "ID"], [], ["E" + n], lambda: [
-            p.matmul(X("E", c)[:, 0, :, k], fan("CG", c, k, 16), T.ID[:, (k + t) & 15::16], True, True) for k in range(16)])
-
-    def hashes(t, c):
-        n = str(c)
-        Eb, Qb, Lb = X("E", c), X("Q", c), X("L", c)
-        es, eq, u1, wi, hi = X("ES", c), X("EQ", c), X("U1", c), X("WI", c), X("HI", c)
-        EB = ["E" + n]
-        copy(es[:], Eb[:, 0], [], ["ES" + n], EB)
-        op("P", ["ES" + n, "ID"], [], ["L" + n], lambda: p.matmul(Lb[:, 0:128], es[:], T.ID[:], True, True))
-
-        def base():
-            r = [p.matmul(Qb[:, 0], T.ID[:], es[:], True, False)]
-            if t > 0:
-                r += [p.matmul(Qb[:, 0], T.ON2[:], X("O1", j)[:], False, False) for j in (0, 1)]
-            return r
-        op("P", ["ES" + n, "ID", "ON2", "O10", "O11"], [], ["Q" + n], base)
-        ts(u1[:], Eb[:, 1], 1.0, A.add, [], ["U1" + n], EB)
-
-        def equal(d):
-            tt(eq[:, d - 1, :, d:16], es[:, :, d:16], Eb[:, 0, :, 0:16 - d], A.is_equal, ["ES" + n], ["EQ%d_%d" % (c, d)], EB)
-            op("P", ["EQ%d_%d" % (c, d), "I613"], [], ["Q" + n],
-               lambda: p.matmul(Qb[:, 0, :, d:16], T.I613[:], eq[:, d - 1, :, d:16], False, d == 15))
-        equal(1)
-        equal(2)
-        copy(X("OFM", c)[:], Lb[:, 0:128], [], ["OFM" + n], ["L" + n])
-        tt(wi[:], u1[:], Eb[:, 0], A.mult, ["U1" + n], ["WI" + n], EB)
-        equal(3)
-        equal(4)
-        ts(wi[:], wi[:], 5, A.arith_shift_right, ["WI" + n], ["WI" + n])
-        copy(K("UI", c, 0, 8), Eb[:, 2, :, 0], [], ["UIa" + n], EB)
-        equal(5)
-        equal(6)
-        ts(K("UI", c, 8, 16), K("UI", c, 0, 8), 3, A.bitwise_and, ["UIa" + n], ["UIb" + n])
-        equal(7)
-        equal(8)
-        ts(X("U3", c)[:], K("UI", c, 8, 16), 256.0, A.mult, ["UIb" + n], ["U3" + n])
-        for d in range(9, 16):
-            equal(d)
-        copy(X("TT", c)[:, :, 0, :], es[:], ["ES" + n], ["TTa" + n])
-        tt(hi[:], wi[:], Qb[:, 0], A.add, ["WI" + n], ["HI" + n], ["Q" + n])
-        ts(hi[:], hi[:], 4095, A.bitwise_and, ["HI" + n], ["HI" + n])
-        ts(X("HF", c)[:], hi[:], -2048.0, A.add, ["HI" + n], ["HF" + n])
-        op("P", ["HF" + n, "ID"], [], ["L" + n], lambda: p.matmul(Lb[:, 0:128], X("HF", c)[:], T.ID[:], True, True))
-        ts(X("H8", c)[:], hi[:], 8, A.arith_shift_right, ["HI" + n], ["H8" + n])
-        ts(X("OFX", c)[:], Lb[:, 0:128], 2048.0, A.add, [], ["OFX" + n], ["L" + n])
-        tt(K("VK", c), X("H8", c)[:], C("KC16"), A.add, ["H8" + n, "KC16"], ["VK" + n])
-
-    def bins(c):
-        n = str(c)
-        op("P", ["XG" + n, "WB"], [], ["L" + n], lambda: [
-            p.matmul(X("L", c)[:, 128 + k:256:16], fan("XG", c, k, 16), T.WB[:], True, True) for k in range(16)])
-
-    def survivors(t, c):
-        n = str(c)
-        Lb, LB = X("L", c), ["L" + n]
-        bi, ind = X("BI", c), X("IN", c)
-        copy(bi[:], Lb[:, 128:256], [], ["BI" + n], LB)
-        ts(bi[:], bi[:], 3, A.bitwise_and, ["BI" + n], ["BI" + n])
-        ink = ["IN%d_%d" % (c, b) for b in range(4)]
-        for b in range(4):
-            ts(ind[:, 128 * b:128 * b + 128], bi[:], b, A.is_equal, ["BI" + n], [ink[b]], (), 4.0, A.mult)
-        scan(X("CT", c)[:], T.RM[:], ind[:], 0.0, A.mult, A.add, ["RM"] + ink, ["CT" + n])
-        tt(K("KI", c), X("CT", c)[:, 15::16], T.KCC[:], A.add, ["CT" + n, "KCC"], ["KI" + n])
-        ts(K("KI", c), K("KI", c), 127, A.bitwise_and, ["KI" + n], ["KI" + n])
-        tt(K("KJ", c, 0, 16), K("KI", c, 0, 16), K("KI", c, 16, 32), A.min, ["KI" + n], ["KJ" + n])
-        tt(K("KJ", c, 16, 24), K("KJ", c, 0, 8), K("KJ", c, 8, 16), A.min, ["KJ" + n], ["KK" + n])
-        ts(K("BN", c, 0, 8), K("KJ", c, 16, 24), 3, A.bitwise_and, ["KK" + n], ["BNa" + n])
-        ts(K("BN", c, 8, 16), K("KJ", c, 16, 24), 2, A.arith_shift_right, ["KK" + n], ["BNb" + n])
-        copy(X("KB", c)[:, ::16], K("BN", c), ["BNa" + n, "BNb" + n], ["KB" + n])
-        scan(X("BB", c)[:], T.RM[:, 0:256], X("KB", c)[:], 0.0, A.mult, A.add, ["RM", "KB" + n], ["BB" + n])
-        tt(K("SV", c), bi[:], X("BB", c)[:, 0:128], A.is_equal, ["BI" + n, "BB" + n], ["SV" + n])
-        op("P", ["SV" + n, "ID"], [], LB, lambda: p.matmul(Lb[:, 0:128], K("SV", c), T.ID[:], True, True))
-        scan(K("PR", c), T.RM[:, 0:128], K("SV", c), 0.0, A.mult, A.add, ["RM", "SV" + n], ["PR" + n])
-        ts(K("AL", c), Lb[:, 0:128], -2.0, A.add, [], ["AL" + n], LB)
-
-    def spread(c, ms):
-        n = str(c)
-        bks = ["BK%d" % k for k in range(16)]
-        for m in ms:
-            D, db = T["D%d" % (m & 1)], "D%d" % (m & 1)
-            op("P", ["AL" + n] + bks, [], [db], lambda: [
-                p.matmul(D[:, 128 * j:128 * j + 128], T.BK[:, 4 * m + j], K("AL", c), True, True) for j in range(4)])
-            op("S", [], ["DS%d_%d" % (c, m)], [db], lambda: [
-                s.activation(fan("DS", c, 4 * m + j, 16), D[:, 128 * j:128 * j + 128], AF.Copy) for j in range(4)])
-
-    def ranks(c):
-        n = str(c)
-        Lb, LB, bb = X("L", c), ["L" + n], X("BB", c)
-        op("P", ["PR" + n, "BB" + n, "ID", "NI", "I2", "KM7", "KM2"], [], LB, lambda: [
-            p.matmul(Lb[:, 384:512], T.ID[:], bb[:, 128:256], True, False),
-            p.matmul(Lb[:, 384:512], T.ID[:], C("KM7"), False, False),
-            p.matmul(Lb[:, 384:512], C("NI"), K("PR", c), False, True),
-            p.matmul(Lb[:, 256:384], C("NI"), bb[:, 128:256], True, False),
-            p.matmul(Lb[:, 256:384], T.ID[:], C("KM2"), False, False),
-            p.matmul(Lb[:, 256:384], C("I2"), K("PR", c), False, True)])
-
-    def places(t, c):
-        n = str(c)
-        Lb, LB = X("L", c), ["L" + n]
-        bb, TTb = X("BB", c), X("TT", c)
-        tt(K("SVL", c), K("SV", c), K("VK", c), A.mult, ["SV" + n, "VK" + n], ["SVL" + n])
-        if t < LEVELS - 1:
-            ts(X("O1", c)[:], bb[:, 128:256], 0.0, A.is_equal, ["BB" + n], ["O1" + n])
-        tt(K("TP", c), K("SV", c), Lb[:, 256:384], A.mult, ["SV" + n], ["TP" + n], LB)
-        scan(K("VM", c), T.RM[:, 0:128], K("SVL", c), 0.0, A.mult, A.max, ["RM", "SVL" + n], ["VM" + n])
-        tt(TTb[:, :, 1, :], K("TP", c), Lb[:, 384:512], A.add, ["TP" + n], ["TTb" + n], LB)
-        tt(X("VT", c)[:], K("VM", c, 15, 128, 16), X("U3", c)[:], A.add, ["VM" + n, "U3" + n], ["VT" + n])
-        tt(TTb[:, :, 2, :], TTb[:, :, 1, :], TTb[:, :, 1, :], A.mult, ["TTb" + n], ["TTc" + n])
-
-    def turn(c):
-        n = str(c)
-        o = 128 + 64 * c
-        op("P", ["VT" + n, "LS"], [], ["L0"], lambda: [
-            p.matmul(T.L0[:, o + 8 * b:o + 8 * b + 8], T.LS[:, b], X("VT", c)[:], True, True) for b in range(8)])
-
-    def lists():
-        r = T.RL
-        tt(T.LM[:], T.DG[:], T.L0[:, 128:256], A.mult, ["DG"], ["LM"], ["L0"])
-        scan(T.LV[:], T.RM8[:], T.LM[:], 0.0, A.mult, A.add, ["RM8", "LM"], ["LV"])
-        copy(T.VI[:], T.LV[:, 7::8], ["LV"], ["VI"])
-        ts(r[:, 0:16], T.VI[:], 15, A.bitwise_and, ["VI"], ["Ra"])
-        ts(r[:, 16:32], T.VI[:], 8, A.arith_shift_right, ["VI"], ["Rb"])
-        ts(r[:, 32:48], T.VI[:], 4, A.arith_shift_right, ["VI"], ["Rc"], (), 15, A.bitwise_and)
-        rr = ["Ra", "Rb", "Rc"]
-        tt(r[:], r[:], T.MUL[:], A.mult, rr + ["MULa", "MULb", "MULc"], rr)
-        tt(r[:], r[:], T.AD[:], A.add, rr + ["ADa", "ADb", "ADc"], rr)
-        copy(T.LST[:], r[:], rr, ["LST"])
-
-    def maximum(c, x):
-        n = str(c)
-        src = ["XG" + n] if x == "X" else ["YG" + n + "a", "YG" + n + "b"]
-        scan(fan(x + "S", c), fan(x + "G", c), fan("DS", c), -1024.0, A.max, A.add,
-             src + ["DS%d_%d" % (c, m) for m in range(4)], [x + "S" + n])
-
-    def leave(t, c):
-        n = str(c)
-        xs, ys = fan("XS", c, 15, 16), fan("YS", c, 15, 16)
-        if t == LEVELS - 1:
-            ts(T.OS[:, :, c, :], ys, 1024.0, A.add, ["YS" + n], ["OS" + n])
-            ts(T.OZ[:, :, c, :], xs, 1024.0, A.add, ["XS" + n], ["OZ" + n])
-            return
-        key = "%d%d" % (t, c)
-        sz, rz = T["SZ" + key], T["RZ" + key]
-        ts(sz[:, :, 0:16], ys, 1024.0, A.add, ["YS" + n], ["SZa" + key])
-        ts(sz[:, :, 16:32], xs, 1024.0, A.add, ["XS" + n], ["SZb" + key])
-        sync("G", ["SZa" + key, "SZb" + key], [], [])
-        for call in calls_of(core, cores, topo):
-            g.remote_dma_fused([RemoteDMATransfer(
-                src=sz[:, cores.index(d), :], dst=rz[:, rank, :],
-                dst_ids=[DstId(rid=topo.addr(d, core)[0], pnc=topo.addr(d, core)[1])],
-                dma_engine_mask=sum(1 << e for e in en), remote_sem=T.sem["arr" + key]) for d, en in call],
-                local_sem=T.sem["snt" + key])
-        copy(rz[:, rank, :], sz[:, rank, :], ["SZa" + key, "SZb" + key], ["RZ" + key + "o"])
-        total = sum(len(en) for o in cores if o != core for call in calls_of(o, cores, topo) for d, en in call if d == core)
-        wr["RZ" + key] = ("arr" + key, total, {})
-
-    def features(c):
-        n = str(c)
-        op("P", ["TTa" + n, "TTb" + n, "TTc" + n, "ID3"], [], ["E" + n], lambda: [
-            p.matmul(X("E", c)[0:96, j], X("TT", c)[:, :, :, j::4], T.ID3[:], True, True) for j in range(4)])
-        op("S", [], ["TL" + n], ["E" + n], lambda: s.activation(X("TL", c)[0:96], X("E", c)[0:96], AF.Copy))
-
-    def pick(c, j):
-        n = str(c)
-        b, key = (X("E", c), "E" + n) if j & 1 else (X("Q", c), "Q" + n)
-        op("P", ["TL" + n, "FQ"], [], [key], lambda: [
-            p.matmul(b[:, i], T.FQ[0:96, i], X("TL", c)[0:96, j], True, True) for i in range(4)])
-        op("S", ["q6"], ["FR%d_%d" % (c, j)], [key],
-           lambda: s.activation(X("FR", c)[:, 4 * j:4 * j + 4], b[:], AF.Relu, bias=T.QC[:, 6:7]))
-
-    def total(c, j):
-        op("P", ["FR%d_%d" % (c, j), "ID"], [], ["E0"], lambda: [
-            p.matmul(T.E0[:, c], T.ID[:], X("FR", c)[:, i], i == 0, i == 15) for i in range(4 * j, 4 * j + 4)])
-
-    def cwrite():
-        copy(T.FC[:], T.E0[:, 0:2], [], ["FC"], ["E0"])
-        op("V", ["FC", "LST"], ["CW"], [], lambda: v.tensor_copy(T.CW[:, 0:1024].indirect(T.LST[:, 16:32]), T.FC[:]))
-
-    def xnew():
-        ts(T.NZ[:], T.XS[:, 15::16], 1024.0, A.add, ["XS0", "XS1"], ["NZ"])
-        op("V", ["XG0", "XG1", "LST", "NZ"], ["XQ"], [], lambda: v.tensor_tensor(
-            T.XQ[:], T.XG[:, 0:4096].indirect(T.LST[:, 32:48]), T.NZ[:], A.add))
-        ts(T.XR[:], T.XQ[:], 1, A.arith_shift_right, ["XQ"], ["XR"])
-
-    def xwrite():
-        op("V", ["XR", "LST"], ["XW"], [], lambda: v.tensor_copy(T.XW[:, 0:4096].indirect(T.LST[:, 0:16]), T.XR[:]))
+    def spread_constants(e, ks):
+        for k in ks:
+            if e == "V":
+                ts(T.BK[:, k], T.BO[:], T.RA[:, k:k + 1], A.mult, ["BO", "RA"], ["BK%d" % k])
+            else:
+                act(T.BK[:, k], T.BO[:], AF.Copy, ["BO", "RA"], ["BK%d" % k], scale=T.RA[:, k:k + 1])
 
     def weights(a, b):
         iota(T.DI[:, a:b], [[1, b - a], [0, 128]], a + 1, 0, ["DI%d" % a])
         sel(T.DI[:, a:b], T.DI[:, a:b], [[0, b - a], [-1, 128]], A.is_equal, 0.0, 0, 1, ["DI%d" % a], ["DI%d" % a])
 
+    def landed(t, c):
+        if t == 0:
+            return T.Z0, ["Z0%d" % c]
+        return T["RZ%d" % (t - 1)], ["RZ%d%d" % (t - 1, c), "RZ%d%do" % (t - 1, c)]
+
+    def seats(t, c):
+        if t == 0:
+            copy(H("OFS", c), T.S3[:, :, c, :], ["S3"], ["OFS%d" % c])
+        else:
+            z, keys = landed(t, c)
+            lin("V", H("OFS", c), z[:, 256 * c:256 * c + 256:2], 4.0, -1.0, keys, ["OFS%d" % c])
+
+    def gather(e, out, win, off, c, h, scale, bias, R, u0, u1):
+        a = 128 * c + 64 * h
+        lin(e, T[out][:, 16 * a + 256 * u0:16 * a + 256 * u1], win.indirect(T[off][:, a + 16 * u0:a + 16 * u1]), scale, bias,
+            R + ["%s%d" % (off, c)], ["%s%d%d%d" % (out, c, h, u) for u in range(u0, u1)])
+
+    def got(name, c, h):
+        return ["%s%d%d%d" % (name, c, h, u) for u in range(4)]
+
+    def cg(e, c, h, u0=0, u1=4):
+        gather(e, "CG", T.CW[:, 0:1024], "OFS", c, h, 1.0, 1024.0, ["CW"], u0, u1)
+
+    def mg(e, c, h, u0=0, u1=4):
+        gather(e, "YG", T.CM[:, 0:1024], "OFM", c, h, 1.0 / 4096, 256.25 - 511.5 / 4096, ["CM0", "CM1"], u0, u1)
+
+    def xg(e, c, h, u0=0, u1=4):
+        gather(e, "XG", T.XW[:, 0:4096], "OFX", c, h, 0.5, 0.0, ["XW"], u0, u1)
+
+    def fan(name, c, h, k):
+        a = 2048 * c + 1024 * h
+        return T[name][:, a + k:a + 1024:16]
+
+    def usum(t, c):
+        z, keys = landed(t, c)
+        zz = z[:, 256 * c + 1:256 * c + 256:2]
+        mm(T["E%d" % c][:, 1], [(M("BO2"), zz), (M("ON"), M("KU"))], keys + ["BO2", "ON", "KU"], ["E%d" % c])
+        mm(T["Q%d" % c][:, 0], [(M("BOM"), zz), (M("ON"), M("KQ")), (M("ID"), M("AB"))],
+           keys + ["BOM", "ON", "KQ", "ID", "AB"], ["Q%d" % c], True, False)
+
+    def members(t, c, h):
+        mm(T["E%d" % c][:, 0, 64 * h:64 * h + 64], [(T.PS[:, (k + t) & 15, 15 - k:143 - k], fan("CG", c, h, k)) for k in range(16)],
+           got("CG", c, h) + ["PS%d" % r for r in range(16)], ["E%d" % c])
+
+    def elist(e, c):
+        lin(e, H("ES", c), T["E%d" % c][:, 0], 1.0, 0.0, [], ["ES%d" % c], ["E%d" % c])
+
+    def diffs(c, j):
+        for i in range(4):
+            mm(T["D%d" % j][:, 128 * i:128 * i + 128], [(T.WD[:, 4 * j + i], H("ES", c))], ["ES%d" % c, "WD%d" % (4 * j + i)], ["D%d" % j])
+
+    def equal(c, j):
+        ts(T.EQ[:, c, 4 * j:4 * j + 4], T["D%d" % j][:], 0.0, A.is_equal, [], ["EQ%d%d" % (c, j)], ["D%d" % j])
+        mm(T["Q%d" % c][:, 0], [(T.RD[:, 4 * j + i], T.EQ[:, c, 4 * j + i]) for i in range(4)],
+           ["EQ%d%d" % (c, j)] + ["RD%d" % (4 * j + i) for i in range(4)], ["Q%d" % c], False, j == 1)
+
+    def hashes(t, c, e="V"):
+        n = str(c)
+        elist(e, c)
+        diffs(c, 0)
+        diffs(c, 1)
+        tt(H("XX", c), H("ES", c), T["E" + n][:, 1], A.mult, ["ES" + n], ["XX" + n], ["E" + n])
+        equal(c, 0)
+        equal(c, 1)
+        lin("V", H("OFM", c), H("ES", c), 1.0, -1024.0, ["ES" + n], ["OFM" + n])
+        tt(H("HI", c), H("XX", c), T["Q" + n][:, 0], A.add, ["XX" + n], ["HI" + n], ["Q" + n])
+        ts(H("HI", c), H("HI", c), 5, A.arith_shift_right, ["HI" + n], ["HI" + n], (), 4095, A.bitwise_and)
+        copy(H("OFX", c), H("HI", c), ["HI" + n], ["OFX" + n])
+
+    def high(c):
+        lin("V", H("HH", c), H("OFX", c), -1.0 / 65536, -6.0 + 127.5 / 65536, ["OFX%d" % c], ["HH%d" % c])
+
+    def bins(c, h):
+        mm(T["E%d" % c][:, 2, 64 * h:64 * h + 64], [(slide(1, k), fan("XG", c, h, k)) for k in range(16)],
+           got("XG", c, h) + ["ZS1"], ["E%d" % c])
+
+    def floors(e, c):
+        n = str(c)
+        lin(e, H("QS", c), T["E" + n][:, 2], -1.0, 0.0, [], ["QS" + n], ["E" + n])
+        for i in range(4):
+            lin("V", T.RR[:, i, 128 * c:128 * c + 128], H("QS", c), -1.0, 1535.625 + i / 4, ["QS" + n], ["RR%d%d" % (c, i)])
+        mm(T["Q" + n][:, 1], [(T.W1[:, i], T.RR[:, i, 128 * c:128 * c + 128]) for i in range(4)],
+           ["W1"] + ["RR%d%d" % (c, i) for i in range(4)], ["Q" + n])
+
+    def duels(c):
+        n = str(c)
+        if TE[0] == "S":
+            act(H("T1", c), T["Q" + n][:, 1], AF.Sign, ["b1"], ["T1" + n], ["Q" + n], bias=q("b1"))
+        else:
+            ts(H("T1", c), T["Q" + n][:, 1], q("nb1"), A.is_gt, ["nb1"], ["T1" + n], ["Q" + n], -0.5, A.add)
+        mm(T["E" + n][:, 3], [(M("W2"), H("T1", c))], ["W2", "T1" + n], ["E" + n])
+
+    def winner(c):
+        n = str(c)
+        th = 3.0 if TE[0] == "S" else 1.5
+        if TE[1] == "S":
+            act(H("T2", c), T["E" + n][:, 3], AF.Sign, [], ["T2" + n], ["E" + n], bias=-th)
+        else:
+            ts(H("T2", c), T["E" + n][:, 3], th, A.is_gt, [], ["T2" + n], ["E" + n], -0.5, A.add)
+        mm(T["Q" + n][:, 2], [(M("ID"), H("QS", c)), (M("ID"), T.RR[:, 0, 128 * c:128 * c + 128]), (M("W3"), H("T2", c))],
+           ["ID", "QS" + n, "RR%d0" % c, "W3", "T2" + n], ["Q" + n])
+
+    def survivors(c):
+        n = str(c)
+        ts(H("AL", c), T["Q" + n][:, 2], 1535.25, A.is_equal, [], ["AL" + n], ["Q" + n], -2.0, A.add)
+
+    def spread(c, h, e="S"):
+        a = 128 * c + 64 * h
+        for m in (0, 1):
+            D, db = T["D%d" % m], "D%d" % m
+            op("P", ["AL%d" % c] + ["BK%d" % k for k in range(16)], [], [db], lambda: [
+                p.matmul(D[:, j::8], T.BK[:, 2 * j + m], T.AL[:, a:a + 64], True, True) for j in range(8)])
+            lin(e, T.DS[:, 16 * a + m:16 * a + 1024:2], D[:], 1.0, 0.0, [], ["DS%d%d%d" % (c, h, m)], [db])
+
+    def maximum(c, h, x):
+        a = 128 * c + 64 * h
+        scan(T[x + "S"][:, 16 * a:16 * a + 1024], T[x + "G"][:, 16 * a:16 * a + 1024], T.DS[:, 16 * a:16 * a + 1024], -1024.0, A.max, A.add,
+             got(x + "G", c, h) + ["DS%d%d0" % (c, h), "DS%d%d1" % (c, h)], ["%sS%d%d" % (x, c, h)])
+
+    def ends(x, c):
+        return T[x + "S"][:, 2048 * c + 15:2048 * c + 2048:16], ["%sS%d0" % (x, c), "%sS%d1" % (x, c)]
+
+    def halved(t, c):
+        src, keys = ends("X", c)
+        lin("V", T["SZ%d" % t][:, 256 * c + 1:256 * c + 256:2], src, 1.0, 255.75, keys, ["SZX%d%d" % (t, c)])
+
+    def leave(t, c):
+        key = "%d%d" % (t, c)
+        sz, rz = T["SZ%d" % t], T["RZ%d" % t]
+        src, keys = ends("Y", c)
+        blk = lambda x, b: x[:, 256 * c + 32 * b:256 * c + 32 * b + 32]
+        copy(sz[:, 256 * c:256 * c + 256:2], src, keys, ["SZY" + key])
+        halved(t, c)
+        sync("G", ["SZX" + key, "SZY" + key], [], [])
+        for call in calls_of(core, cores, topo):
+            g.remote_dma_fused([RemoteDMATransfer(
+                src=blk(sz, cores.index(d)), dst=blk(rz, rank),
+                dst_ids=[DstId(rid=topo.addr(d, core)[0], pnc=topo.addr(d, core)[1])],
+                dma_engine_mask=sum(1 << e for e in en), remote_sem=T.sem["arr" + key]) for d, en in call],
+                local_sem=T.sem["snt" + key])
+        copy(blk(rz, rank), blk(sz, rank), ["SZX" + key, "SZY" + key], ["RZ" + key + "o"])
+        total = sum(len(en) for o in cores if o != core for call in calls_of(o, cores, topo) for d, en in call if d == core)
+        wr["RZ" + key] = ("arr" + key, total, {})
+
+    def result(x, c):
+        src, keys = ends(x, c)
+        if x == "Y":
+            lin("V", T.OS[:, :, c, :], src, 4.0, -1.0, keys, ["OS%d" % c])
+        else:
+            lin("V", T.OZ[:, :, c, :], src, 2.0, 512.0, keys, ["OZ%d" % c])
+
+    def places(c):
+        for j, w in enumerate(("TA", "TU")):
+            mm(T["E%d" % c][:, j], [(M(w), H("AL", c))], [w, "AL%d" % c], ["E%d" % c])
+
+    def powers(c):
+        pw = [T.PW[:, j, 128 * c:128 * c + 128] for j in (0, 1)]
+        for j, b in enumerate(("bA", "bB")):
+            act(pw[j], T["E%d" % c][:, j], AF.Exp, [b], ["PW%d%d" % (c, j)], ["E%d" % c], bias=q(b), scale=LN2)
+        mm(T["Q%d" % c][:, 0], [(M("ID"), pw[0]), (M("ID"), pw[1])], ["ID", "PW%d0" % c, "PW%d1" % c], ["Q%d" % c])
+
+    def keyed(c):
+        tt(H("VV", c), H("ES", c), T["Q%d" % c][:, 0], A.mult, ["ES%d" % c], ["VV%d" % c], ["Q%d" % c])
+
+    def cut(c, a=0, b=16):
+        p0 = P0[c]
+        order = sorted(range(16), key=lambda r: (r + 1) / p0 if r < p0 else (16 - r) / (16.01 - p0))
+        for i in range(a, b):
+            r = order[i]
+            cl, key = T.CL[:, r, 128 * c:128 * c + 128], "CL%d_%d" % (c, r)
+            if r >= p0:
+                act(cl, H("VV", c), AF.Relu, ["VV%d" % c], [key], bias=-2.0 ** (r - 1))
+            else:
+                ts(cl, H("VV", c), 2.0 ** (r - 1), A.max, ["VV%d" % c], [key], (), 2.0 ** r, A.min)
+            mm(T["E%d" % c][:, 2], [(slide(2 if r > p0 else 0, r), cl)], [key, "ZS0", "ZS2"], ["E%d" % c], i == 0, i == 15)
+
+    def column(e, c):
+        b = "bF%d" % c
+        lin(e, H("FC", c), T["E%d" % c][:, 2], q("sF"), q(b), ["sF", b], ["FC%d" % c], ["E%d" % c])
+
+    def cwrite(cs):
+        a, b = cs[0], cs[-1] + 1
+        op("V", ["FC%d" % c for c in cs] + ["LC"], ["CW"], [], lambda: v.tensor_copy(
+            T.CW[:, 0:1024].indirect(T.LC[:, 8 * a:8 * b]), T.FC[:, 128 * a:128 * b]))
+
+    def uturn(t):
+        z, k0 = landed(t, 0)
+        mm(T.X2[:, 256:272], [(slide(0, a), z[:, 2 * a + 1::32]) for a in range(16)], k0 + landed(t, 1)[1] + ["ZS0"], ["X2"])
+
+    def clist():
+        r = T.LI[:, 0:16]
+        lin("V", r, T.X2[:, 256:272], 2.0, 8.0, [], ["LIa"], ["X2"])
+        ts(r, r, 3, A.bitwise_and, ["LIa"], ["LIa"])
+        tt(r, r, T.AD[:, 16:32], A.add, ["LIa", "ADb"], ["LIa"])
+        copy(T.LC[:], r, ["LIa"], ["LC"])
+
+    def first():
+        mm(T.D1[:, 0:256], [(M("ID"), T.HH[:]), (M("TB"), T.AL[:])], ["ID", "TB", "HH0", "HH1", "AL0", "AL1"], ["D1"])
+        act(T.VL[:], T.D1[:, 0:256], AF.Relu, ["bV"], ["VL"], ["D1"], bias=q("bV"), scale=-65536.0)
+        mm(T.X2[:, 272:288], [(slide(0, a), T.VL[:, a::16]) for a in range(16)], ["VL", "ZS0"], ["X2"])
+
+    def alone():
+        mm(T.D0[:, 0:256], [(T.BO[:], T.AL[:])], ["BO", "AL0", "AL1"], ["D0"])
+        act(T.JK[:], T.D0[:, 0:256], AF.Sign, [], ["JK", "acc"], ["D0"], bias=-30.5, scale=-1.0, acc=q("acc"))
+
+    def carry():
+        ts(M("AB"), M("ON"), q("acc"), A.mult, ["ON", "acc"], ["AB"], (), 16.0, A.mult)
+
+    def xlists():
+        tt(T.LI[:, 16:32], T.AD[:, 0:16], T.X2[:, 272:288], A.add, ["ADa"], ["LIb"], ["X2"])
+        ts(T.LI[:, 32:48], T.LI[:, 16:32], 4095, A.bitwise_and, ["LIb"], ["LIc"])
+        ts(T.LI[:, 48:64], T.LI[:, 16:32], 12, A.arith_shift_right, ["LIb"], ["LId"])
+        copy(T.LX[:], T.LI[:, 32:64], ["LIc", "LId"], ["LX"])
+
+    def xnew(t):
+        keys = [k for c in (0, 1) for h in (0, 1) for k in got("XG", c, h)] + ["SZX%d0" % t, "SZX%d1" % t]
+        op("V", keys + ["LX"], ["XQ"], [], lambda: v.tensor_tensor(
+            T.XQ[:], T.XG[:, 0:4096].indirect(T.LX[:, 16:32]), T["SZ%d" % t][:, 1::2], A.add))
+
+    def xwrite():
+        op("V", ["XQ", "LX"], ["XW"], [], lambda: v.tensor_copy(T.XW[:, 0:4096].indirect(T.LX[:, 0:16]), T.XQ[:]))
+
+    first_constants()
     for t in range(LEVELS):
         last = t == LEVELS - 1
         seats(t, 0)
         if t == 0:
             seats(t, 1)
-            ts(T.CW[:], T.CM[:], 1023, A.bitwise_and, ["CM"], ["CW"])
-        cgather("S", 0, 0, 64)
-        cgather("V", 0, 64, 128)
-        zrow(t, 0)
+            ts(T.CW[:, 0:512], T.CM[:, 0:512], 1023, A.bitwise_and, ["CM0"], ["CW"])
+            ts(T.CW[:, 512:1024], T.CM[:, 512:1024], 1023, A.bitwise_and, ["CM1"], ["CW"])
+        cg("S", 0, 0)
+        cg("V", 0, 1)
         if t > 0:
+            carry()
             seats(t, 1)
-        cgather("S", 1, 0, 64)
-        cgather("S", 1, 64, 128)
-        zrow(t, 1)
+        cg("S", 1, 0)
+        cg("S", 1, 1)
+        members(t, 0, 0)
+        usum(t, 0)
+        members(t, 0, 1)
         if t == 0:
-            ts(T.MW[:], T.CM[:], 10, A.arith_shift_right, ["CM"], ["MW"])
+            second_constants()
+            weights(0, 8)
+            weights(8, 16)
         else:
-            xnew()
-        members(t, 0)
+            xlists()
+            xnew(t - 1)
         hashes(t, 0)
-        mgather("S", 0, 0, 64)
+        mg("S", 0, 0)
+        usum(t, 1)
+        members(t, 1, 0)
+        members(t, 1, 1)
         if t == 0:
-            late_constants()
+            third_constants()
         else:
             xwrite()
-        members(t, 1)
-        xgather("S", 0)
+        xg("S", 0, 0)
+        xg("S", 0, 1)
         hashes(t, 1)
-        xgather("S", 1)
-        mgather("S", 1, 0, 64)
-        bins(0)
-        bins(1)
-        survivors(t, 0)
-        ranks(0)
-        spread(0, (0, 1, 2, 3))
-        places(t, 0)
-        features(0)
-        for j in range(4):
-            pick(0, j)
-        mgather("V", 0, 64, 128)
-        mgather("S", 1, 64, 128)
-        survivors(t, 1)
-        ranks(1)
-        spread(1, (0, 1))
-        places(t, 1)
-        features(1)
-        turn(0)
-        turn(1)
-        spread(1, (2, 3))
-        for j in range(4):
-            total(0, j)
-        pick(1, 0)
-        pick(1, 1)
-        total(1, 0)
-        pick(1, 2)
-        total(1, 1)
-        pick(1, 3)
-        total(1, 2)
-        total(1, 3)
-        maximum(0, "X")
-        maximum(0, "Y")
-        leave(t, 0)
-        maximum(1, "X")
-        maximum(1, "Y")
-        leave(t, 1)
+        bins(0, 0)
+        uturn(t)
+        xg("V", 1, 0)
+        xg("S", 1, 1)
+        bins(0, 1)
+        mg("S", 0, 1)
+        if t == 0:
+            spread_constants("V", range(16))
+        floors("V", 0)
+        bins(1, 0)
+        high(0)
+        high(1)
+        clist()
+        duels(0)
+        bins(1, 1)
+        mg("V", 1, 0, 0, 1)
+        winner(0)
+        floors("V", 1)
+        survivors(0)
+        spread(0, 0)
+        places(0)
+        duels(1)
+        mg("V", 1, 0, 1, 2)
+        winner(1)
+        spread(0, 1)
+        mg("V", 1, 0, 2, 3)
+        survivors(1)
+        powers(0)
         if not last:
-            weights(32 * t, 32 * t + 16)
-            weights(32 * t + 16, 32 * t + 32)
-        lists()
-        if last:
-            xnew()
-            xwrite()
-        cwrite()
-    dma("Y", "os", T.ys[:], T.OS[:], ["OS0", "OS1"], [])
+            maximum(0, 0, "Y")
+            maximum(0, 0, "X")
+            mg("S", 1, 1)
+            maximum(0, 1, "Y")
+            maximum(0, 1, "X")
+            leave(t, 0)
+            spread(1, 0)
+            mg("V", 1, 0, 3, 4)
+            places(1)
+            keyed(0)
+            spread(1, 1)
+            cut(0)
+            maximum(1, 0, "Y")
+            maximum(1, 0, "X")
+            powers(1)
+            column("S", 0)
+            maximum(1, 1, "Y")
+            maximum(1, 1, "X")
+            leave(t, 1)
+            for a in ((16, 24, 32) if t == 0 else (40, 48, 56)):
+                weights(a, a + 8)
+            keyed(1)
+            cut(1)
+            column("S", 1)
+            first()
+            alone()
+            cwrite((0, 1))
+    first()
+    places(1)
+    spread(1, 0)
+    maximum(0, 0, "X")
+    maximum(0, 1, "X")
+    spread(1, 1)
+    halved(2, 0)
+    xlists()
+    keyed(0)
+    cut(0)
+    powers(1)
+    maximum(1, 0, "X")
+    maximum(1, 1, "X")
+    mg("S", 1, 1)
+    halved(2, 1)
+    xnew(2)
+    xwrite()
+    column("S", 0)
+    keyed(1)
+    cut(1)
+    dis = ["DI%d" % a for a in range(0, 64, 8)]
+    column("S", 1)
+    mm(T.Q0[:, 0, 0:64], [(T.DI[:, m], T.XW[:, 64 * m:64 * m + 64]) for m in range(64)], ["XW"] + dis, ["Q0"])
+    mg("V", 1, 0, 3, 4)
+    cwrite((0, 1))
+    act(T.CF[:], T.CW[:], AF.Copy, ["CW"], ["CF"])
+    mm(T.Q1[:, 0, 0:64], [(T.DI[:, m], T.CF[:, 64 * m:64 * m + 64]) for m in range(16)], ["CF"] + dis, ["Q1"])
+    for c in (0, 1):
+        result("X", c)
     dma("Y", "oz", T.yz[:], T.OZ[:], ["OZ0", "OZ1"], [])
-    dis = ["DI0", "DI16", "DI32", "DI48"]
-    op("P", ["XW"] + dis, [], ["L0"], lambda: [
-        p.matmul(T.L0[:, 0:64], T.DI[:, m], T.XW[:, 64 * m:64 * m + 64], m == 0, m == 63) for m in range(64)])
-    copy(T.CF[:], T.CW[:], ["CW"], ["CF"])
-    op("P", ["CF"] + dis, [], ["L1"], lambda: [
-        p.matmul(T.L1[:, 0:64], T.DI[:, m], T.CF[:, 64 * m:64 * m + 64], m == 0, m == 15) for m in range(16)])
-    copy(T.OX[:], T.L0[:, 0:64], [], ["OX"], ["L0"])
-    dma("Y", "ox", T.yx[:], T.OX[:], ["OX"], [])
-    copy(T.OC[:], T.L1[:, 0:64], [], ["OC"], ["L1"])
-    dma("Y", "oc", T.yc[:], T.OC[:], ["OC"], [])
+    for c in (0, 1):
+        maximum(c, 0, "Y")
+        maximum(c, 1, "Y")
+        result("Y", c)
+    dma("Y", "os", T.ys[:], T.OS[:], ["OS0", "OS1"], [])
+    act(T.OX[:], T.Q0[:, 0, 0:64], AF.Copy, [], ["OX"], ["Q0"])
+    dma("S", "ox", T.yx[:], T.OX[:], ["OX"], [])
+    act(T.OC[:], T.Q1[:, 0, 0:64], AF.Copy, [], ["OC"], ["Q1"])
+    dma("S", "oc", T.yc[:], T.OC[:], ["OC"], [])
     for sem in sorted(cnt):
         g.wait_ge(T.sem[sem], cnt[sem])
     for t in range(LEVELS - 1):

@@ -5,13 +5,12 @@ from concourse.mybir import dt, AluOpType, AxisListType, ActivationFunctionType
 A = AluOpType
 AF = ActivationFunctionType
 LEVELS = 3
-TE = ("V", "V")
 P0 = (16, 11)
 LN2 = math.log(2.0)
 
 _B, _H, _F, _I, _U = "bfloat16", "float16", "float32", "int32", "uint16"
-MATS = ("ON", "ID", "BO2", "BOM", "KU", "KQ", "AB", "CJ", "TA", "TU", "TB", "W2", "W3", "CA", "TRI")
-COLS = ("P", "P1", "p", "g16", "cv", "sg", "a", "b", "nd", "dw", "dg", "b1", "bA", "bB", "bV", "sF", "bF0", "bF1", "nb1", "acc", "t0", "t1", "a32")
+MATS = ("ON", "ID", "BO2", "BOM", "KU", "KQ", "AB", "TA", "TU", "TB", "W2", "W3V", "W3S", "CA", "TRI")
+COLS = ("P", "p", "g16", "g1", "cv", "sg", "a", "b", "nd", "dw", "dg", "b1", "nb1", "bA", "bB", "bV", "sF", "bF0", "bF1", "acc", "t0")
 SCRATCH = {
     "XW": ("sbuf", [128, 4096], _B), "CM": ("sbuf", [128, 1024], _I), "CW": ("sbuf", [128, 1024], _I),
     "S3": ("sbuf", [128, 8, 2, 16], _I), "Z3": ("sbuf", [128, 8, 2, 16], _B), "CF": ("sbuf", [128, 1024], _H),
@@ -52,14 +51,9 @@ def calls_of(src, cores, topo):
     off = [c for c in cores if c != src and c not in here]
     off.sort(key=lambda c: (2 if topo.mates(src, c) else 1 if topo.same_plane(src, c) else 0, c))
     eng = topo.engines(src, off[0])
-    half = len(off) - 2
-    w = len(eng) // half
-    first = [(d, eng[w * i:w * i + w]) for i, d in enumerate(off[:half])]
-    w = len(eng) // 2
-    second = [(d, eng[w * i:w * i + w]) for i, d in enumerate(off[half:])]
-    for d in here:
-        second.append((d, [e for e in topo.engines(src, d) if e not in eng]))
-    return [first, second]
+    call = [(d, [e]) for d, e in zip(off, eng)]
+    call += [(d, [e]) for d, e in zip(here, [e for e in topo.engines(src, here[0]) if e not in eng])]
+    return [call]
 
 
 def rank_program(g, core, T, topo):
@@ -175,53 +169,67 @@ def rank_program(g, core, T, topo):
     dma("Y", "dz", T.Z3[:], T.z0[:], [], ["Z3"])
     dma("Y", "dx", T.XW[:], T.x0[:], [], ["XW"])
 
-    def first_constants():
-        fill(M("ON"), 1.0, ["ON"])
+    def k_rows():
         iota(T.QI[:], [[-1, 16]], 0, 1, ["QI"], False)
-        iota(T.QC[:, 0:2], [[1, 2]], 0, 1, ["P", "P1"])
+        iota(q("P"), [[1, 1]], 0, 1, ["P"])
         iota(T.CI[:], [[1, 144]], 1, 0, ["CI"])
-        iota(T.JI[:, 0], [[1, 8]], 1, 1, ["JIa"], False)
-        iota(T.JI[:, 1], [[-1, 8]], -1, 1, ["JIb"], False)
-        iota(M("CJ"), [[1, 128]], 0, 0, ["CJ"])
-        sel(T.BO[:], M("ON"), [[-16, 8], [0, 16]], A.is_ge, 0.0, 0, 1, ["ON"], ["BO"])
-        sel(T.BO[:], T.BO[:], [[16, 8], [0, 16]], A.is_ge, 0.0, 15, -1, ["BO"], ["BO"])
-        sel(M("ID"), M("ON"), [[-1, 128]], A.is_equal, 0.0, 0, 1, ["ON"], ["ID"])
+        fill(M("ON"), 1.0, ["ON"])
         fill(M("KU"), 41.0 / 128, ["KU"])
         fill(M("KQ"), (4096 - 41 * 1024) / 128, ["KQ"])
         fill(M("AB"), -4096.0, ["AB"])
         ts(T.QJ[:], T.QI[:], 15, A.bitwise_and, ["QI"], ["QJ"])
         copy(q("p"), T.QJ[:, 0:1], ["QJ"], ["p"])
-        ts(T.JI[:], T.JI[:], 15, A.bitwise_and, ["JIa", "JIb"], ["JIa", "JIb"])
+        ts(T.PT[:], T.QJ[:], 0, A.is_equal, ["QJ"], ["PT"])
         col("g16", "P", "p", A.subtract)
-        col("cv", "g16", 16.0, A.add)
-        ts(T.JT[:, 0], T.JI[:, 0], q("g16"), A.add, ["JIa", "g16"], ["JTa"])
-        ts(T.JT[:, 1], T.JI[:, 1], q("p"), A.max, ["JIb", "g16", "p"], ["JTb"], (), q("g16"), A.add)
-        ts(T.PT[:], T.QJ[:], 0, A.is_equal, ["QJ", "cv"], ["PT"], (), q("cv"), A.mult)
-        for r in range(16):
-            ts(T.PS[:, r], T.CI[:], T.PT[:, r:r + 1], A.is_equal, ["CI", "PT"], ["PS%d" % r])
-        for d in range(8):
-            ts(T.WD[:, d], M("CJ"), T.JT[:, 0, d:d + 1], A.is_equal, ["CJ", "JTa"], ["WD%d" % d], (), -1.0, A.mult)
-        wd = ["WD%d" % d for d in range(8)]
-        sel(T.WD[:], T.WD[:], [[0, 8], [-1, 128]], A.not_equal, 1.0, 0, 1, wd, wd)
-        scalar_constants()
-        act(M("BO2"), T.BO[:], AF.Copy, ["BO"], ["BO2"], scale=2.0)
-        act(M("BOM"), T.BO[:], AF.Copy, ["BO"], ["BOM"], scale=-2048.0)
-        for c in (0, 1):
-            act(T.Z0[:, 256 * c + 1:256 * c + 256:2], T.Z3[:, :, c, :], AF.Identity, ["Z3"], ["Z0%d" % c], bias=-0.25, scale=0.5)
-
-    def second_constants():
-        for d in range(8):
-            ts(T.RD[:, d], M("CJ"), T.JT[:, 1, d:d + 1], A.is_equal, ["CJ", "JTb"], ["RD%d" % d], (),
-               613.0 * (32 if d < 7 else 16), A.mult)
-        ts(T.RA[:], T.QJ[:], 0, A.is_equal, ["QJ"], ["RA"], (), 256.0, A.mult)
-        ts(T.RB[:], T.QJ[:], 1, A.is_equal, ["QJ"], ["RB"], (), 256.0, A.mult)
         ts(T.QK[:, 0:1], T.QJ[:, 0:1], 1, A.bitwise_and, ["QJ"], ["QK0"])
-        ts(T.QK[:, 1:2], T.QJ[:, 0:1], 2, A.arith_shift_right, ["QJ"], ["QK1"])
-        ts(T.QK[:, 2:3], T.QJ[:, 0:1], 3, A.bitwise_and, ["QJ"], ["QK2"])
-        tt(T.RA[:, 0:15], T.RA[:, 0:15], T.RB[:, 0:15], A.subtract, ["RA", "RB"], ["RA"])
+        col("cv", "g16", 16.0, A.add)
         ts(q("sg"), T.QK[:, 0:1], -1.0, A.mult, ["QK0"], ["sg"], (), 0.5, A.add)
-        copy(q("a"), T.QK[:, 1:2], ["QK1"], ["a"])
-        copy(q("b"), T.QK[:, 2:3], ["QK2"], ["b"])
+        ts(T.ZS[:, 0], T.CI[:], q("cv"), A.is_equal, ["CI", "cv"], ["ZS0"])
+        act(T.QB[:, 0:1], q("p"), AF.Exp, ["p"], ["QB"], bias=11 * LN2, scale=-LN2)
+        act(q("sF"), T.QB[:, 0:1], AF.Copy, ["QB"], ["sF"])
+
+    def k_blocks():
+        iota(T.JI[:, 0], [[1, 8]], 1, 1, ["JIa"], False)
+        iota(T.JI[:, 1], [[-1, 8]], -1, 1, ["JIb"], False)
+        sel(T.BO[:], M("ON"), [[-16, 8], [0, 16]], A.is_ge, 0.0, 0, 1, ["ON"], ["BO"])
+        sel(T.BO[:], T.BO[:], [[16, 8], [0, 16]], A.is_ge, 0.0, 15, -1, ["BO"], ["BO"])
+        sel(M("ID"), M("ON"), [[-1, 128]], A.is_equal, 0.0, 0, 1, ["ON"], ["ID"])
+
+    def k_pick(e, a, b):
+        for r in range(a, b):
+            lin(e, T.PS[:, r], T.ZS[:, 0], T.PT[:, r:r + 1], 0.0, ["ZS0", "PT"], ["PS%d" % r])
+
+    def k_pairs():
+        ts(T.JI[:], T.JI[:], 15, A.bitwise_and, ["JIa", "JIb"], ["JIa", "JIb"])
+        col("g1", "g16", 1.0, A.add)
+        ts(T.JT[:, 0], T.JI[:, 0], q("g1"), A.add, ["JIa", "g1"], ["JTa"])
+        ts(T.JT[:, 1], T.JI[:, 1], q("p"), A.max, ["JIb", "g1", "p"], ["JTb"], (), q("g1"), A.add)
+        for d in range(8):
+            ts(T.WD[:, d], T.CI[:, 0:128], T.JT[:, 0, d:d + 1], A.is_equal, ["CI", "JTa"], ["WD%d" % d], (), -1.0, A.mult)
+        for j in (0, 4):
+            wd = ["WD%d" % d for d in range(j, j + 4)]
+            sel(T.WD[:, j:j + 4], T.WD[:, j:j + 4], [[0, 4], [-1, 128]], A.not_equal, 1.0, 0, 1, wd, wd)
+
+    def k_later():
+        for d in range(8):
+            ts(T.RD[:, d], T.CI[:, 0:128], T.JT[:, 1, d:d + 1], A.is_equal, ["CI", "JTb"], ["RD%d" % d], (),
+               613.0 * (32 if d < 7 else 16), A.mult)
+
+    def k_sums(e):
+        lin(e, M("BO2"), T.BO[:], 2.0, 0.0, ["BO"], ["BO2"])
+        lin(e, M("BOM"), T.BO[:], -2048.0, 0.0, ["BO"], ["BOM"])
+
+    def k_start(e, c):
+        lin(e, T.Z0[:, 256 * c + 1:256 * c + 256:2], T.Z3[:, :, c, :], 0.5, -0.25, ["Z3"], ["Z0%d" % c])
+
+    def k_slides():
+        ts(T.ZS[:, 1], T.ZS[:, 0], q("sg"), A.mult, ["ZS0", "sg"], ["ZS1"])
+        tt(T.ZS[:, 2, 0:143], T.ZS[:, 0, 0:143], T.ZS[:, 0, 1:144], A.subtract, ["ZS0"], ["ZS2"])
+        ts(T.RA[:], T.PT[:], 256.0, A.mult, ["PT"], ["RA"])
+        ts(T.RB[:], T.QJ[:], 1, A.is_equal, ["QJ"], ["RB"], (), 256.0, A.mult)
+        tt(T.RA[:, 0:15], T.RA[:, 0:15], T.RB[:, 0:15], A.subtract, ["RA", "RB"], ["RA"])
+
+    def k_order():
         iota(T.CR[:], [[-1, 8]], 4, 0, ["CR"], False)
         iota(M("CA"), [[0, 8], [1, 4], [0, 4]], 0, 0, ["CA"])
         sel(M("TRI"), T.BO[:], [[1, 128]], A.is_gt, 0.0, 0, -1, ["BO"], ["TRI"])
@@ -232,55 +240,52 @@ def rank_program(g, core, T, topo):
         iota(T.BS[:, 0:16], [[128, 2], [16, 8]], 0, 0, ["BSa"], False)
         iota(T.BS[:, 16:32], [[16, 2], [32, 8]], 0, 0, ["BSb"], False)
 
-    def third_constants():
-        ts(T.ZS[:, 0], T.CI[:], q("cv"), A.is_equal, ["CI", "cv"], ["ZS0"])
-        ts(T.ZS[:, 1], T.CI[:], q("cv"), A.is_equal, ["CI", "cv", "sg"], ["ZS1"], (), q("sg"), A.mult)
-        tt(T.ZS[:, 2, 0:143], T.ZS[:, 0, 0:143], T.ZS[:, 0, 1:144], A.subtract, ["ZS0"], ["ZS2"])
+    def k_duels():
+        ts(T.QK[:, 1:2], T.QJ[:, 0:1], 2, A.arith_shift_right, ["QJ"], ["QK1"])
+        ts(T.QK[:, 2:3], T.QJ[:, 0:1], 3, A.bitwise_and, ["QJ"], ["QK2"])
         ts(T.CR[:], T.CR[:], 3, A.bitwise_and, ["CR"], ["CR"])
+        copy(T.QC[:, COLS.index("a"):COLS.index("b") + 1], T.QK[:, 1:3], ["QK1", "QK2"], ["a", "b"])
         col("nd", "a", "b", A.not_equal)
-        col("dg", "a", "b", A.is_equal, -1.0, A.mult)
-        col("dw", "a", "b", A.is_equal, 4.0, A.mult)
         col("t0", "a", "b", A.is_lt, -0.5, A.add)
-        col("a32", "a", 1.0 / (32 if TE[1] == "S" else 16), A.mult)
-        ts(T.EA[:, 0], T.CR[:], q("a"), A.is_equal, ["CR", "a", "nd"], ["EA0"], (), q("nd"), A.mult)
         ts(T.EA[:, 1], T.CR[:], q("b"), A.is_equal, ["CR", "b"], ["EA1"])
-        col("dw", "dw", 1.0, A.add)
+        ts(T.EA[:, 0], T.CR[:], q("a"), A.is_equal, ["CR", "a", "nd"], ["EA0"], (), q("nd"), A.mult)
+        col("dw", "nd", -4.0, A.mult, 5.0, A.add)
         tt(T.EA[:, 1], T.EA[:, 1], T.EA[:, 0], A.subtract, ["EA0", "EA1"], ["EA1"])
-        ts(M("W2"), M("CA"), q("a"), A.is_equal, ["CA", "a", "dw"], ["W2"], (), q("dw"), A.mult)
+        col("dg", "nd", -1.0, A.add)
         tt(T.EA[:, 2, 0:4], T.EA[:, 1, 0:4], T.EA[:, 1, 1:5], A.subtract, ["EA1"], ["EA2"])
         ts(q("b1"), T.EA[:, 1, 0:1], 16.0, A.mult, ["EA1", "t0"], ["b1"], (), q("t0"), A.add)
-        ts(M("W2"), M("W2"), q("dg"), A.add, ["W2", "dg"], ["W2"])
+        ts(M("W2"), M("CA"), q("a"), A.is_equal, ["CA", "a", "dw"], ["W2"], (), q("dw"), A.mult)
         col("nb1", "b1", -1.0, A.mult)
-        ts(M("W3"), T.BO[:], q("a32"), A.mult, ["BO", "a32"], ["W3"])
-        for i in range(4):
-            ts(T.W1T[:, i], T.BO[:], T.EA[:, 2, i:i + 1], A.mult, ["BO", "EA2"], ["W1T%d" % i])
+        ts(M("W2"), M("W2"), q("dg"), A.add, ["W2", "dg"], ["W2"])
+        ts(M("W3V"), T.BO[:], q("a"), A.mult, ["BO", "a"], ["W3V"], (), 1.0 / 16, A.mult)
         tt(M("W2"), M("W2"), T.BO[:], A.mult, ["W2", "BO"], ["W2"])
+        ts(M("W3S"), T.BO[:], q("a"), A.mult, ["BO", "a"], ["W3S"], (), 1.0 / 32, A.mult)
+
+    def k_counts(e):
         for i in range(4):
+            lin(e, T.W1T[:, i], T.BO[:], T.EA[:, 2, i:i + 1], 0.0, ["BO", "EA2"], ["W1T%d" % i])
             mm(T.X1[:, 128 * i:128 * i + 128], [(T.W1T[:, i], M("ID"))], ["W1T%d" % i, "ID"], ["X1"])
+
+    def k_turned(e):
+        lin(e, T.W1[:], T.X1[:], 1.0, 0.0, [], ["W1"], ["X1"])
+
+    def k_biases():
         col("bA", "p", 2 * LN2, A.mult, 53 * LN2, A.add)
         col("bB", "p", -LN2, A.mult, -109 * LN2, A.add)
         col("bV", "p", -126976.0, A.mult, 3801088.0, A.add)
-        for c in (0, 1):
-            b = "bF%d" % c
-            col(b, "p", P0[c] - 0.5, A.is_gt, 16384.0, A.mult)
-            ts(q("t1"), q("p"), 1024.0, A.mult, ["p"], ["t1"], (), -31744.0, A.add) if c == 0 else None
-            col(b, b, "t1", A.add)
-        copy(T.W1[:], T.X1[:], [], ["W1"], ["X1"])
+        col("bF0", "p", 1024.0, A.mult, -31744.0, A.add)
+        col("bF1", "p", P0[1] - 0.5, A.is_gt, 16384.0, A.mult)
+        col("bF1", "bF1", "bF0", A.add)
+
+    def k_lists():
         ts(T.BS[:], T.BS[:], q("p"), A.add, ["BSa", "BSb", "p"], ["BSa", "BSb"])
         ts(T.AD[:, 0:16], T.BS[:, 0:16], 65536.0, A.mult, ["BSa"], ["ADa"])
         ts(T.AD[:, 16:32], T.BS[:, 16:32], 4.0, A.mult, ["BSb"], ["ADb"])
         tt(T.AD[:, 0:16], T.AD[:, 0:16], T.BS[:, 16:32], A.add, ["ADa", "BSb"], ["ADa"])
 
-    def scalar_constants():
-        act(T.QB[:, 0:1], q("p"), AF.Exp, ["p"], ["QB"], bias=11 * LN2, scale=-LN2)
-        act(q("sF"), T.QB[:, 0:1], AF.Copy, ["QB"], ["sF"])
-
-    def spread_constants(e, ks):
-        for k in ks:
-            if e == "V":
-                ts(T.BK[:, k], T.BO[:], T.RA[:, k:k + 1], A.mult, ["BO", "RA"], ["BK%d" % k])
-            else:
-                act(T.BK[:, k], T.BO[:], AF.Copy, ["BO", "RA"], ["BK%d" % k], scale=T.RA[:, k:k + 1])
+    def k_steps(e, a, b):
+        for k in range(a, b):
+            lin(e, T.BK[:, k], T.BO[:], T.RA[:, k:k + 1], 0.0, ["BO", "RA"], ["BK%d" % k])
 
     def weights(a, b):
         iota(T.DI[:, a:b], [[1, b - a], [0, 128]], a + 1, 0, ["DI%d" % a])
@@ -342,15 +347,16 @@ def rank_program(g, core, T, topo):
         mm(T["Q%d" % c][:, 0], [(T.RD[:, 4 * j + i], T.EQ[:, c, 4 * j + i]) for i in range(4)],
            ["EQ%d%d" % (c, j)] + ["RD%d" % (4 * j + i) for i in range(4)], ["Q%d" % c], False, j == 1)
 
-    def hashes(t, c, e="V"):
+    def jury(c, e="V"):
         n = str(c)
         elist(e, c)
         diffs(c, 0)
         diffs(c, 1)
-        tt(H("XX", c), H("ES", c), T["E" + n][:, 1], A.mult, ["ES" + n], ["XX" + n], ["E" + n])
-        equal(c, 0)
-        equal(c, 1)
         lin("V", H("OFM", c), H("ES", c), 1.0, -1024.0, ["ES" + n], ["OFM" + n])
+        tt(H("XX", c), H("ES", c), T["E" + n][:, 1], A.mult, ["ES" + n], ["XX" + n], ["E" + n])
+
+    def hashes(c):
+        n = str(c)
         tt(H("HI", c), H("XX", c), T["Q" + n][:, 0], A.add, ["XX" + n], ["HI" + n], ["Q" + n])
         ts(H("HI", c), H("HI", c), 5, A.arith_shift_right, ["HI" + n], ["HI" + n], (), 4095, A.bitwise_and)
         copy(H("OFX", c), H("HI", c), ["HI" + n], ["OFX" + n])
@@ -370,35 +376,38 @@ def rank_program(g, core, T, topo):
         mm(T["Q" + n][:, 1], [(T.W1[:, i], T.RR[:, i, 128 * c:128 * c + 128]) for i in range(4)],
            ["W1"] + ["RR%d%d" % (c, i) for i in range(4)], ["Q" + n])
 
-    def duels(c):
+    size = {}
+
+    def duels(e, c):
         n = str(c)
-        if TE[0] == "S":
+        size[c] = 1.0 if e == "S" else 0.5
+        if e == "S":
             act(H("T1", c), T["Q" + n][:, 1], AF.Sign, ["b1"], ["T1" + n], ["Q" + n], bias=q("b1"))
         else:
             ts(H("T1", c), T["Q" + n][:, 1], q("nb1"), A.is_gt, ["nb1"], ["T1" + n], ["Q" + n], -0.5, A.add)
         mm(T["E" + n][:, 3], [(M("W2"), H("T1", c))], ["W2", "T1" + n], ["E" + n])
 
-    def winner(c):
+    def winner(e, c):
         n = str(c)
-        th = 3.0 if TE[0] == "S" else 1.5
-        if TE[1] == "S":
+        th = 3.0 * size[c]
+        if e == "S":
             act(H("T2", c), T["E" + n][:, 3], AF.Sign, [], ["T2" + n], ["E" + n], bias=-th)
         else:
             ts(H("T2", c), T["E" + n][:, 3], th, A.is_gt, [], ["T2" + n], ["E" + n], -0.5, A.add)
-        mm(T["Q" + n][:, 2], [(M("ID"), H("QS", c)), (M("ID"), T.RR[:, 0, 128 * c:128 * c + 128]), (M("W3"), H("T2", c))],
-           ["ID", "QS" + n, "RR%d0" % c, "W3", "T2" + n], ["Q" + n])
+        mm(T["Q" + n][:, 2], [(M("ID"), H("QS", c)), (M("ID"), T.RR[:, 0, 128 * c:128 * c + 128]), (M("W3" + e), H("T2", c))],
+           ["ID", "QS" + n, "RR%d0" % c, "W3" + e, "T2" + n], ["Q" + n])
 
     def survivors(c):
         n = str(c)
         ts(H("AL", c), T["Q" + n][:, 2], 1535.25, A.is_equal, [], ["AL" + n], ["Q" + n], -2.0, A.add)
 
-    def spread(c, h, e="S"):
+    def spread(c, h, es="SS"):
         a = 128 * c + 64 * h
         for m in (0, 1):
-            D, db = T["D%d" % m], "D%d" % m
+            D, db = T["X%d" % (m + 1)], "X%d" % (m + 1)
             op("P", ["AL%d" % c] + ["BK%d" % k for k in range(16)], [], [db], lambda: [
                 p.matmul(D[:, j::8], T.BK[:, 2 * j + m], T.AL[:, a:a + 64], True, True) for j in range(8)])
-            lin(e, T.DS[:, 16 * a + m:16 * a + 1024:2], D[:], 1.0, 0.0, [], ["DS%d%d%d" % (c, h, m)], [db])
+            lin(es[m], T.DS[:, 16 * a + m:16 * a + 1024:2], D[:], 1.0, 0.0, [], ["DS%d%d%d" % (c, h, m)], [db])
 
     def maximum(c, h, x):
         a = 128 * c + 64 * h
@@ -473,11 +482,11 @@ def rank_program(g, core, T, topo):
 
     def uturn(t):
         z, k0 = landed(t, 0)
-        mm(T.X2[:, 256:272], [(slide(0, a), z[:, 2 * a + 1::32]) for a in range(16)], k0 + landed(t, 1)[1] + ["ZS0"], ["X2"])
+        mm(T.Q1[:, 3, 0:16], [(slide(0, a), z[:, 2 * a + 1::32]) for a in range(16)], k0 + landed(t, 1)[1] + ["ZS0"], ["Q1"])
 
     def clist():
         r = T.LI[:, 0:16]
-        lin("V", r, T.X2[:, 256:272], 2.0, 8.0, [], ["LIa"], ["X2"])
+        lin("V", r, T.Q1[:, 3, 0:16], 2.0, 8.0, [], ["LIa"], ["Q1"])
         ts(r, r, 3, A.bitwise_and, ["LIa"], ["LIa"])
         tt(r, r, T.AD[:, 16:32], A.add, ["LIa", "ADb"], ["LIa"])
         copy(T.LC[:], r, ["LIa"], ["LC"])
@@ -485,7 +494,7 @@ def rank_program(g, core, T, topo):
     def first():
         mm(T.D1[:, 0:256], [(M("ID"), T.HH[:]), (M("TB"), T.AL[:])], ["ID", "TB", "HH0", "HH1", "AL0", "AL1"], ["D1"])
         act(T.VL[:], T.D1[:, 0:256], AF.Relu, ["bV"], ["VL"], ["D1"], bias=q("bV"), scale=-65536.0)
-        mm(T.X2[:, 272:288], [(slide(0, a), T.VL[:, a::16]) for a in range(16)], ["VL", "ZS0"], ["X2"])
+        mm(T.Q1[:, 3, 16:32], [(slide(0, a), T.VL[:, a::16]) for a in range(16)], ["VL", "ZS0"], ["Q1"])
 
     def alone():
         mm(T.D0[:, 0:256], [(T.BO[:], T.AL[:])], ["BO", "AL0", "AL1"], ["D0"])
@@ -495,7 +504,7 @@ def rank_program(g, core, T, topo):
         ts(M("AB"), M("ON"), q("acc"), A.mult, ["ON", "acc"], ["AB"], (), 16.0, A.mult)
 
     def xlists():
-        tt(T.LI[:, 16:32], T.AD[:, 0:16], T.X2[:, 272:288], A.add, ["ADa"], ["LIb"], ["X2"])
+        tt(T.LI[:, 16:32], T.AD[:, 0:16], T.Q1[:, 3, 16:32], A.add, ["ADa"], ["LIb"], ["Q1"])
         ts(T.LI[:, 32:48], T.LI[:, 16:32], 4095, A.bitwise_and, ["LIb"], ["LIc"])
         ts(T.LI[:, 48:64], T.LI[:, 16:32], 12, A.arith_shift_right, ["LIb"], ["LId"])
         copy(T.LX[:], T.LI[:, 32:64], ["LIc", "LId"], ["LX"])
@@ -508,138 +517,90 @@ def rank_program(g, core, T, topo):
     def xwrite():
         op("V", ["XQ", "LX"], ["XW"], [], lambda: v.tensor_copy(T.XW[:, 0:4096].indirect(T.LX[:, 0:16]), T.XQ[:]))
 
-    first_constants()
-    for t in range(LEVELS):
-        last = t == LEVELS - 1
-        seats(t, 0)
-        if t == 0:
-            seats(t, 1)
-            ts(T.CW[:, 0:512], T.CM[:, 0:512], 1023, A.bitwise_and, ["CM0"], ["CW"])
-            ts(T.CW[:, 512:1024], T.CM[:, 512:1024], 1023, A.bitwise_and, ["CM1"], ["CW"])
-        cg("S", 0, 0)
-        cg("V", 0, 1)
-        if t > 0:
-            carry()
-            seats(t, 1)
-        cg("S", 1, 0)
-        cg("S", 1, 1)
-        members(t, 0, 0)
-        usum(t, 0)
-        members(t, 0, 1)
-        if t == 0:
-            second_constants()
-            weights(0, 8)
-            weights(8, 16)
-        else:
-            xlists()
-            xnew(t - 1)
-        hashes(t, 0)
-        mg("S", 0, 0)
-        usum(t, 1)
-        members(t, 1, 0)
-        members(t, 1, 1)
-        if t == 0:
-            third_constants()
-        else:
-            xwrite()
-        xg("S", 0, 0)
-        xg("S", 0, 1)
-        hashes(t, 1)
-        bins(0, 0)
-        uturn(t)
-        xg("V", 1, 0)
-        xg("S", 1, 1)
-        bins(0, 1)
-        mg("S", 0, 1)
-        if t == 0:
-            spread_constants("V", range(16))
-        floors("V", 0)
-        bins(1, 0)
-        high(0)
-        high(1)
-        clist()
-        duels(0)
-        bins(1, 1)
-        mg("V", 1, 0, 0, 1)
-        winner(0)
-        floors("V", 1)
-        survivors(0)
-        spread(0, 0)
-        places(0)
-        duels(1)
-        mg("V", 1, 0, 1, 2)
-        winner(1)
-        spread(0, 1)
-        mg("V", 1, 0, 2, 3)
-        survivors(1)
-        powers(0)
-        if not last:
-            maximum(0, 0, "Y")
-            maximum(0, 0, "X")
-            mg("S", 1, 1)
-            maximum(0, 1, "Y")
-            maximum(0, 1, "X")
-            leave(t, 0)
-            spread(1, 0)
-            mg("V", 1, 0, 3, 4)
-            places(1)
-            keyed(0)
-            spread(1, 1)
-            cut(0)
-            maximum(1, 0, "Y")
-            maximum(1, 0, "X")
-            powers(1)
-            column("S", 0)
-            maximum(1, 1, "Y")
-            maximum(1, 1, "X")
-            leave(t, 1)
-            for a in ((16, 24, 32) if t == 0 else (40, 48, 56)):
-                weights(a, a + 8)
-            keyed(1)
-            cut(1)
-            column("S", 1)
-            first()
-            alone()
-            cwrite((0, 1))
-    first()
-    places(1)
-    spread(1, 0)
-    maximum(0, 0, "X")
-    maximum(0, 1, "X")
-    spread(1, 1)
-    halved(2, 0)
-    xlists()
-    keyed(0)
-    cut(0)
-    powers(1)
-    maximum(1, 0, "X")
-    maximum(1, 1, "X")
-    mg("S", 1, 1)
-    halved(2, 1)
-    xnew(2)
-    xwrite()
-    column("S", 0)
-    keyed(1)
-    cut(1)
+    def committees(j):
+        ts(T.CW[:, 512 * j:512 * j + 512], T.CM[:, 512 * j:512 * j + 512], 1023, A.bitwise_and, ["CM%d" % j], ["CW"])
+
     dis = ["DI%d" % a for a in range(0, 64, 8)]
-    column("S", 1)
-    mm(T.Q0[:, 0, 0:64], [(T.DI[:, m], T.XW[:, 64 * m:64 * m + 64]) for m in range(64)], ["XW"] + dis, ["Q0"])
-    mg("V", 1, 0, 3, 4)
-    cwrite((0, 1))
-    act(T.CF[:], T.CW[:], AF.Copy, ["CW"], ["CF"])
-    mm(T.Q1[:, 0, 0:64], [(T.DI[:, m], T.CF[:, 64 * m:64 * m + 64]) for m in range(16)], ["CF"] + dis, ["Q1"])
-    for c in (0, 1):
-        result("X", c)
-    dma("Y", "oz", T.yz[:], T.OZ[:], ["OZ0", "OZ1"], [])
-    for c in (0, 1):
-        maximum(c, 0, "Y")
-        maximum(c, 1, "Y")
-        result("Y", c)
-    dma("Y", "os", T.ys[:], T.OS[:], ["OS0", "OS1"], [])
-    act(T.OX[:], T.Q0[:, 0, 0:64], AF.Copy, [], ["OX"], ["Q0"])
-    dma("S", "ox", T.yx[:], T.OX[:], ["OX"], [])
-    act(T.OC[:], T.Q1[:, 0, 0:64], AF.Copy, [], ["OC"], ["Q1"])
-    dma("S", "oc", T.yc[:], T.OC[:], ["OC"], [])
+
+    def xsum():
+        mm(T.Q0[:, 0, 0:64], [(T.DI[:, m], T.XW[:, 64 * m:64 * m + 64]) for m in range(64)], ["XW"] + dis, ["Q0"])
+
+    def xout():
+        act(T.OX[:], T.Q0[:, 0, 0:64], AF.Copy, [], ["OX"], ["Q0"])
+        dma("S", "ox", T.yx[:], T.OX[:], ["OX"], [])
+
+    def csum():
+        act(T.CF[:], T.CW[:], AF.Copy, ["CW"], ["CF"])
+        mm(T.E0[:, 0, 0:64], [(T.DI[:, m], T.CF[:, 64 * m:64 * m + 64]) for m in range(16)], ["CF"] + dis[:2], ["E0"])
+
+    def cout():
+        act(T.OC[:], T.E0[:, 0, 0:64], AF.Copy, [], ["OC"], ["E0"])
+        dma("S", "oc", T.yc[:], T.OC[:], ["OC"], [])
+
+    def sout():
+        dma("Y", "os", T.ys[:], T.OS[:], ["OS0", "OS1"], [])
+
+    def zout():
+        dma("Y", "oz", T.yz[:], T.OZ[:], ["OZ0", "OZ1"], [])
+
+    for t in range(LEVELS - 1):
+        if t == 0: k_rows()
+        if t == 1: carry()
+        if t == 0: k_pick("S", 12, 16); k_blocks(); k_order(); k_slides(); k_pick("S", 0, 4); k_pairs()
+        if t == 0: k_pick("S", 4, 8); k_sums("V"); k_later(); k_pick("S", 8, 12); committees(0); seats(t, 1)
+        if t == 1: xlists()
+        if t == 0: k_steps("S", 0, 4)
+        seats(t, 0)
+        if t == 0: k_steps("V", 4, 8); committees(1); weights(0, 8); weights(8, 16); k_start("V", 0)
+        cg("S", 0, 0, 2, 4); usum(t, 0); cg("V", 0, 0, 0, 2); cg("V", 0, 1, 2, 4)
+        if t == 0: k_duels()
+        if t == 1: seats(t, 1)
+        members(t, 0, 0)
+        if t == 1: xnew(t - 1)
+        cg("S", 0, 1, 0, 2); cg("S", 1, 1, 2, 4); members(t, 0, 1); cg("V", 1, 1, 0, 2); jury(0, "S")
+        if t == 0: k_counts("S")
+        cg("S", 1, 0, 2, 4); members(t, 1, 1); equal(0, 0); equal(0, 1)
+        if t == 1: xwrite()
+        cg("S", 1, 0, 0, 2)
+        if t == 0: k_biases()
+        mg("S", 0, 0, 0, 2)
+        if t == 0: k_start("V", 1)
+        hashes(0); members(t, 1, 0)
+        if t == 0: k_turned("V")
+        usum(t, 1); jury(1, "S"); equal(1, 0); equal(1, 1); xg("V", 0, 1, 0, 2); xg("S", 0, 0, 0, 2)
+        xg("S", 0, 1, 2, 4); bins(0, 1); hashes(1); xg("S", 0, 0, 2, 4); bins(0, 0)
+        if t == 0: k_steps("S", 8, 12)
+        uturn(t)
+        if t == 0: k_steps("V", 12, 16)
+        xg("V", 1, 0, 0, 2); floors("V", 0); xg("V", 1, 1, 0, 2); xg("S", 1, 0, 2, 4); bins(1, 0); xg("S", 1, 1, 2, 4)
+        mg("S", 0, 1, 0, 2); bins(1, 1); duels("V", 0); winner("S", 0); mg("V", 1, 0, 3, 4); mg("S", 0, 0, 2, 4)
+        mg("V", 1, 0, 2, 3); floors("V", 1); survivors(0); spread(0, 0, "SS"); mg("V", 1, 0, 1, 2); duels("V", 1)
+        places(0); high(0); spread(0, 1, "SS"); mg("S", 1, 0, 0, 1); mg("V", 0, 1, 2, 4); winner("V", 1)
+        maximum(0, 0, "X"); powers(0); maximum(0, 0, "Y"); mg("S", 1, 1, 2, 4); survivors(1); maximum(0, 1, "Y")
+        maximum(0, 1, "X"); leave(t, 0)
+        if t == 0: k_lists()
+        clist(); keyed(0); high(1); spread(1, 0, "SS"); spread(1, 1, "SS"); cut(0, 0, 4); cut(0, 4, 8)
+        mg("S", 1, 1, 0, 2); cut(0, 8, 12); cut(0, 12, 16); places(1); alone(); powers(1); maximum(1, 0, "X")
+        maximum(1, 0, "Y"); maximum(1, 1, "X"); maximum(1, 1, "Y"); leave(t, 1); keyed(1); cut(1, 0, 8); column("S", 0)
+        cut(1, 8, 16); column("S", 1); first(); cwrite((0,)); cwrite((1,))
+        for a in (16, 24, 32):
+            weights(24 * t + a, 24 * t + a + 8)
+    t = LEVELS - 1
+    seats(t, 0); carry(); usum(t, 0); cg("S", 0, 1, 0, 2); cg("V", 0, 1, 2, 4); members(t, 0, 1); cg("S", 0, 0, 2, 4)
+    cg("V", 0, 0, 0, 2); members(t, 0, 0); xlists(); xnew(t - 1); jury(0, "S"); seats(t, 1); cg("S", 1, 1, 0, 2)
+    cg("S", 1, 0, 0, 2); cg("S", 1, 1, 2, 4); uturn(t); usum(t, 1); equal(0, 0); equal(0, 1); mg("S", 0, 0, 0, 2)
+    cg("V", 1, 0, 2, 4); xwrite(); members(t, 1, 0); hashes(0); xg("S", 0, 0, 2, 4); members(t, 1, 1); jury(1, "V")
+    equal(1, 0); equal(1, 1); xg("V", 0, 1, 0, 2); hashes(1); xg("S", 0, 0, 0, 2); bins(0, 0); xg("S", 0, 1, 2, 4)
+    xg("V", 1, 0, 2, 4); bins(0, 1); xg("S", 1, 0, 0, 2); xg("S", 1, 1, 0, 2); bins(1, 0); floors("V", 0); duels("S", 0)
+    xg("V", 1, 1, 2, 4); mg("V", 1, 0, 3, 4); high(1); bins(1, 1); mg("S", 1, 0, 1, 2); winner("V", 0); floors("V", 1)
+    survivors(0); places(0); high(0); mg("S", 0, 0, 2, 4); duels("S", 1); mg("V", 0, 1, 0, 2); powers(0); keyed(0)
+    winner("S", 1); survivors(1); mg("S", 1, 0, 0, 1); spread(0, 0, "VS"); spread(0, 1, "SS"); cut(0, 0, 4)
+    spread(1, 0, "SS"); clist(); spread(1, 1, "SS"); places(1); maximum(0, 0, "Y"); maximum(0, 0, "X")
+    maximum(0, 1, "X"); result("X", 0); halved(2, 0); cut(0, 4, 8); cut(0, 8, 12); cut(0, 12, 16); maximum(1, 0, "X")
+    maximum(1, 1, "X"); powers(1); keyed(1); result("X", 1); mg("S", 0, 1, 2, 4); first(); halved(2, 1); cut(1, 0, 8)
+    cut(1, 8, 16); maximum(0, 1, "Y"); xlists(); xnew(2); xwrite(); column("S", 0); cwrite((0,)); mg("S", 1, 1, 0, 2)
+    mg("S", 1, 1, 2, 4); zout(); column("S", 1); cwrite((1,)); maximum(1, 1, "Y"); xsum(); mg("S", 1, 0, 2, 3)
+    maximum(1, 0, "Y"); result("Y", 0); result("Y", 1); csum(); sout(); xout(); cout()
     for sem in sorted(cnt):
         g.wait_ge(T.sem[sem], cnt[sem])
     for t in range(LEVELS - 1):

@@ -5,12 +5,13 @@ from concourse.mybir import dt, AluOpType, AxisListType, ActivationFunctionType
 A = AluOpType
 AF = ActivationFunctionType
 LEVELS = 3
-P0 = (16, 11)
+ROWS = (0, 1, 7, 2, 3, 6, 4, 5)
+P0 = 12
 LN2 = math.log(2.0)
 
 _B, _H, _F, _I, _U = "bfloat16", "float16", "float32", "int32", "uint16"
-MATS = ("ON", "ID", "BO2", "BOM", "KU", "KQ", "AB", "TA", "TU", "TB", "W2", "W3V", "W3S", "CA", "TRI")
-COLS = ("P", "p", "g16", "g1", "cv", "sg", "a", "b", "nd", "dw", "dg", "b1", "nb1", "bA", "bB", "bV", "sF", "bF0", "bF1", "acc", "t0")
+MATS = ("ON", "ID", "BO2", "BOM", "KU", "KQ", "K16", "AB", "TA", "TU", "TB", "W2", "W3V", "W3S", "CA", "TRI")
+COLS = ("P", "p", "g16", "g1", "cv", "sg", "a", "b", "nd", "dw", "dg", "b1", "nb1", "bA", "bB", "bV", "sF", "bF", "acc", "t0", "t1")
 SCRATCH = {
     "XW": ("sbuf", [128, 4096], _B), "CM": ("sbuf", [128, 1024], _I), "CW": ("sbuf", [128, 1024], _I),
     "S3": ("sbuf", [128, 8, 2, 16], _I), "Z3": ("sbuf", [128, 8, 2, 16], _B), "CF": ("sbuf", [128, 1024], _H),
@@ -39,8 +40,7 @@ SCRATCH = {
     "OX": ("sbuf", [128, 64], _F), "OC": ("sbuf", [128, 64], _F),
     "E0": ("psum", [128, 4, 128], _F), "E1": ("psum", [128, 4, 128], _F),
     "Q0": ("psum", [128, 4, 128], _F), "Q1": ("psum", [128, 4, 128], _F),
-    "D0": ("psum", [128, 512], _F), "D1": ("psum", [128, 512], _F),
-    "X1": ("psum", [128, 512], _F), "X2": ("psum", [128, 512], _F),
+    "D": ("psum", [128, 2, 512], _F), "X": ("psum", [128, 2, 512], _F),
 }
 SEMAPHORES = ["V", "S", "P", "G", "ds", "dz", "dc0", "dc1", "dx", "os", "oz", "ox", "oc"] + [
     k + t + c for k in ("arr", "snt") for t in "01" for c in "01"]
@@ -177,6 +177,7 @@ def rank_program(g, core, T, topo):
         fill(M("KU"), 41.0 / 128, ["KU"])
         fill(M("KQ"), (4096 - 41 * 1024) / 128, ["KQ"])
         fill(M("AB"), -4096.0, ["AB"])
+        fill(M("K16"), 16.0, ["K16"])
         ts(T.QJ[:], T.QI[:], 15, A.bitwise_and, ["QI"], ["QJ"])
         copy(q("p"), T.QJ[:, 0:1], ["QJ"], ["p"])
         ts(T.PT[:], T.QJ[:], 0, A.is_equal, ["QJ"], ["PT"])
@@ -264,18 +265,18 @@ def rank_program(g, core, T, topo):
     def k_counts(e):
         for i in range(4):
             lin(e, T.W1T[:, i], T.BO[:], T.EA[:, 2, i:i + 1], 0.0, ["BO", "EA2"], ["W1T%d" % i])
-            mm(T.X1[:, 128 * i:128 * i + 128], [(T.W1T[:, i], M("ID"))], ["W1T%d" % i, "ID"], ["X1"])
+            mm(T.X[:, 0, 128 * i:128 * i + 128], [(T.W1T[:, i], M("ID"))], ["W1T%d" % i, "ID"], ["X0"])
 
     def k_turned(e):
-        lin(e, T.W1[:], T.X1[:], 1.0, 0.0, [], ["W1"], ["X1"])
+        lin(e, T.W1[:], T.X[:, 0], 1.0, 0.0, [], ["W1"], ["X0"])
 
     def k_biases():
         col("bA", "p", 2 * LN2, A.mult, 53 * LN2, A.add)
         col("bB", "p", -LN2, A.mult, -109 * LN2, A.add)
         col("bV", "p", -126976.0, A.mult, 3801088.0, A.add)
-        col("bF0", "p", 1024.0, A.mult, -31744.0, A.add)
-        col("bF1", "p", P0[1] - 0.5, A.is_gt, 16384.0, A.mult)
-        col("bF1", "bF1", "bF0", A.add)
+        col("t1", "p", 1024.0, A.mult, -31744.0, A.add)
+        col("bF", "p", P0 - 0.5, A.is_gt, 16384.0, A.mult)
+        col("bF", "bF", "t1", A.add)
 
     def k_lists():
         ts(T.BS[:], T.BS[:], q("p"), A.add, ["BSa", "BSb", "p"], ["BSa", "BSb"])
@@ -340,20 +341,21 @@ def rank_program(g, core, T, topo):
 
     def diffs(c, j):
         for i in range(4):
-            mm(T["D%d" % j][:, 128 * i:128 * i + 128], [(T.WD[:, 4 * j + i], H("ES", c))], ["ES%d" % c, "WD%d" % (4 * j + i)], ["D%d" % j])
+            mm(T.D[:, j, 128 * i:128 * i + 128], [(T.WD[:, 4 * j + i], H("ES", c))], ["ES%d" % c, "WD%d" % (4 * j + i)], ["D%d" % j])
 
-    def equal(c, j):
-        ts(T.EQ[:, c, 4 * j:4 * j + 4], T["D%d" % j][:], 0.0, A.is_equal, [], ["EQ%d%d" % (c, j)], ["D%d" % j])
+    def equal(c, a, b):
+        ts(T.EQ[:, c, 4 * a:4 * b], T.D[:, a:b], 0.0, A.is_equal, [], ["EQ%d%d" % (c, j) for j in range(a, b)],
+           ["D%d" % j for j in range(a, b)])
+
+    def repeats(c, j):
         mm(T["Q%d" % c][:, 0], [(T.RD[:, 4 * j + i], T.EQ[:, c, 4 * j + i]) for i in range(4)],
            ["EQ%d%d" % (c, j)] + ["RD%d" % (4 * j + i) for i in range(4)], ["Q%d" % c], False, j == 1)
 
-    def jury(c, e="V"):
-        n = str(c)
-        elist(e, c)
-        diffs(c, 0)
-        diffs(c, 1)
-        lin("V", H("OFM", c), H("ES", c), 1.0, -1024.0, ["ES" + n], ["OFM" + n])
-        tt(H("XX", c), H("ES", c), T["E" + n][:, 1], A.mult, ["ES" + n], ["XX" + n], ["E" + n])
+    def mlist(c):
+        lin("V", H("OFM", c), H("ES", c), 1.0, -1024.0, ["ES%d" % c], ["OFM%d" % c])
+
+    def product(c):
+        tt(H("XX", c), H("ES", c), T["E%d" % c][:, 1], A.mult, ["ES%d" % c], ["XX%d" % c], ["E%d" % c])
 
     def hashes(c):
         n = str(c)
@@ -361,18 +363,23 @@ def rank_program(g, core, T, topo):
         ts(H("HI", c), H("HI", c), 5, A.arith_shift_right, ["HI" + n], ["HI" + n], (), 4095, A.bitwise_and)
         copy(H("OFX", c), H("HI", c), ["HI" + n], ["OFX" + n])
 
-    def high(c):
-        lin("V", H("HH", c), H("OFX", c), -1.0 / 65536, -6.0 + 127.5 / 65536, ["OFX%d" % c], ["HH%d" % c])
+    def high(e):
+        src = "OFX" if e == "V" else "HI"
+        lin(e, T.HH[:], T[src][:], -1.0 / 65536, -6.0 + 127.5 / 65536, ["OFX0", "HI0", "OFX1", "HI1"], ["HH"])
 
     def bins(c, h):
         mm(T["E%d" % c][:, 2, 64 * h:64 * h + 64], [(slide(1, k), fan("XG", c, h, k)) for k in range(16)],
            got("XG", c, h) + ["ZS1"], ["E%d" % c])
 
-    def floors(e, c):
+    def quarter(e, c):
+        lin(e, H("QS", c), T["E%d" % c][:, 2], -1.0, 0.0, [], ["QS%d" % c], ["E%d" % c])
+
+    def floors(e, c, j):
+        for i in (2 * j, 2 * j + 1):
+            lin(e, T.RR[:, i, 128 * c:128 * c + 128], H("QS", c), -1.0, 1535.625 + i / 4, ["QS%d" % c], ["RR%d%d" % (c, i)])
+
+    def counts(c):
         n = str(c)
-        lin(e, H("QS", c), T["E" + n][:, 2], -1.0, 0.0, [], ["QS" + n], ["E" + n])
-        for i in range(4):
-            lin("V", T.RR[:, i, 128 * c:128 * c + 128], H("QS", c), -1.0, 1535.625 + i / 4, ["QS" + n], ["RR%d%d" % (c, i)])
         mm(T["Q" + n][:, 1], [(T.W1[:, i], T.RR[:, i, 128 * c:128 * c + 128]) for i in range(4)],
            ["W1"] + ["RR%d%d" % (c, i) for i in range(4)], ["Q" + n])
 
@@ -385,49 +392,58 @@ def rank_program(g, core, T, topo):
             act(H("T1", c), T["Q" + n][:, 1], AF.Sign, ["b1"], ["T1" + n], ["Q" + n], bias=q("b1"))
         else:
             ts(H("T1", c), T["Q" + n][:, 1], q("nb1"), A.is_gt, ["nb1"], ["T1" + n], ["Q" + n], -0.5, A.add)
-        mm(T["E" + n][:, 3], [(M("W2"), H("T1", c))], ["W2", "T1" + n], ["E" + n])
+
+    def scores(c):
+        mm(T["E%d" % c][:, 3], [(M("W2"), H("T1", c))], ["W2", "T1%d" % c], ["E%d" % c])
 
     def winner(e, c):
         n = str(c)
         th = 3.0 * size[c]
+        size[n] = e
         if e == "S":
             act(H("T2", c), T["E" + n][:, 3], AF.Sign, [], ["T2" + n], ["E" + n], bias=-th)
         else:
             ts(H("T2", c), T["E" + n][:, 3], th, A.is_gt, [], ["T2" + n], ["E" + n], -0.5, A.add)
+
+    def match(c):
+        n = str(c)
+        e = size[n]
         mm(T["Q" + n][:, 2], [(M("ID"), H("QS", c)), (M("ID"), T.RR[:, 0, 128 * c:128 * c + 128]), (M("W3" + e), H("T2", c))],
-           ["ID", "QS" + n, "RR%d0" % c, "W3" + e, "T2" + n], ["Q" + n])
+           ["ID", "QS" + n, "RR%d0" % c, "W3V", "W3S", "T2" + n], ["Q" + n])
 
     def survivors(c):
         n = str(c)
         ts(H("AL", c), T["Q" + n][:, 2], 1535.25, A.is_equal, [], ["AL" + n], ["Q" + n], -2.0, A.add)
 
-    def spread(c, h, es="SS"):
-        a = 128 * c + 64 * h
-        for m in (0, 1):
-            D, db = T["X%d" % (m + 1)], "X%d" % (m + 1)
-            op("P", ["AL%d" % c] + ["BK%d" % k for k in range(16)], [], [db], lambda: [
-                p.matmul(D[:, j::8], T.BK[:, 2 * j + m], T.AL[:, a:a + 64], True, True) for j in range(8)])
-            lin(es[m], T.DS[:, 16 * a + m:16 * a + 1024:2], D[:], 1.0, 0.0, [], ["DS%d%d%d" % (c, h, m)], [db])
+    def steps(c, h, m):
+        a, db = 128 * c + 64 * h, "XD"[h]
+        op("P", ["AL%d" % c] + ["BK%d" % k for k in range(16)], [], [db + str(m)], lambda: [
+            p.matmul(T[db][:, m, j::8], T.BK[:, 2 * j + m], T.AL[:, a:a + 64], True, True) for j in range(8)])
 
-    def maximum(c, h, x):
-        a = 128 * c + 64 * h
-        scan(T[x + "S"][:, 16 * a:16 * a + 1024], T[x + "G"][:, 16 * a:16 * a + 1024], T.DS[:, 16 * a:16 * a + 1024], -1024.0, A.max, A.add,
-             got(x + "G", c, h) + ["DS%d%d0" % (c, h), "DS%d%d1" % (c, h)], ["%sS%d%d" % (x, c, h)])
+    def spread(e, c, h, m):
+        a, db = 128 * c + 64 * h, "XD"[h]
+        lin(e, T.DS[:, 16 * a + m:16 * a + 1024:2], T[db][:, m], 1.0, 0.0, [], ["DS%d%d%d" % (c, h, m)], [db + str(m)])
+
+    def maximum(x, c, h0, h1):
+        a, b, hs = 2048 * c + 1024 * h0, 2048 * c + 1024 * h1, range(h0, h1)
+        scan(T[x + "S"][:, a:b], T[x + "G"][:, a:b], T.DS[:, a:b], -1024.0, A.max, A.add,
+             [k for h in hs for k in got(x + "G", c, h) + ["DS%d%d0" % (c, h), "DS%d%d1" % (c, h)]], ["%sS%d%d" % (x, c, h) for h in hs])
 
     def ends(x, c):
         return T[x + "S"][:, 2048 * c + 15:2048 * c + 2048:16], ["%sS%d0" % (x, c), "%sS%d1" % (x, c)]
 
-    def halved(t, c):
+    def halved(e, t, c):
         src, keys = ends("X", c)
-        lin("V", T["SZ%d" % t][:, 256 * c + 1:256 * c + 256:2], src, 1.0, 255.75, keys, ["SZX%d%d" % (t, c)])
+        lin(e, T["SZ%d" % t][:, 256 * c + 1:256 * c + 256:2], src, 1.0, 255.75, keys, ["SZX%d%d" % (t, c)])
+
+    def sampled(e, t, c):
+        src, keys = ends("Y", c)
+        lin(e, T["SZ%d" % t][:, 256 * c:256 * c + 256:2], src, 1.0, 0.0, keys, ["SZY%d%d" % (t, c)])
 
     def leave(t, c):
         key = "%d%d" % (t, c)
         sz, rz = T["SZ%d" % t], T["RZ%d" % t]
-        src, keys = ends("Y", c)
         blk = lambda x, b: x[:, 256 * c + 32 * b:256 * c + 32 * b + 32]
-        copy(sz[:, 256 * c:256 * c + 256:2], src, keys, ["SZY" + key])
-        halved(t, c)
         sync("G", ["SZX" + key, "SZY" + key], [], [])
         for call in calls_of(core, cores, topo):
             g.remote_dma_fused([RemoteDMATransfer(
@@ -435,50 +451,48 @@ def rank_program(g, core, T, topo):
                 dst_ids=[DstId(rid=topo.addr(d, core)[0], pnc=topo.addr(d, core)[1])],
                 dma_engine_mask=sum(1 << e for e in en), remote_sem=T.sem["arr" + key]) for d, en in call],
                 local_sem=T.sem["snt" + key])
-        copy(blk(rz, rank), blk(sz, rank), ["SZX" + key, "SZY" + key], ["RZ" + key + "o"])
+        sel(blk(rz, rank), blk(sz, rank), [[0, 32]], A.is_ge, 0.0, 0, 0, ["SZX" + key, "SZY" + key], ["RZ" + key + "o"])
         total = sum(len(en) for o in cores if o != core for call in calls_of(o, cores, topo) for d, en in call if d == core)
         wr["RZ" + key] = ("arr" + key, total, {})
 
-    def result(x, c):
+    def result(e, x, c):
         src, keys = ends(x, c)
         if x == "Y":
-            lin("V", T.OS[:, :, c, :], src, 4.0, -1.0, keys, ["OS%d" % c])
+            lin(e, T.OS[:, :, c, :], src, 4.0, -1.0, keys, ["OS%d" % c])
         else:
-            lin("V", T.OZ[:, :, c, :], src, 2.0, 512.0, keys, ["OZ%d" % c])
+            lin(e, T.OZ[:, :, c, :], src, 2.0, 512.0, keys, ["OZ%d" % c])
 
-    def places(c):
+    def places():
         for j, w in enumerate(("TA", "TU")):
-            mm(T["E%d" % c][:, j], [(M(w), H("AL", c))], [w, "AL%d" % c], ["E%d" % c])
+            mm(T.E0[:, 2 * j:2 * j + 2], [(M(w), T.AL[:])], [w, "AL0", "AL1"], ["E0"])
 
-    def powers(c):
-        pw = [T.PW[:, j, 128 * c:128 * c + 128] for j in (0, 1)]
+    def powers():
         for j, b in enumerate(("bA", "bB")):
-            act(pw[j], T["E%d" % c][:, j], AF.Exp, [b], ["PW%d%d" % (c, j)], ["E%d" % c], bias=q(b), scale=LN2)
-        mm(T["Q%d" % c][:, 0], [(M("ID"), pw[0]), (M("ID"), pw[1])], ["ID", "PW%d0" % c, "PW%d1" % c], ["Q%d" % c])
+            act(T.PW[:, j], T.E0[:, 2 * j:2 * j + 2], AF.Exp, [b], ["PW%d" % j], ["E0"], bias=q(b), scale=LN2)
 
-    def keyed(c):
-        tt(H("VV", c), H("ES", c), T["Q%d" % c][:, 0], A.mult, ["ES%d" % c], ["VV%d" % c], ["Q%d" % c])
+    def power():
+        mm(T.Q0[:, 0:2], [(M("ID"), T.PW[:, 0]), (M("ID"), T.PW[:, 1])], ["ID", "PW0", "PW1"], ["Q0"])
 
-    def cut(c, a=0, b=16):
-        p0 = P0[c]
-        order = sorted(range(16), key=lambda r: (r + 1) / p0 if r < p0 else (16 - r) / (16.01 - p0))
-        for i in range(a, b):
-            r = order[i]
-            cl, key = T.CL[:, r, 128 * c:128 * c + 128], "CL%d_%d" % (c, r)
-            if r >= p0:
-                act(cl, H("VV", c), AF.Relu, ["VV%d" % c], [key], bias=-2.0 ** (r - 1))
+    def keyed():
+        tt(T.VV[:], T.ES[:], T.Q0[:, 0:2], A.mult, ["ES0", "ES1"], ["VV"], ["Q0"])
+
+    def cut(j):
+        for r in (2 * j, 2 * j + 1):
+            if r >= P0:
+                act(T.CL[:, r], T.VV[:], AF.Relu, ["VV"], ["CL%d" % r], bias=-2.0 ** (r - 1))
             else:
-                ts(cl, H("VV", c), 2.0 ** (r - 1), A.max, ["VV%d" % c], [key], (), 2.0 ** r, A.min)
-            mm(T["E%d" % c][:, 2], [(slide(2 if r > p0 else 0, r), cl)], [key, "ZS0", "ZS2"], ["E%d" % c], i == 0, i == 15)
+                ts(T.CL[:, r], T.VV[:], 2.0 ** (r - 1), A.max, ["VV"], ["CL%d" % r], (), 2.0 ** r, A.min)
 
-    def column(e, c):
-        b = "bF%d" % c
-        lin(e, H("FC", c), T["E%d" % c][:, 2], q("sF"), q(b), ["sF", b], ["FC%d" % c], ["E%d" % c])
+    def rows(j):
+        rs = (2 * j, 2 * j + 1)
+        mm(T.E1[:, 0:2], [(slide(2 if r > P0 else 0, r), T.CL[:, r]) for r in rs],
+           ["CL%d" % r for r in rs] + ["ZS0", "ZS2"], ["E1"], j == ROWS[0], j == ROWS[-1])
 
-    def cwrite(cs):
-        a, b = cs[0], cs[-1] + 1
-        op("V", ["FC%d" % c for c in cs] + ["LC"], ["CW"], [], lambda: v.tensor_copy(
-            T.CW[:, 0:1024].indirect(T.LC[:, 8 * a:8 * b]), T.FC[:, 128 * a:128 * b]))
+    def column(e):
+        lin(e, T.FC[:], T.E1[:, 0:2], q("sF"), q("bF"), ["sF", "bF"], ["FC"], ["E1"])
+
+    def cwrite():
+        op("V", ["FC", "LC"], ["CW"], [], lambda: v.tensor_copy(T.CW[:, 0:1024].indirect(T.LC[:]), T.FC[:]))
 
     def uturn(t):
         z, k0 = landed(t, 0)
@@ -491,17 +505,22 @@ def rank_program(g, core, T, topo):
         tt(r, r, T.AD[:, 16:32], A.add, ["LIa", "ADb"], ["LIa"])
         copy(T.LC[:], r, ["LIa"], ["LC"])
 
+    def before(t):
+        mm(T.Q1[:, 0:2], [(M("ID"), T.HH[:]), (M("TB"), T.AL[:])], ["ID", "TB", "HH", "AL0", "AL1"], ["Q1"])
+        if t < LEVELS - 1:
+            mm(T.Q0[:, 2:4], [(T.BO[:], T.AL[:])], ["BO", "AL0", "AL1"], ["Q0"])
+
     def first():
-        mm(T.D1[:, 0:256], [(M("ID"), T.HH[:]), (M("TB"), T.AL[:])], ["ID", "TB", "HH0", "HH1", "AL0", "AL1"], ["D1"])
-        act(T.VL[:], T.D1[:, 0:256], AF.Relu, ["bV"], ["VL"], ["D1"], bias=q("bV"), scale=-65536.0)
+        act(T.VL[:], T.Q1[:, 0:2], AF.Relu, ["bV"], ["VL"], ["Q1"], bias=q("bV"), scale=-65536.0)
+
+    def fturn():
         mm(T.Q1[:, 3, 16:32], [(slide(0, a), T.VL[:, a::16]) for a in range(16)], ["VL", "ZS0"], ["Q1"])
 
     def alone():
-        mm(T.D0[:, 0:256], [(T.BO[:], T.AL[:])], ["BO", "AL0", "AL1"], ["D0"])
-        act(T.JK[:], T.D0[:, 0:256], AF.Sign, [], ["JK", "acc"], ["D0"], bias=-30.5, scale=-1.0, acc=q("acc"))
+        act(T.JK[:], T.Q0[:, 2:4], AF.Sign, [], ["JK", "acc"], ["Q0"], bias=-30.5, scale=-1.0, acc=q("acc"))
 
-    def carry():
-        ts(M("AB"), M("ON"), q("acc"), A.mult, ["ON", "acc"], ["AB"], (), 16.0, A.mult)
+    def carry(e):
+        lin(e, M("AB"), M("K16"), q("acc"), 0.0, ["K16", "acc"], ["AB"])
 
     def xlists():
         tt(T.LI[:, 16:32], T.AD[:, 0:16], T.Q1[:, 3, 16:32], A.add, ["ADa"], ["LIb"], ["Q1"])
@@ -544,63 +563,73 @@ def rank_program(g, core, T, topo):
         dma("Y", "oz", T.yz[:], T.OZ[:], ["OZ0", "OZ1"], [])
 
     for t in range(LEVELS - 1):
-        if t == 0: k_rows()
-        if t == 1: carry()
-        if t == 0: k_pick("S", 12, 16); k_blocks(); k_order(); k_slides(); k_pick("S", 0, 4); k_pairs()
-        if t == 0: k_pick("S", 4, 8); k_sums("V"); k_later(); k_pick("S", 8, 12); committees(0); seats(t, 1)
-        if t == 1: xlists()
-        if t == 0: k_steps("S", 0, 4)
+        if t == 0: k_rows(); k_pick("S", 8, 12); k_pick("S", 4, 8); k_pick("S", 0, 4); k_blocks(); k_pairs()
+        if t == 0: k_start("S", 0)
+        if t == 1: carry("S")
+        if t == 0: k_slides(); k_pick("S", 12, 16)
         seats(t, 0)
-        if t == 0: k_steps("V", 4, 8); committees(1); weights(0, 8); weights(8, 16); k_start("V", 0)
-        cg("S", 0, 0, 2, 4); usum(t, 0); cg("V", 0, 0, 0, 2); cg("V", 0, 1, 2, 4)
-        if t == 0: k_duels()
+        if t == 0: committees(0); k_sums("V")
+        usum(t, 0)
+        if t == 0: k_order(); weights(0, 8); weights(8, 16); committees(1); seats(t, 1)
+        cg("V", 0, 0, 2, 4); cg("S", 0, 0, 0, 2); members(t, 0, 0); cg("V", 0, 1, 0, 2)
         if t == 1: seats(t, 1)
-        members(t, 0, 0)
-        if t == 1: xnew(t - 1)
-        cg("S", 0, 1, 0, 2); cg("S", 1, 1, 2, 4); members(t, 0, 1); cg("V", 1, 1, 0, 2); jury(0, "S")
-        if t == 0: k_counts("S")
-        cg("S", 1, 0, 2, 4); members(t, 1, 1); equal(0, 0); equal(0, 1)
+        if t == 0: k_duels()
+        cg("S", 0, 1, 2, 4); members(t, 0, 1)
+        if t == 1: xlists(); xnew(t - 1)
+        cg("S", 1, 1, 0, 4); cg("S", 1, 0, 0, 4)
+        if t == 0: k_steps("S", 0, 4)
+        elist("V", 0)
+        if t == 0: k_later()
         if t == 1: xwrite()
-        cg("S", 1, 0, 0, 2)
-        if t == 0: k_biases()
-        mg("S", 0, 0, 0, 2)
+        mlist(0); diffs(0, 0); diffs(0, 1); equal(0, 0, 2); members(t, 1, 1); members(t, 1, 0); repeats(0, 0)
         if t == 0: k_start("V", 1)
-        hashes(0); members(t, 1, 0)
-        if t == 0: k_turned("V")
-        usum(t, 1); jury(1, "S"); equal(1, 0); equal(1, 1); xg("V", 0, 1, 0, 2); xg("S", 0, 0, 0, 2)
-        xg("S", 0, 1, 2, 4); bins(0, 1); hashes(1); xg("S", 0, 0, 2, 4); bins(0, 0)
-        if t == 0: k_steps("S", 8, 12)
-        uturn(t)
+        product(0); mg("S", 0, 1, 0, 4)
+        if t == 0: k_steps("S", 4, 8)
+        elist("V", 1)
         if t == 0: k_steps("V", 12, 16)
-        xg("V", 1, 0, 0, 2); floors("V", 0); xg("V", 1, 1, 0, 2); xg("S", 1, 0, 2, 4); bins(1, 0); xg("S", 1, 1, 2, 4)
-        mg("S", 0, 1, 0, 2); bins(1, 1); duels("V", 0); winner("S", 0); mg("V", 1, 0, 3, 4); mg("S", 0, 0, 2, 4)
-        mg("V", 1, 0, 2, 3); floors("V", 1); survivors(0); spread(0, 0, "SS"); mg("V", 1, 0, 1, 2); duels("V", 1)
-        places(0); high(0); spread(0, 1, "SS"); mg("S", 1, 0, 0, 1); mg("V", 0, 1, 2, 4); winner("V", 1)
-        maximum(0, 0, "X"); powers(0); maximum(0, 0, "Y"); mg("S", 1, 1, 2, 4); survivors(1); maximum(0, 1, "Y")
-        maximum(0, 1, "X"); leave(t, 0)
+        repeats(0, 1); hashes(0); xg("S", 0, 1, 0, 4); diffs(1, 0); xg("S", 0, 0, 0, 2); diffs(1, 1); equal(1, 0, 2)
+        usum(t, 1); repeats(1, 0); product(1); repeats(1, 1)
+        if t == 0: k_counts("V")
+        xg("V", 0, 0, 2, 4); hashes(1); xg("V", 1, 0, 0, 4)
+        if t == 0: k_turned("S")
+        xg("S", 1, 1, 0, 4); bins(0, 0); bins(0, 1); quarter("V", 0); floors("V", 0, 0); mlist(1); floors("S", 0, 1)
+        mg("V", 0, 0, 2, 4); bins(1, 0); mg("S", 1, 0, 2, 4); counts(0); duels("V", 0)
+        if t == 0: k_biases()
+        bins(1, 1); quarter("V", 1); floors("V", 1, 1)
+        if t == 0: k_steps("S", 8, 12)
+        floors("V", 1, 0); scores(0); winner("S", 0); match(0); mg("S", 0, 0, 0, 2); counts(1); duels("S", 1)
+        survivors(0); steps(0, 0, 0); steps(0, 0, 1); mg("V", 1, 0, 0, 2); scores(1); steps(0, 1, 0); winner("V", 1)
+        match(1); spread("V", 0, 0, 1); survivors(1); high("S"); spread("S", 0, 0, 0); steps(0, 1, 1)
+        maximum("Y", 0, 0, 1); maximum("X", 0, 0, 1); spread("S", 0, 1, 0); places(); spread("S", 0, 1, 1)
+        steps(1, 1, 1); steps(1, 0, 1); maximum("Y", 0, 1, 2); maximum("X", 0, 1, 2); sampled("V", t, 0)
+        halved("V", t, 0); leave(t, 0); powers(); power(); keyed(); cut(3); spread("S", 1, 1, 1); cut(0)
+        spread("S", 1, 0, 1); steps(1, 1, 0); steps(1, 0, 0); spread("S", 1, 1, 0); rows(0); uturn(t); cut(2); before(t)
+        spread("S", 1, 0, 0); maximum("X", 1, 0, 2); mg("S", 1, 1, 0, 4); cut(1); rows(1); cut(7); rows(7)
+        halved("S", t, 1); cut(6); maximum("Y", 1, 0, 2); sampled("V", t, 1); leave(t, 1); cut(4); first(); cut(5)
+        rows(2); rows(3); rows(6); rows(4)
         if t == 0: k_lists()
-        clist(); keyed(0); high(1); spread(1, 0, "SS"); spread(1, 1, "SS"); cut(0, 0, 4); cut(0, 4, 8)
-        mg("S", 1, 1, 0, 2); cut(0, 8, 12); cut(0, 12, 16); places(1); alone(); powers(1); maximum(1, 0, "X")
-        maximum(1, 0, "Y"); maximum(1, 1, "X"); maximum(1, 1, "Y"); leave(t, 1); keyed(1); cut(1, 0, 8); column("S", 0)
-        cut(1, 8, 16); column("S", 1); first(); cwrite((0,)); cwrite((1,))
+        rows(5); column("S"); clist(); alone(); fturn(); cwrite()
         for a in (16, 24, 32):
             weights(24 * t + a, 24 * t + a + 8)
     t = LEVELS - 1
-    seats(t, 0); carry(); usum(t, 0); cg("S", 0, 1, 0, 2); cg("V", 0, 1, 2, 4); members(t, 0, 1); cg("S", 0, 0, 2, 4)
-    cg("V", 0, 0, 0, 2); members(t, 0, 0); xlists(); xnew(t - 1); jury(0, "S"); seats(t, 1); cg("S", 1, 1, 0, 2)
-    cg("S", 1, 0, 0, 2); cg("S", 1, 1, 2, 4); uturn(t); usum(t, 1); equal(0, 0); equal(0, 1); mg("S", 0, 0, 0, 2)
-    cg("V", 1, 0, 2, 4); xwrite(); members(t, 1, 0); hashes(0); xg("S", 0, 0, 2, 4); members(t, 1, 1); jury(1, "V")
-    equal(1, 0); equal(1, 1); xg("V", 0, 1, 0, 2); hashes(1); xg("S", 0, 0, 0, 2); bins(0, 0); xg("S", 0, 1, 2, 4)
-    xg("V", 1, 0, 2, 4); bins(0, 1); xg("S", 1, 0, 0, 2); xg("S", 1, 1, 0, 2); bins(1, 0); floors("V", 0); duels("S", 0)
-    xg("V", 1, 1, 2, 4); mg("V", 1, 0, 3, 4); high(1); bins(1, 1); mg("S", 1, 0, 1, 2); winner("V", 0); floors("V", 1)
-    survivors(0); places(0); high(0); mg("S", 0, 0, 2, 4); duels("S", 1); mg("V", 0, 1, 0, 2); powers(0); keyed(0)
-    winner("S", 1); survivors(1); mg("S", 1, 0, 0, 1); spread(0, 0, "VS"); spread(0, 1, "SS"); cut(0, 0, 4)
-    spread(1, 0, "SS"); clist(); spread(1, 1, "SS"); places(1); maximum(0, 0, "Y"); maximum(0, 0, "X")
-    maximum(0, 1, "X"); result("X", 0); halved(2, 0); cut(0, 4, 8); cut(0, 8, 12); cut(0, 12, 16); maximum(1, 0, "X")
-    maximum(1, 1, "X"); powers(1); keyed(1); result("X", 1); mg("S", 0, 1, 2, 4); first(); halved(2, 1); cut(1, 0, 8)
-    cut(1, 8, 16); maximum(0, 1, "Y"); xlists(); xnew(2); xwrite(); column("S", 0); cwrite((0,)); mg("S", 1, 1, 0, 2)
-    mg("S", 1, 1, 2, 4); zout(); column("S", 1); cwrite((1,)); maximum(1, 1, "Y"); xsum(); mg("S", 1, 0, 2, 3)
-    maximum(1, 0, "Y"); result("Y", 0); result("Y", 1); csum(); sout(); xout(); cout()
+    carry("S"); usum(t, 0); seats(t, 0); cg("V", 0, 1, 0, 2); cg("S", 0, 1, 2, 4); members(t, 0, 1); cg("V", 0, 0, 0, 2)
+    cg("S", 0, 0, 2, 4); seats(t, 1); members(t, 0, 0); elist("V", 0); mlist(0); usum(t, 1); cg("S", 1, 1, 0, 4)
+    product(0); xlists(); diffs(0, 0); diffs(0, 1); equal(0, 0, 2); xnew(t - 1); xwrite(); members(t, 1, 1)
+    repeats(0, 0); cg("S", 1, 0, 0, 4); mg("S", 0, 1, 0, 4); repeats(0, 1); members(t, 1, 0); elist("V", 1); diffs(1, 0)
+    hashes(0); product(1); diffs(1, 1); equal(1, 0, 2); repeats(1, 0); xg("V", 0, 0, 2, 4); xg("S", 0, 1, 0, 4)
+    repeats(1, 1); hashes(1); bins(0, 1); xg("S", 0, 0, 0, 2); bins(0, 0); xg("V", 1, 0, 0, 4); uturn(t)
+    xg("S", 1, 1, 0, 4); bins(1, 1); quarter("V", 0); floors("V", 0, 0); floors("S", 0, 1); counts(0); bins(1, 0)
+    mg("S", 0, 0, 0, 2); mlist(1); mg("V", 1, 0, 0, 2); clist(); duels("S", 0); quarter("S", 1); scores(0)
+    winner("V", 0); match(0); floors("S", 1, 0); floors("V", 1, 1); counts(1); survivors(0); steps(0, 0, 0); high("S")
+    duels("S", 1); scores(1); winner("S", 1); mg("V", 0, 0, 2, 4); steps(0, 1, 1); steps(0, 0, 1); spread("V", 0, 1, 1)
+    spread("S", 0, 0, 0); match(1); survivors(1); spread("S", 0, 0, 1); steps(0, 1, 0); spread("V", 0, 1, 0); places()
+    powers(); before(t); maximum("X", 0, 0, 2); first(); steps(1, 0, 0); spread("S", 1, 0, 0); power(); keyed(); cut(2)
+    cut(0); cut(3); cut(1); steps(1, 0, 1); spread("S", 1, 0, 1); steps(1, 1, 0); spread("S", 1, 1, 0); steps(1, 1, 1)
+    cut(4); spread("S", 1, 1, 1); cut(7); cut(6); fturn(); maximum("X", 1, 0, 2); rows(0); rows(1); xlists(); rows(7)
+    halved("S", 2, 0); rows(2); mg("S", 1, 1, 0, 4); rows(3); halved("V", 2, 1); rows(6); rows(4); cut(5); rows(5)
+    column("S"); mg("S", 1, 0, 2, 4); xnew(2); result("S", "X", 0); xwrite(); xsum(); result("S", "X", 1); cwrite()
+    csum(); zout(); maximum("Y", 0, 0, 2); result("S", "Y", 0); xout(); maximum("Y", 1, 0, 2); result("V", "Y", 1)
+    sout(); cout()
     for sem in sorted(cnt):
         g.wait_ge(T.sem[sem], cnt[sem])
     for t in range(LEVELS - 1):

import math
from concourse.bass import DstId, RemoteDMATransfer
from concourse.mybir import dt, AluOpType, AxisListType, ActivationFunctionType

A = AluOpType
AF = ActivationFunctionType
LEVELS = 3
ROWS = (0, 1, 7, 2, 3, 6, 4, 5)
P0 = 12
LN2 = math.log(2.0)

_B, _H, _F, _I, _U = "bfloat16", "float16", "float32", "int32", "uint16"
MATS = ("ON", "ID", "BO2", "BOM", "KU", "KQ", "K16", "AB", "TA", "TU", "TB", "W2", "W3V", "W3S", "CA", "TRI")
COLS = ("P", "p", "g16", "g1", "cv", "sg", "a", "b", "nd", "dw", "dg", "b1", "nb1", "bA", "bB", "bV", "sF", "bF", "acc", "t0", "t1")
SCRATCH = {
    "XW": ("sbuf", [128, 4096], _B), "CM": ("sbuf", [128, 1024], _I), "CW": ("sbuf", [128, 1024], _I),
    "S3": ("sbuf", [128, 8, 2, 16], _I), "Z3": ("sbuf", [128, 8, 2, 16], _B), "CF": ("sbuf", [128, 1024], _H),
    "MT": ("sbuf", [128, len(MATS), 128], _B), "BO": ("sbuf", [128, 8, 16], _B), "QC": ("sbuf", [128, 32], _F),
    "QB": ("sbuf", [128, 2], _B), "QI": ("sbuf", [128, 16], _I), "QJ": ("sbuf", [128, 16], _I), "QK": ("sbuf", [128, 4], _I),
    "CI": ("sbuf", [128, 144], _B), "PT": ("sbuf", [128, 16], _F), "PS": ("sbuf", [128, 16, 144], _B),
    "ZS": ("sbuf", [128, 3, 144], _B), "JI": ("sbuf", [128, 2, 8], _I), "JT": ("sbuf", [128, 2, 8], _F),
    "WD": ("sbuf", [128, 8, 128], _B), "RD": ("sbuf", [128, 8, 128], _H), "BK": ("sbuf", [128, 16, 128], _B),
    "RA": ("sbuf", [128, 16], _F), "RB": ("sbuf", [128, 16], _F), "CR": ("sbuf", [128, 8], _I), "EA": ("sbuf", [128, 3, 8], _F),
    "W1": ("sbuf", [128, 4, 128], _B), "W1T": ("sbuf", [128, 4, 128], _B),
    "AD": ("sbuf", [128, 32], _I), "BS": ("sbuf", [128, 32], _I), "DI": ("sbuf", [128, 64, 128], _B),
    "CG": ("sbuf", [128, 4096], _H), "YG": ("sbuf", [128, 4096], _H), "XG": ("sbuf", [128, 4096], _B),
    "XS": ("sbuf", [128, 4096], _H), "YS": ("sbuf", [128, 4096], _H), "DS": ("sbuf", [128, 4096], _B),
    "OFS": ("sbuf", [128, 256], _U), "OFM": ("sbuf", [128, 256], _U), "OFX": ("sbuf", [128, 256], _U),
    "ES": ("sbuf", [128, 256], _H), "EQ": ("sbuf", [128, 2, 8, 128], _B), "XX": ("sbuf", [128, 256], _F),
    "HI": ("sbuf", [128, 256], _I), "HH": ("sbuf", [128, 256], _H), "QS": ("sbuf", [128, 256], _H),
    "RR": ("sbuf", [128, 4, 256], _H), "T1": ("sbuf", [128, 256], _B), "T2": ("sbuf", [128, 256], _B),
    "AL": ("sbuf", [128, 256], _B), "PW": ("sbuf", [128, 2, 256], _B), "VV": ("sbuf", [128, 256], _H),
    "CL": ("sbuf", [128, 16, 256], _H), "VL": ("sbuf", [128, 256], _H), "JK": ("sbuf", [128, 256], _B),
    "FC": ("sbuf", [128, 256], _F), "XQ": ("sbuf", [128, 256], _I),
    "LI": ("sbuf", [128, 64], _I), "LC": ("sbuf", [128, 16], _U), "LX": ("sbuf", [128, 32], _U),
    "Z0": ("sbuf", [128, 512], _H),
    "SZ0": ("sbuf", [128, 512], _H), "SZ1": ("sbuf", [128, 512], _H), "SZ2": ("sbuf", [128, 512], _H),
    "RZ0": ("sbuf", [128, 512], _H), "RZ1": ("sbuf", [128, 512], _H),
    "OS": ("sbuf", [128, 8, 2, 16], _F), "OZ": ("sbuf", [128, 8, 2, 16], _B),
    "OX": ("sbuf", [128, 64], _F), "OC": ("sbuf", [128, 64], _F),
    "E0": ("psum", [128, 4, 128], _F), "E1": ("psum", [128, 4, 128], _F),
    "Q0": ("psum", [128, 4, 128], _F), "Q1": ("psum", [128, 4, 128], _F),
    "D": ("psum", [128, 2, 512], _F), "X": ("psum", [128, 2, 512], _F),
}
SEMAPHORES = ["V", "S", "P", "G", "ds", "dz", "dc0", "dc1", "dx", "os", "oz", "ox", "oc"] + [
    k + t + c for k in ("arr", "snt") for t in "01" for c in "01"]


def calls_of(src, cores, topo):
    here = [c for c in topo.cores_of(src) if c in cores and c != src]
    off = [c for c in cores if c != src and c not in here]
    off.sort(key=lambda c: (2 if topo.mates(src, c) else 1 if topo.same_plane(src, c) else 0, c))
    eng = topo.engines(src, off[0])
    call = [(d, [e]) for d, e in zip(off, eng)]
    call += [(d, [e]) for d, e in zip(here, [e for e in topo.engines(src, here[0]) if e not in eng])]
    return [call]


def rank_program(g, core, T, topo):
    rank = T.rank_of(core)
    if rank is None:
        return
    cores = list(T.cores)
    E = {"V": g.vector, "S": g.scalar, "P": g.tensor, "G": g, "Y": g.sync}
    cnt, known = {}, {e: {} for e in E}
    wr, rd, bank = {}, {}, {}

    def sync(e, R, W, B):
        need = {}
        toks = [wr[r] for r in list(R) + list(W) if r in wr]
        for w in W:
            toks += list(rd.get(w, {}).values())
        for b in B:
            toks += [t for f, t in bank.get(b, {}).items() if f != e]
        for t in toks:
            if t[0] not in need or need[t[0]][1] < t[1]:
                need[t[0]] = t
        for sem in sorted(need, key=lambda x: x == e):
            sm, val, clk = need[sem]
            if known[e].get(sm, 0) < val:
                E[e].wait_ge(T.sem[sm], val)
                for k2, v2 in clk.items():
                    known[e][k2] = max(known[e].get(k2, 0), v2)
                known[e][sm] = val

    def note(e, tok, R, W, B):
        for w in W:
            wr[w] = tok
            rd[w] = {}
        for r in R:
            rd.setdefault(r, {})[tok[0]] = tok
        for b in B:
            bank.setdefault(b, {})[e] = tok

    def op(e, R, W, B, f):
        sync(e, R, W, B)
        ins = f()
        for i in (ins if isinstance(ins, list) else [ins]):
            i.then_inc(T.sem[e], 1)
            cnt[e] = cnt.get(e, 0) + 1
        note(e, (e, cnt[e], dict(known[e])), R, W, B)

    def dma(e, sem, out, in_, R, W):
        sync(e, R, W, [])
        E[e].dma_start(out, in_).then_inc(T.sem[sem], 16)
        cnt[sem] = cnt.get(sem, 0) + 16
        note(e, (sem, cnt[sem], dict(known[e])), R, W, [])

    v, s, p = g.vector, g.scalar, g.tensor

    def copy(out, in_, R, W, B=()):
        op("V", R, W, B, lambda: v.tensor_copy(out, in_))

    def ts(out, in0, s1, op0, R, W, B=(), s2=None, op1=None):
        if op1 is None:
            op("V", R, W, B, lambda: v.tensor_scalar(out, in0, s1, None, op0))
        else:
            op("V", R, W, B, lambda: v.tensor_scalar(out, in0, s1, s2, op0, op1))

    def tt(out, a, b, o, R, W, B=()):
        op("V", R, W, B, lambda: v.tensor_tensor(out, a, b, o))

    def scan(out, a, b, ini, o0, o1, R, W, B=()):
        op("V", R, W, B, lambda: v.tensor_tensor_scan(out, a, b, ini, o0, o1))

    def fill(ap, x, W):
        op("V", [], W, [], lambda: v.memset(ap, x))

    def act(out, in_, fn, R, W, B=(), bias=0.0, scale=1.0, acc=None):
        op("S", R, W, B, lambda: s.activation(out, in_, fn, bias=bias, scale=scale, accum_out=acc))

    def lin(e, out, in_, scale, bias, R, W, B=()):
        if e == "V":
            ts(out, in_, scale, A.mult, R, W, B, bias, A.add)
        else:
            act(out, in_, AF.Identity, R, W, B, bias, scale)

    def mm(out, terms, R, B, start=True, stop=True):
        n = len(terms)
        op("P", R, [], B, lambda: [p.matmul(out, a, b, start and i == 0, stop and i == n - 1) for i, (a, b) in enumerate(terms)])

    def iota(out, pat, base, cm, W, small=True):
        op("G", [], W, [], lambda: g.iota(out, pat, base, cm, allow_small_or_imprecise_dtypes=True) if small
           else g.iota(out, pat, base, cm))

    def sel(out, in_, pat, cmp, fl, base, cm, R, W):
        op("G", R, W, [], lambda: g.affine_select(out, in_, pat, cmp, fl, base, cm))

    def M(name):
        return T.MT[:, MATS.index(name)]

    def q(name):
        i = COLS.index(name)
        return T.QC[:, i:i + 1]

    def col(name, src, s1, o0, s2=None, o1=None):
        R = [x for x in (src, s1, s2) if isinstance(x, str)]
        ts(q(name), q(src), q(s1) if isinstance(s1, str) else s1, o0, R, [name], (), q(s2) if isinstance(s2, str) else s2, o1)

    def H(name, c):
        return T[name][:, 128 * c:128 * c + 128]

    def slide(j, k):
        return T.ZS[:, j, 15 - k:143 - k]

    dma("S", "dc0", T.CM[:, 0:512], T.cm[:, 0:512], [], ["CM0"])
    dma("Y", "ds", T.S3[:], T.s0[:], [], ["S3"])
    dma("Y", "dc1", T.CM[:, 512:1024], T.cm[:, 512:1024], [], ["CM1"])
    dma("Y", "dz", T.Z3[:], T.z0[:], [], ["Z3"])
    dma("Y", "dx", T.XW[:], T.x0[:], [], ["XW"])

    def k_rows():
        iota(T.QI[:], [[-1, 16]], 0, 1, ["QI"], False)
        iota(q("P"), [[1, 1]], 0, 1, ["P"])
        iota(T.CI[:], [[1, 144]], 1, 0, ["CI"])
        fill(M("ON"), 1.0, ["ON"])
        fill(M("KU"), 41.0 / 128, ["KU"])
        fill(M("KQ"), (4096 - 41 * 1024) / 128, ["KQ"])
        fill(M("AB"), -4096.0, ["AB"])
        fill(M("K16"), 16.0, ["K16"])
        ts(T.QJ[:], T.QI[:], 15, A.bitwise_and, ["QI"], ["QJ"])
        copy(q("p"), T.QJ[:, 0:1], ["QJ"], ["p"])
        ts(T.PT[:], T.QJ[:], 0, A.is_equal, ["QJ"], ["PT"])
        col("g16", "P", "p", A.subtract)
        ts(T.QK[:, 0:1], T.QJ[:, 0:1], 1, A.bitwise_and, ["QJ"], ["QK0"])
        col("cv", "g16", 16.0, A.add)
        ts(q("sg"), T.QK[:, 0:1], -1.0, A.mult, ["QK0"], ["sg"], (), 0.5, A.add)
        ts(T.ZS[:, 0], T.CI[:], q("cv"), A.is_equal, ["CI", "cv"], ["ZS0"])
        act(T.QB[:, 0:1], q("p"), AF.Exp, ["p"], ["QB"], bias=11 * LN2, scale=-LN2)
        act(q("sF"), T.QB[:, 0:1], AF.Copy, ["QB"], ["sF"])

    def k_blocks():
        iota(T.JI[:, 0], [[1, 8]], 1, 1, ["JIa"], False)
        iota(T.JI[:, 1], [[-1, 8]], -1, 1, ["JIb"], False)
        sel(T.BO[:], M("ON"), [[-16, 8], [0, 16]], A.is_ge, 0.0, 0, 1, ["ON"], ["BO"])
        sel(T.BO[:], T.BO[:], [[16, 8], [0, 16]], A.is_ge, 0.0, 15, -1, ["BO"], ["BO"])
        sel(M("ID"), M("ON"), [[-1, 128]], A.is_equal, 0.0, 0, 1, ["ON"], ["ID"])

    def k_pick(e, a, b):
        for r in range(a, b):
            lin(e, T.PS[:, r], T.ZS[:, 0], T.PT[:, r:r + 1], 0.0, ["ZS0", "PT"], ["PS%d" % r])

    def k_pairs():
        ts(T.JI[:], T.JI[:], 15, A.bitwise_and, ["JIa", "JIb"], ["JIa", "JIb"])
        col("g1", "g16", 1.0, A.add)
        ts(T.JT[:, 0], T.JI[:, 0], q("g1"), A.add, ["JIa", "g1"], ["JTa"])
        ts(T.JT[:, 1], T.JI[:, 1], q("p"), A.max, ["JIb", "g1", "p"], ["JTb"], (), q("g1"), A.add)
        for d in range(8):
            ts(T.WD[:, d], T.CI[:, 0:128], T.JT[:, 0, d:d + 1], A.is_equal, ["CI", "JTa"], ["WD%d" % d], (), -1.0, A.mult)
        for j in (0, 4):
            wd = ["WD%d" % d for d in range(j, j + 4)]
            sel(T.WD[:, j:j + 4], T.WD[:, j:j + 4], [[0, 4], [-1, 128]], A.not_equal, 1.0, 0, 1, wd, wd)

    def k_later():
        for d in range(8):
            ts(T.RD[:, d], T.CI[:, 0:128], T.JT[:, 1, d:d + 1], A.is_equal, ["CI", "JTb"], ["RD%d" % d], (),
               613.0 * (32 if d < 7 else 16), A.mult)

    def k_sums(e):
        lin(e, M("BO2"), T.BO[:], 2.0, 0.0, ["BO"], ["BO2"])
        lin(e, M("BOM"), T.BO[:], -2048.0, 0.0, ["BO"], ["BOM"])

    def k_start(e, c):
        lin(e, T.Z0[:, 256 * c + 1:256 * c + 256:2], T.Z3[:, :, c, :], 0.5, -0.25, ["Z3"], ["Z0%d" % c])

    def k_slides():
        ts(T.ZS[:, 1], T.ZS[:, 0], q("sg"), A.mult, ["ZS0", "sg"], ["ZS1"])
        tt(T.ZS[:, 2, 0:143], T.ZS[:, 0, 0:143], T.ZS[:, 0, 1:144], A.subtract, ["ZS0"], ["ZS2"])
        ts(T.RA[:], T.PT[:], 256.0, A.mult, ["PT"], ["RA"])
        ts(T.RB[:], T.QJ[:], 1, A.is_equal, ["QJ"], ["RB"], (), 256.0, A.mult)
        tt(T.RA[:, 0:15], T.RA[:, 0:15], T.RB[:, 0:15], A.subtract, ["RA", "RB"], ["RA"])

    def k_order():
        iota(T.CR[:], [[-1, 8]], 4, 0, ["CR"], False)
        iota(M("CA"), [[0, 8], [1, 4], [0, 4]], 0, 0, ["CA"])
        sel(M("TRI"), T.BO[:], [[1, 128]], A.is_gt, 0.0, 0, -1, ["BO"], ["TRI"])
        sel(M("TU"), T.BO[:], [[-1, 128]], A.is_gt, 0.0, 0, 1, ["BO"], ["TU"])
        sel(M("TA"), M("TRI"), [[-1, 128]], A.not_equal, 64.0, 0, 1, ["TRI"], ["TA"])
        sel(M("TB"), M("TRI"), [[-1, 128]], A.not_equal, -64.0, 0, 1, ["TRI"], ["TB"])
        sel(M("TU"), M("TU"), [[-1, 128]], A.not_equal, -64.0, 0, 1, ["TU"], ["TU"])
        iota(T.BS[:, 0:16], [[128, 2], [16, 8]], 0, 0, ["BSa"], False)
        iota(T.BS[:, 16:32], [[16, 2], [32, 8]], 0, 0, ["BSb"], False)

    def k_duels():
        ts(T.QK[:, 1:2], T.QJ[:, 0:1], 2, A.arith_shift_right, ["QJ"], ["QK1"])
        ts(T.QK[:, 2:3], T.QJ[:, 0:1], 3, A.bitwise_and, ["QJ"], ["QK2"])
        ts(T.CR[:], T.CR[:], 3, A.bitwise_and, ["CR"], ["CR"])
        copy(T.QC[:, COLS.index("a"):COLS.index("b") + 1], T.QK[:, 1:3], ["QK1", "QK2"], ["a", "b"])
        col("nd", "a", "b", A.not_equal)
        col("t0", "a", "b", A.is_lt, -0.5, A.add)
        ts(T.EA[:, 1], T.CR[:], q("b"), A.is_equal, ["CR", "b"], ["EA1"])
        ts(T.EA[:, 0], T.CR[:], q("a"), A.is_equal, ["CR", "a", "nd"], ["EA0"], (), q("nd"), A.mult)
        col("dw", "nd", -4.0, A.mult, 5.0, A.add)
        tt(T.EA[:, 1], T.EA[:, 1], T.EA[:, 0], A.subtract, ["EA0", "EA1"], ["EA1"])
        col("dg", "nd", -1.0, A.add)
        tt(T.EA[:, 2, 0:4], T.EA[:, 1, 0:4], T.EA[:, 1, 1:5], A.subtract, ["EA1"], ["EA2"])
        ts(q("b1"), T.EA[:, 1, 0:1], 16.0, A.mult, ["EA1", "t0"], ["b1"], (), q("t0"), A.add)
        ts(M("W2"), M("CA"), q("a"), A.is_equal, ["CA", "a", "dw"], ["W2"], (), q("dw"), A.mult)
        col("nb1", "b1", -1.0, A.mult)
        ts(M("W2"), M("W2"), q("dg"), A.add, ["W2", "dg"], ["W2"])
        ts(M("W3V"), T.BO[:], q("a"), A.mult, ["BO", "a"], ["W3V"], (), 1.0 / 16, A.mult)
        tt(M("W2"), M("W2"), T.BO[:], A.mult, ["W2", "BO"], ["W2"])
        ts(M("W3S"), T.BO[:], q("a"), A.mult, ["BO", "a"], ["W3S"], (), 1.0 / 32, A.mult)

    def k_counts(e):
        for i in range(4):
            lin(e, T.W1T[:, i], T.BO[:], T.EA[:, 2, i:i + 1], 0.0, ["BO", "EA2"], ["W1T%d" % i])
            mm(T.X[:, 0, 128 * i:128 * i + 128], [(T.W1T[:, i], M("ID"))], ["W1T%d" % i, "ID"], ["X0"])

    def k_turned(e):
        lin(e, T.W1[:], T.X[:, 0], 1.0, 0.0, [], ["W1"], ["X0"])

    def k_biases():
        col("bA", "p", 2 * LN2, A.mult, 53 * LN2, A.add)
        col("bB", "p", -LN2, A.mult, -109 * LN2, A.add)
        col("bV", "p", -126976.0, A.mult, 3801088.0, A.add)
        col("t1", "p", 1024.0, A.mult, -31744.0, A.add)
        col("bF", "p", P0 - 0.5, A.is_gt, 16384.0, A.mult)
        col("bF", "bF", "t1", A.add)

    def k_lists():
        ts(T.BS[:], T.BS[:], q("p"), A.add, ["BSa", "BSb", "p"], ["BSa", "BSb"])
        ts(T.AD[:, 0:16], T.BS[:, 0:16], 65536.0, A.mult, ["BSa"], ["ADa"])
        ts(T.AD[:, 16:32], T.BS[:, 16:32], 4.0, A.mult, ["BSb"], ["ADb"])
        tt(T.AD[:, 0:16], T.AD[:, 0:16], T.BS[:, 16:32], A.add, ["ADa", "BSb"], ["ADa"])

    def k_steps(e, a, b):
        for k in range(a, b):
            lin(e, T.BK[:, k], T.BO[:], T.RA[:, k:k + 1], 0.0, ["BO", "RA"], ["BK%d" % k])

    def weights(a, b):
        iota(T.DI[:, a:b], [[1, b - a], [0, 128]], a + 1, 0, ["DI%d" % a])
        sel(T.DI[:, a:b], T.DI[:, a:b], [[0, b - a], [-1, 128]], A.is_equal, 0.0, 0, 1, ["DI%d" % a], ["DI%d" % a])

    def landed(t, c):
        if t == 0:
            return T.Z0, ["Z0%d" % c]
        return T["RZ%d" % (t - 1)], ["RZ%d%d" % (t - 1, c), "RZ%d%do" % (t - 1, c)]

    def seats(t, c):
        if t == 0:
            copy(H("OFS", c), T.S3[:, :, c, :], ["S3"], ["OFS%d" % c])
        else:
            z, keys = landed(t, c)
            lin("V", H("OFS", c), z[:, 256 * c:256 * c + 256:2], 4.0, -1.0, keys, ["OFS%d" % c])

    def gather(e, out, win, off, c, h, scale, bias, R, u0, u1):
        a = 128 * c + 64 * h
        lin(e, T[out][:, 16 * a + 256 * u0:16 * a + 256 * u1], win.indirect(T[off][:, a + 16 * u0:a + 16 * u1]), scale, bias,
            R + ["%s%d" % (off, c)], ["%s%d%d%d" % (out, c, h, u) for u in range(u0, u1)])

    def got(name, c, h):
        return ["%s%d%d%d" % (name, c, h, u) for u in range(4)]

    def cg(e, c, h, u0=0, u1=4):
        gather(e, "CG", T.CW[:, 0:1024], "OFS", c, h, 1.0, 1024.0, ["CW"], u0, u1)

    def mg(e, c, h, u0=0, u1=4):
        gather(e, "YG", T.CM[:, 0:1024], "OFM", c, h, 1.0 / 4096, 256.25 - 511.5 / 4096, ["CM0", "CM1"], u0, u1)

    def xg(e, c, h, u0=0, u1=4):
        gather(e, "XG", T.XW[:, 0:4096], "OFX", c, h, 0.5, 0.0, ["XW"], u0, u1)

    def fan(name, c, h, k):
        a = 2048 * c + 1024 * h
        return T[name][:, a + k:a + 1024:16]

    def usum(t, c):
        z, keys = landed(t, c)
        zz = z[:, 256 * c + 1:256 * c + 256:2]
        mm(T["E%d" % c][:, 1], [(M("BO2"), zz), (M("ON"), M("KU"))], keys + ["BO2", "ON", "KU"], ["E%d" % c])
        mm(T["Q%d" % c][:, 0], [(M("BOM"), zz), (M("ON"), M("KQ")), (M("ID"), M("AB"))],
           keys + ["BOM", "ON", "KQ", "ID", "AB"], ["Q%d" % c], True, False)

    def members(t, c, h):
        mm(T["E%d" % c][:, 0, 64 * h:64 * h + 64], [(T.PS[:, (k + t) & 15, 15 - k:143 - k], fan("CG", c, h, k)) for k in range(16)],
           got("CG", c, h) + ["PS%d" % r for r in range(16)], ["E%d" % c])

    def elist(e, c):
        lin(e, H("ES", c), T["E%d" % c][:, 0], 1.0, 0.0, [], ["ES%d" % c], ["E%d" % c])

    def diffs(c, j):
        for i in range(4):
            mm(T.D[:, j, 128 * i:128 * i + 128], [(T.WD[:, 4 * j + i], H("ES", c))], ["ES%d" % c, "WD%d" % (4 * j + i)], ["D%d" % j])

    def equal(c, a, b):
        ts(T.EQ[:, c, 4 * a:4 * b], T.D[:, a:b], 0.0, A.is_equal, [], ["EQ%d%d" % (c, j) for j in range(a, b)],
           ["D%d" % j for j in range(a, b)])

    def repeats(c, j):
        mm(T["Q%d" % c][:, 0], [(T.RD[:, 4 * j + i], T.EQ[:, c, 4 * j + i]) for i in range(4)],
           ["EQ%d%d" % (c, j)] + ["RD%d" % (4 * j + i) for i in range(4)], ["Q%d" % c], False, j == 1)

    def mlist(c):
        lin("V", H("OFM", c), H("ES", c), 1.0, -1024.0, ["ES%d" % c], ["OFM%d" % c])

    def product(c):
        tt(H("XX", c), H("ES", c), T["E%d" % c][:, 1], A.mult, ["ES%d" % c], ["XX%d" % c], ["E%d" % c])

    def hashes(c):
        n = str(c)
        tt(H("HI", c), H("XX", c), T["Q" + n][:, 0], A.add, ["XX" + n], ["HI" + n], ["Q" + n])
        ts(H("HI", c), H("HI", c), 5, A.arith_shift_right, ["HI" + n], ["HI" + n], (), 4095, A.bitwise_and)
        copy(H("OFX", c), H("HI", c), ["HI" + n], ["OFX" + n])

    def high(e):
        src = "OFX" if e == "V" else "HI"
        lin(e, T.HH[:], T[src][:], -1.0 / 65536, -6.0 + 127.5 / 65536, ["OFX0", "HI0", "OFX1", "HI1"], ["HH"])

    def bins(c, h):
        mm(T["E%d" % c][:, 2, 64 * h:64 * h + 64], [(slide(1, k), fan("XG", c, h, k)) for k in range(16)],
           got("XG", c, h) + ["ZS1"], ["E%d" % c])

    def quarter(e, c):
        lin(e, H("QS", c), T["E%d" % c][:, 2], -1.0, 0.0, [], ["QS%d" % c], ["E%d" % c])

    def floors(e, c, j):
        for i in (2 * j, 2 * j + 1):
            lin(e, T.RR[:, i, 128 * c:128 * c + 128], H("QS", c), -1.0, 1535.625 + i / 4, ["QS%d" % c], ["RR%d%d" % (c, i)])

    def counts(c):
        n = str(c)
        mm(T["Q" + n][:, 1], [(T.W1[:, i], T.RR[:, i, 128 * c:128 * c + 128]) for i in range(4)],
           ["W1"] + ["RR%d%d" % (c, i) for i in range(4)], ["Q" + n])

    size = {}

    def duels(e, c):
        n = str(c)
        size[c] = 1.0 if e == "S" else 0.5
        if e == "S":
            act(H("T1", c), T["Q" + n][:, 1], AF.Sign, ["b1"], ["T1" + n], ["Q" + n], bias=q("b1"))
        else:
            ts(H("T1", c), T["Q" + n][:, 1], q("nb1"), A.is_gt, ["nb1"], ["T1" + n], ["Q" + n], -0.5, A.add)

    def scores(c):
        mm(T["E%d" % c][:, 3], [(M("W2"), H("T1", c))], ["W2", "T1%d" % c], ["E%d" % c])

    def winner(e, c):
        n = str(c)
        th = 3.0 * size[c]
        size[n] = e
        if e == "S":
            act(H("T2", c), T["E" + n][:, 3], AF.Sign, [], ["T2" + n], ["E" + n], bias=-th)
        else:
            ts(H("T2", c), T["E" + n][:, 3], th, A.is_gt, [], ["T2" + n], ["E" + n], -0.5, A.add)

    def match(c):
        n = str(c)
        e = size[n]
        mm(T["Q" + n][:, 2], [(M("ID"), H("QS", c)), (M("ID"), T.RR[:, 0, 128 * c:128 * c + 128]), (M("W3" + e), H("T2", c))],
           ["ID", "QS" + n, "RR%d0" % c, "W3V", "W3S", "T2" + n], ["Q" + n])

    def survivors(c):
        n = str(c)
        ts(H("AL", c), T["Q" + n][:, 2], 1535.25, A.is_equal, [], ["AL" + n], ["Q" + n], -2.0, A.add)

    def steps(c, h, m):
        a, db = 128 * c + 64 * h, "XD"[h]
        op("P", ["AL%d" % c] + ["BK%d" % k for k in range(16)], [], [db + str(m)], lambda: [
            p.matmul(T[db][:, m, j::8], T.BK[:, 2 * j + m], T.AL[:, a:a + 64], True, True) for j in range(8)])

    def spread(e, c, h, m):
        a, db = 128 * c + 64 * h, "XD"[h]
        lin(e, T.DS[:, 16 * a + m:16 * a + 1024:2], T[db][:, m], 1.0, 0.0, [], ["DS%d%d%d" % (c, h, m)], [db + str(m)])

    def maximum(x, c, h0, h1):
        a, b, hs = 2048 * c + 1024 * h0, 2048 * c + 1024 * h1, range(h0, h1)
        scan(T[x + "S"][:, a:b], T[x + "G"][:, a:b], T.DS[:, a:b], -1024.0, A.max, A.add,
             [k for h in hs for k in got(x + "G", c, h) + ["DS%d%d0" % (c, h), "DS%d%d1" % (c, h)]], ["%sS%d%d" % (x, c, h) for h in hs])

    def ends(x, c):
        return T[x + "S"][:, 2048 * c + 15:2048 * c + 2048:16], ["%sS%d0" % (x, c), "%sS%d1" % (x, c)]

    def halved(e, t, c):
        src, keys = ends("X", c)
        lin(e, T["SZ%d" % t][:, 256 * c + 1:256 * c + 256:2], src, 1.0, 255.75, keys, ["SZX%d%d" % (t, c)])

    def sampled(e, t, c):
        src, keys = ends("Y", c)
        lin(e, T["SZ%d" % t][:, 256 * c:256 * c + 256:2], src, 1.0, 0.0, keys, ["SZY%d%d" % (t, c)])

    def leave(t, c):
        key = "%d%d" % (t, c)
        sz, rz = T["SZ%d" % t], T["RZ%d" % t]
        blk = lambda x, b: x[:, 256 * c + 32 * b:256 * c + 32 * b + 32]
        sync("G", ["SZX" + key, "SZY" + key], [], [])
        for call in calls_of(core, cores, topo):
            g.remote_dma_fused([RemoteDMATransfer(
                src=blk(sz, cores.index(d)), dst=blk(rz, rank),
                dst_ids=[DstId(rid=topo.addr(d, core)[0], pnc=topo.addr(d, core)[1])],
                dma_engine_mask=sum(1 << e for e in en), remote_sem=T.sem["arr" + key]) for d, en in call],
                local_sem=T.sem["snt" + key])
        sel(blk(rz, rank), blk(sz, rank), [[0, 32]], A.is_ge, 0.0, 0, 0, ["SZX" + key, "SZY" + key], ["RZ" + key + "o"])
        total = sum(len(en) for o in cores if o != core for call in calls_of(o, cores, topo) for d, en in call if d == core)
        wr["RZ" + key] = ("arr" + key, total, {})

    def result(e, x, c):
        src, keys = ends(x, c)
        if x == "Y":
            lin(e, T.OS[:, :, c, :], src, 4.0, -1.0, keys, ["OS%d" % c])
        else:
            lin(e, T.OZ[:, :, c, :], src, 2.0, 512.0, keys, ["OZ%d" % c])

    def places():
        for j, w in enumerate(("TA", "TU")):
            mm(T.E0[:, 2 * j:2 * j + 2], [(M(w), T.AL[:])], [w, "AL0", "AL1"], ["E0"])

    def powers():
        for j, b in enumerate(("bA", "bB")):
            act(T.PW[:, j], T.E0[:, 2 * j:2 * j + 2], AF.Exp, [b], ["PW%d" % j], ["E0"], bias=q(b), scale=LN2)

    def power():
        mm(T.Q0[:, 0:2], [(M("ID"), T.PW[:, 0]), (M("ID"), T.PW[:, 1])], ["ID", "PW0", "PW1"], ["Q0"])

    def keyed():
        tt(T.VV[:], T.ES[:], T.Q0[:, 0:2], A.mult, ["ES0", "ES1"], ["VV"], ["Q0"])

    def cut(j):
        for r in (2 * j, 2 * j + 1):
            if r >= P0:
                act(T.CL[:, r], T.VV[:], AF.Relu, ["VV"], ["CL%d" % r], bias=-2.0 ** (r - 1))
            else:
                ts(T.CL[:, r], T.VV[:], 2.0 ** (r - 1), A.max, ["VV"], ["CL%d" % r], (), 2.0 ** r, A.min)

    def rows(j):
        rs = (2 * j, 2 * j + 1)
        mm(T.E1[:, 0:2], [(slide(2 if r > P0 else 0, r), T.CL[:, r]) for r in rs],
           ["CL%d" % r for r in rs] + ["ZS0", "ZS2"], ["E1"], j == ROWS[0], j == ROWS[-1])

    def column(e):
        lin(e, T.FC[:], T.E1[:, 0:2], q("sF"), q("bF"), ["sF", "bF"], ["FC"], ["E1"])

    def cwrite():
        op("V", ["FC", "LC"], ["CW"], [], lambda: v.tensor_copy(T.CW[:, 0:1024].indirect(T.LC[:]), T.FC[:]))

    def uturn(t):
        z, k0 = landed(t, 0)
        mm(T.Q1[:, 3, 0:16], [(slide(0, a), z[:, 2 * a + 1::32]) for a in range(16)], k0 + landed(t, 1)[1] + ["ZS0"], ["Q1"])

    def clist():
        r = T.LI[:, 0:16]
        lin("V", r, T.Q1[:, 3, 0:16], 2.0, 8.0, [], ["LIa"], ["Q1"])
        ts(r, r, 3, A.bitwise_and, ["LIa"], ["LIa"])
        tt(r, r, T.AD[:, 16:32], A.add, ["LIa", "ADb"], ["LIa"])
        copy(T.LC[:], r, ["LIa"], ["LC"])

    def before(t):
        mm(T.Q1[:, 0:2], [(M("ID"), T.HH[:]), (M("TB"), T.AL[:])], ["ID", "TB", "HH", "AL0", "AL1"], ["Q1"])
        if t < LEVELS - 1:
            mm(T.Q0[:, 2:4], [(T.BO[:], T.AL[:])], ["BO", "AL0", "AL1"], ["Q0"])

    def first():
        act(T.VL[:], T.Q1[:, 0:2], AF.Relu, ["bV"], ["VL"], ["Q1"], bias=q("bV"), scale=-65536.0)

    def fturn():
        mm(T.Q1[:, 3, 16:32], [(slide(0, a), T.VL[:, a::16]) for a in range(16)], ["VL", "ZS0"], ["Q1"])

    def alone():
        act(T.JK[:], T.Q0[:, 2:4], AF.Sign, [], ["JK", "acc"], ["Q0"], bias=-30.5, scale=-1.0, acc=q("acc"))

    def carry(e):
        lin(e, M("AB"), M("K16"), q("acc"), 0.0, ["K16", "acc"], ["AB"])

    def xlists():
        tt(T.LI[:, 16:32], T.AD[:, 0:16], T.Q1[:, 3, 16:32], A.add, ["ADa"], ["LIb"], ["Q1"])
        ts(T.LI[:, 32:48], T.LI[:, 16:32], 4095, A.bitwise_and, ["LIb"], ["LIc"])
        ts(T.LI[:, 48:64], T.LI[:, 16:32], 12, A.arith_shift_right, ["LIb"], ["LId"])
        copy(T.LX[:], T.LI[:, 32:64], ["LIc", "LId"], ["LX"])

    def xnew(t):
        keys = [k for c in (0, 1) for h in (0, 1) for k in got("XG", c, h)] + ["SZX%d0" % t, "SZX%d1" % t]
        op("V", keys + ["LX"], ["XQ"], [], lambda: v.tensor_tensor(
            T.XQ[:], T.XG[:, 0:4096].indirect(T.LX[:, 16:32]), T["SZ%d" % t][:, 1::2], A.add))

    def xwrite():
        op("V", ["XQ", "LX"], ["XW"], [], lambda: v.tensor_copy(T.XW[:, 0:4096].indirect(T.LX[:, 0:16]), T.XQ[:]))

    def committees(j):
        ts(T.CW[:, 512 * j:512 * j + 512], T.CM[:, 512 * j:512 * j + 512], 1023, A.bitwise_and, ["CM%d" % j], ["CW"])

    dis = ["DI%d" % a for a in range(0, 64, 8)]

    def xsum():
        mm(T.Q0[:, 0, 0:64], [(T.DI[:, m], T.XW[:, 64 * m:64 * m + 64]) for m in range(64)], ["XW"] + dis, ["Q0"])

    def xout():
        act(T.OX[:], T.Q0[:, 0, 0:64], AF.Copy, [], ["OX"], ["Q0"])
        dma("S", "ox", T.yx[:], T.OX[:], ["OX"], [])

    def csum():
        act(T.CF[:], T.CW[:], AF.Copy, ["CW"], ["CF"])
        mm(T.E0[:, 0, 0:64], [(T.DI[:, m], T.CF[:, 64 * m:64 * m + 64]) for m in range(16)], ["CF"] + dis[:2], ["E0"])

    def cout():
        act(T.OC[:], T.E0[:, 0, 0:64], AF.Copy, [], ["OC"], ["E0"])
        dma("S", "oc", T.yc[:], T.OC[:], ["OC"], [])

    def sout():
        dma("Y", "os", T.ys[:], T.OS[:], ["OS0", "OS1"], [])

    def zout():
        dma("Y", "oz", T.yz[:], T.OZ[:], ["OZ0", "OZ1"], [])

    for t in range(LEVELS - 1):
        if t == 0: k_rows(); k_pick("S", 8, 12); k_pick("S", 4, 8); k_pick("S", 0, 4); k_blocks(); k_pairs()
        if t == 0: k_start("S", 0)
        if t == 1: carry("S")
        if t == 0: k_slides(); k_pick("S", 12, 16)
        seats(t, 0)
        if t == 0: committees(0); k_sums("V")
        usum(t, 0)
        if t == 0: k_order(); weights(0, 8); weights(8, 16); committees(1); seats(t, 1)
        cg("V", 0, 0, 2, 4); cg("S", 0, 0, 0, 2); members(t, 0, 0); cg("V", 0, 1, 0, 2)
        if t == 1: seats(t, 1)
        if t == 0: k_duels()
        cg("S", 0, 1, 2, 4); members(t, 0, 1)
        if t == 1: xlists(); xnew(t - 1)
        cg("S", 1, 1, 0, 4); cg("S", 1, 0, 0, 4)
        if t == 0: k_steps("S", 0, 4)
        elist("V", 0)
        if t == 0: k_later()
        if t == 1: xwrite()
        mlist(0); diffs(0, 0); diffs(0, 1); equal(0, 0, 2); members(t, 1, 1); members(t, 1, 0); repeats(0, 0)
        if t == 0: k_start("V", 1)
        product(0); mg("S", 0, 1, 0, 4)
        if t == 0: k_steps("S", 4, 8)
        elist("V", 1)
        if t == 0: k_steps("V", 12, 16)
        repeats(0, 1); hashes(0); xg("S", 0, 1, 0, 4); diffs(1, 0); xg("S", 0, 0, 0, 2); diffs(1, 1); equal(1, 0, 2)
        usum(t, 1); repeats(1, 0); product(1); repeats(1, 1)
        if t == 0: k_counts("V")
        xg("V", 0, 0, 2, 4); hashes(1); xg("V", 1, 0, 0, 4)
        if t == 0: k_turned("S")
        xg("S", 1, 1, 0, 4); bins(0, 0); bins(0, 1); quarter("V", 0); floors("V", 0, 0); mlist(1); floors("S", 0, 1)
        mg("V", 0, 0, 2, 4); bins(1, 0); mg("S", 1, 0, 2, 4); counts(0); duels("V", 0)
        if t == 0: k_biases()
        bins(1, 1); quarter("V", 1); floors("V", 1, 1)
        if t == 0: k_steps("S", 8, 12)
        floors("V", 1, 0); scores(0); winner("S", 0); match(0); mg("S", 0, 0, 0, 2); counts(1); duels("S", 1)
        survivors(0); steps(0, 0, 0); steps(0, 0, 1); mg("V", 1, 0, 0, 2); scores(1); steps(0, 1, 0); winner("V", 1)
        match(1); spread("V", 0, 0, 1); survivors(1); high("S"); spread("S", 0, 0, 0); steps(0, 1, 1)
        maximum("Y", 0, 0, 1); maximum("X", 0, 0, 1); spread("S", 0, 1, 0); places(); spread("S", 0, 1, 1)
        steps(1, 1, 1); steps(1, 0, 1); maximum("Y", 0, 1, 2); maximum("X", 0, 1, 2); sampled("V", t, 0)
        halved("V", t, 0); leave(t, 0); powers(); power(); keyed(); cut(3); spread("S", 1, 1, 1); cut(0)
        spread("S", 1, 0, 1); steps(1, 1, 0); steps(1, 0, 0); spread("S", 1, 1, 0); rows(0); uturn(t); cut(2); before(t)
        spread("S", 1, 0, 0); maximum("X", 1, 0, 2); mg("S", 1, 1, 0, 4); cut(1); rows(1); cut(7); rows(7)
        halved("S", t, 1); cut(6); maximum("Y", 1, 0, 2); sampled("V", t, 1); leave(t, 1); cut(4); first(); cut(5)
        rows(2); rows(3); rows(6); rows(4)
        if t == 0: k_lists()
        rows(5); column("S"); clist(); alone(); fturn(); cwrite()
        for a in (16, 24, 32):
            weights(24 * t + a, 24 * t + a + 8)
    t = LEVELS - 1
    carry("S"); usum(t, 0); seats(t, 0); cg("V", 0, 1, 0, 2); cg("S", 0, 1, 2, 4); members(t, 0, 1); cg("V", 0, 0, 0, 2)
    cg("S", 0, 0, 2, 4); seats(t, 1); members(t, 0, 0); elist("V", 0); mlist(0); usum(t, 1); cg("S", 1, 1, 0, 4)
    product(0); xlists(); diffs(0, 0); diffs(0, 1); equal(0, 0, 2); xnew(t - 1); xwrite(); members(t, 1, 1)
    repeats(0, 0); cg("S", 1, 0, 0, 4); mg("S", 0, 1, 0, 4); repeats(0, 1); members(t, 1, 0); elist("V", 1); diffs(1, 0)
    hashes(0); product(1); diffs(1, 1); equal(1, 0, 2); repeats(1, 0); xg("V", 0, 0, 2, 4); xg("S", 0, 1, 0, 4)
    repeats(1, 1); hashes(1); bins(0, 1); xg("S", 0, 0, 0, 2); bins(0, 0); xg("V", 1, 0, 0, 4); uturn(t)
    xg("S", 1, 1, 0, 4); bins(1, 1); quarter("V", 0); floors("V", 0, 0); floors("S", 0, 1); counts(0); bins(1, 0)
    mg("S", 0, 0, 0, 2); mlist(1); mg("V", 1, 0, 0, 2); clist(); duels("S", 0); quarter("S", 1); scores(0)
    winner("V", 0); match(0); floors("S", 1, 0); floors("V", 1, 1); counts(1); survivors(0); steps(0, 0, 0); high("S")
    duels("S", 1); scores(1); winner("S", 1); mg("V", 0, 0, 2, 4); steps(0, 1, 1); steps(0, 0, 1); spread("V", 0, 1, 1)
    spread("S", 0, 0, 0); match(1); survivors(1); spread("S", 0, 0, 1); steps(0, 1, 0); spread("V", 0, 1, 0); places()
    powers(); before(t); maximum("X", 0, 0, 2); first(); steps(1, 0, 0); spread("S", 1, 0, 0); power(); keyed(); cut(2)
    cut(0); cut(3); cut(1); steps(1, 0, 1); spread("S", 1, 0, 1); steps(1, 1, 0); spread("S", 1, 1, 0); steps(1, 1, 1)
    cut(4); spread("S", 1, 1, 1); cut(7); cut(6); fturn(); maximum("X", 1, 0, 2); rows(0); rows(1); xlists(); rows(7)
    halved("S", 2, 0); rows(2); mg("S", 1, 1, 0, 4); rows(3); halved("V", 2, 1); rows(6); rows(4); cut(5); rows(5)
    column("S"); mg("S", 1, 0, 2, 4); xnew(2); result("S", "X", 0); xwrite(); xsum(); result("S", "X", 1); cwrite()
    csum(); zout(); maximum("Y", 0, 0, 2); result("S", "Y", 0); xout(); maximum("Y", 1, 0, 2); result("V", "Y", 1)
    sout(); cout()
    for sem in sorted(cnt):
        g.wait_ge(T.sem[sem], cnt[sem])
    for t in range(LEVELS - 1):
        for c in (0, 1):
            g.wait_ge(T.sem["snt%d%d" % (t, c)], sum(len(en) for call in calls_of(core, cores, topo) for d, en in call))
